import numpy as np
import ml_dtypes


def mxq(x, axis, fmt="e4m3"):
    dtype, down = {"e4m3": (ml_dtypes.float8_e4m3fn, 7), "e5m2": (ml_dtypes.float8_e5m2, 14)}[fmt]
    v = np.moveaxis(np.asarray(x, np.float32).astype(ml_dtypes.bfloat16).astype(np.float64), axis, -1)
    blocks = v.reshape(v.shape[:-1] + (-1, 32))
    amax = np.abs(blocks).max(-1, keepdims=True)
    byte = np.maximum(np.where(amax > 0, np.frexp(amax)[1] - 1 + 127, 0) - down, 1)
    scale = np.exp2(byte - 127.0)
    codes = (blocks / scale).astype(np.float32).astype(dtype).astype(np.float64)
    return np.moveaxis((codes * scale).reshape(v.shape), -1, axis)


WIDE = False


def mx_kscale(k):
    if not WIDE:
        return np.ones(k)
    levels = np.array([30, -30])
    if k % 512:
        return np.exp2(np.random.permutation(np.resize(levels, k // 32))).repeat(32)
    a = np.empty((k // 512, 16))
    for p in range(k // 512):
        a[p, :8] = np.random.permutation(np.resize(levels, 8))
        for g in range(8):
            far = levels[np.abs(levels - a[p, g]) >= 10]
            a[p, g + 8] = far[np.random.randint(len(far))]
    return np.exp2(a.ravel()).repeat(32)


def f64(x):
    return np.asarray(x).astype(np.float64)


E2M1 = np.array([0.0, 0.5, 1.0, 1.5, 2.0, 3.0, 4.0, 6.0, -0.0, -0.5, -1.0, -1.5, -2.0, -3.0, -4.0, -6.0])


def pack_weight(w, fmt):
    k, n = w.shape
    w = f64(np.asarray(w, np.float32).astype(ml_dtypes.bfloat16)).reshape(k // 32, 32, n)
    amax = np.abs(w).max(1)
    if fmt == "e4m3":
        byte = np.frexp(amax)[1] - 1 + 127 - 7
    else:
        mant, ex = np.frexp(amax / 6.0)
        byte = np.where(mant > 0.5, ex, ex - 1) + 127
    byte = np.clip(np.where(amax > 0, byte, 1), 1, 254)
    scaled = (w * np.exp2(127.0 - byte)[:, None, :]).reshape(k, n).astype(np.float32)
    by_word = np.ascontiguousarray(scaled.reshape(k // 512, 128, 4, n).transpose(0, 1, 3, 2))
    if fmt == "e4m3":
        words = by_word.astype(ml_dtypes.float8_e4m3fn).view(np.uint8)
    else:
        c = by_word.astype(ml_dtypes.float4_e2m1fn).view(np.uint8) & 0xF
        words = (c[..., 0::2] | (c[..., 1::2] << 4)).reshape(k // 512, 128, 2 * n)
    return np.ascontiguousarray(words), np.ascontiguousarray(byte.astype(np.uint8).reshape(k // 512, 16, n))


def unpack_weight(words, scales, fmt):
    g, _, n = scales.shape
    words = np.ascontiguousarray(words).reshape(g, 128, n, -1)
    if fmt == "e4m3":
        vals = words.view(ml_dtypes.float8_e4m3fn).astype(np.float64)
    else:
        nib = np.empty((g, 128, n, 4), np.uint8)
        nib[..., 0::2] = words & 0xF
        nib[..., 1::2] = words >> 4
        vals = E2M1[nib]
    vals = vals * np.repeat(np.exp2(scales.astype(np.float64) - 127.0), 8, axis=1)[..., None]
    return vals.transpose(0, 1, 3, 2).reshape(g * 512, n)


def planes(y):
    n, m = y.shape
    v = y.astype(np.float32).astype(ml_dtypes.bfloat16).astype(np.float64).reshape(n // 32, 32, m)
    top = np.abs(v).max(1)
    byte = np.clip(np.where(top > 0, np.frexp(top)[1] - 1 + 127 - 7, 1), 1, 254)
    codes = (v * np.exp2(127.0 - byte)[:, None, :]).reshape(n, m).astype(np.float32).astype(ml_dtypes.float8_e4m3fn).view(np.uint8)
    words = codes.reshape(n // 512, 128, 4, m).transpose(0, 1, 3, 2)
    return np.ascontiguousarray(words), np.ascontiguousarray(byte.astype(np.uint8).reshape(n // 512, 16, m))


def silu(v):
    return v / (1.0 + np.exp(-np.maximum(v, -700.0)))


K, L, R, M, T = 512, 512, 512, 1536, 1024


def setup_inputs():
    n = np.random.standard_normal
    s1 = mx_kscale(K)[:, None]
    s2 = mx_kscale(L)[:, None]
    u = mx_kscale(R)[:, None]
    p_w = pack_weight(n((R, M)) / np.sqrt(R) / u, "e2m1")
    return {
        "x": (n((K, T)) * s1).astype(np.float32),
        "wx": (n((K, R)) / np.sqrt(K) / s1 * u.T).astype(np.float32),
        "c": (n((L, T)) * s2).astype(np.float32),
        "wc": (n((L, R)) / np.sqrt(L) / s2).astype(np.float32),
        "w_words": p_w[0],
        "w_scales": p_w[1],
        "b": (0.3 * n(1536)).astype(np.float32),
    }


def reference(x, wx, c, wc, w_words, w_scales, b):
    x_ = mxq(f64(x), 0, "e4m3")
    wx_ = mxq(f64(wx), 0, "e4m3")
    c_ = mxq(f64(c), 0, "e5m2")
    wc_ = mxq(f64(wc), 0, "e4m3")
    w_ = unpack_weight(w_words, w_scales, "e2m1")
    h_ = mxq((wx_.T @ x_) * (wc_.T @ c_), 0, "e4m3")
    y = h_.T @ w_
    out_0 = silu(y + f64(b)[None, :])
    return (out_0,) + planes(out_0)

@@ -1,0 +1,360 @@
+from contextlib import ExitStack
+
+import concourse.mybir as mybir
+from concourse.masks import make_identity
+
+K, L, R, M, T = 512, 512, 512, 1536, 1024
+FLOPS = 2 * K * R * T + 2 * L * R * T + 2 * R * M * T
+
+F32 = mybir.dt.float32
+BF16 = mybir.dt.bfloat16
+I32 = mybir.dt.int32
+U32 = mybir.dt.uint32
+U8 = mybir.dt.uint8
+E4M3 = mybir.dt.float8_e4m3fn_x4
+E5M2 = mybir.dt.float8_e5m2_x4
+E2M1 = mybir.dt.float4_e2m1fn_x4
+ALU = mybir.AluOpType
+ACT = mybir.ActivationFunctionType
+
+P = 128
+HALF = 512
+BANK = 512
+STAGE_TAGS = {"c1": "stage_a", "x1": "stage_a", "o0": "stage_a", "h1": "stage_b", "o1": "stage_b"}
+
+
+def tile_mix_bilin_tm_pl_silu_kernel(tc, x, wx, c, wc, w_words, w_scales, b, out_0, out_1, out_2):
+    nc = tc.nc
+    with ExitStack() as ctx:
+        sb = ctx.enter_context(tc.tile_pool(name="sb", bufs=1))
+        psum = ctx.enter_context(tc.psum_pool(name="psum", bufs=1))
+        ctx.enter_context(tc.manual_schedule())
+
+        def new(name, shape, dtype, tag=None, bufs=1):
+            return sb.tile(shape, dtype, name=name, tag=tag or name, bufs=bufs, align_bytes=64)
+
+        def new_bank(name, n):
+            return psum.tile([P, BANK], F32, name=name, tag="bank%d" % n)
+
+        def load(name, src):
+            raw = new(name, [P, 4, src.shape[1]], F32)
+            nc.sync.dma_start(out=raw[:], in_=src.rearrange("(p k) t -> p k t", k=4))
+            return raw
+
+        def cast(engine, out, in_):
+            if engine == "V":
+                nc.vector.tensor_copy(out=out, in_=in_)
+            elif engine == "S":
+                nc.scalar.copy(out=out, in_=in_)
+            else:
+                nc.gpsimd.tensor_scalar(out=out, in0=in_, scalar1=1.0, scalar2=-0.0, op0=ALU.mult, op1=ALU.add)
+
+        def interleave(engine, dst, raw, lo, hi):
+            cast(engine, dst[:, lo:hi, :], raw[:, :, lo:hi].rearrange("p k t -> p t k"))
+
+        def deal(engine, dst, raw, lo, hi):
+            cast(engine, dst[:, :, lo:hi, :].rearrange("p j m k -> p m j k"),
+                 raw[:, :, 4 * lo:4 * hi].rearrange("p k (m j) -> p m j k", j=4))
+
+        def quantize(codes, scales, values, fmt):
+            nc.vector.quantize_mx(out=codes.bitcast(fmt), scales=scales, in_=values)
+
+        def mx(name, width):
+            return new(name + "_codes", [P, width], U32), new(name + "_scales", [P, width], U8)
+
+        b_cols = new("b_cols", [P, M // P], F32)
+        nc.scalar.dma_start(out=b_cols[:], in_=b.rearrange("(p c) -> p c", p=P))
+        wc_raw = load("wc_raw", wc)
+        c_raw = [load("c_raw0", c[:, :HALF])]
+        wx_raw = load("wx_raw", wx)
+        x_raw = [load("x_raw0", x[:, :HALF])]
+        w_codes = new("w_codes", [P, 2 * M], U8)
+        nc.sync.dma_start(out=w_codes[:].bitcast(I32), in_=w_words[0].bitcast(I32))
+        w_plane = new("w_plane", [P, M], U8)
+        nc.vector.memset(w_plane[:].bitcast(I32), 0)
+        for q in range(4):
+            nc.sync.dma_start(out=w_plane[32 * q:32 * q + 4, :].bitcast(I32), in_=w_scales[0, 4 * q:4 * q + 4, :].bitcast(I32))
+        c_raw.append(load("c_raw1", c[:, HALF:]))
+        x_raw.append(load("x_raw1", x[:, HALF:]))
+
+        warm = new("warm", [P, 8], F32)
+        nc.vector.memset(warm[:], 0.0)
+        warm_out = new("warm_out", [P, 8], F32)
+        nc.scalar.activation(out=warm_out[:], in_=warm[:], func=ACT.Silu)
+
+        ident = new("ident", [P, P], F32)
+        make_identity(nc, ident[:])
+
+        bias = new("bias", [P, M], F32)
+        bias_v = bias[:].rearrange("p (n c) -> p n c", c=M // P)
+        for g in range(3):
+            bank = new_bank("bias%d" % g, g)
+            for e in range(4):
+                col = 4 * g + e
+                nc.tensor.transpose(bank[:, P * e:P * (e + 1)], b_cols[:, col:col + 1].to_broadcast([P, P]), ident[:])
+            nc.scalar.copy(out=bias_v[:, :, 4 * g:4 * g + 4], in_=bank[:].rearrange("p (e n) -> p n e", e=4))
+
+        wc_q, wc_s = mx("wc", R)
+        wx_q, wx_s = mx("wx", R)
+        c_mx = [mx("c%d" % a, HALF) for a in range(2)]
+        x_mx = [mx("x%d" % a, HALF) for a in range(2)]
+        h_mx = [mx("h%d" % a, HALF) for a in range(2)]
+        pc_sb = [new("pc%d" % a, [P, 4, 4, P], F32) for a in range(2)]
+        out_scales = [new("out_scales%d" % a, [P, M], U8) for a in range(2)]
+
+        def flat(t):
+            return t.rearrange("p a b -> p (a b)")
+
+        staged = {}
+
+        def stage(name):
+            if name not in staged:
+                staged[name] = new(name + "_bf", [P, 2048], BF16, tag=STAGE_TAGS.get(name, name + "_bf"))
+            return staged[name]
+
+        def cast_rows(engine, name, raw, lo, hi):
+            interleave(engine, stage(name)[:].rearrange("p (t k) -> p t k", k=4), raw, lo, hi)
+
+        def cast_dealt(engine, name, raw, lo, hi):
+            deal(engine, stage(name)[:].rearrange("p (j m k) -> p j m k", j=4, k=4), raw, lo // 4, hi // 4)
+
+        def quantize_cols(name, pair, fmt, lo, hi):
+            quantize(pair[0][:, lo:hi], pair[1][:, lo:hi], staged[name][:, 4 * lo:4 * hi], fmt)
+
+        banks = {}
+
+        def pc_matmul(a, j):
+            bank = new_bank("pc%d_%d" % (a, j), 4 + j)
+            cols = slice(P * j, P * (j + 1))
+            nc.tensor.matmul_mx(out=bank[:], lhsT=wc_q[:, cols].bitcast(E4M3), lhsT_scale=wc_s[:, cols],
+                                rhs=c_mx[a][0][:].bitcast(E5M2), rhs_scale=c_mx[a][1][:], start=True, stop=True)
+            banks["pc", a, j] = bank
+
+        def pc_copy(a, j):
+            bank = banks["pc", a, j]
+            nc.scalar.copy(out=pc_sb[a][:, j], in_=bank[:].rearrange("p (m i) -> p i m", i=4))
+
+        def px_matmul(a, q):
+            bank = new_bank("px%d_%d" % (a, q), 4 * a + q)
+            tok = slice(P * q, P * (q + 1))
+            for j in range(4):
+                cols = slice(P * j, P * (j + 1))
+                nc.tensor.matmul_mx(out=bank[:, cols], lhsT=wx_q[:, cols].bitcast(E4M3), lhsT_scale=wx_s[:, cols],
+                                    rhs=x_mx[a][0][:, tok].bitcast(E4M3), rhs_scale=x_mx[a][1][:, tok], start=True, stop=True)
+            banks["px", a, q] = bank
+
+        def product(a, i):
+            h = stage("h%d" % a)[:].rearrange("p (i m j) -> p i m j", i=4, j=4)
+            nc.vector.tensor_tensor(out=h[:, i], in0=banks["px", a, i][:].rearrange("p (j m) -> p m j", j=4),
+                                    in1=pc_sb[a][:, :, i, :].rearrange("p j m -> p m j"), op=ALU.mult)
+
+        act = [new("act%d" % n, [P, 4, BANK], F32) for n in range(6)]
+        out_v = out_0.rearrange("(a p i) n -> a p i n", a=2, i=4)
+        z_tiles = {}
+
+        def y_matmul(n, i):
+            a, n0 = n // 3, BANK * (n % 3)
+            bank = new_bank("y%d_%d" % (n, i), i)
+            banks["y", n, i] = bank
+            cols = slice(P * i, P * (i + 1))
+            nc.tensor.matmul_mx(out=bank[:], lhsT=h_mx[a][0][:, cols].bitcast(E4M3), lhsT_scale=h_mx[a][1][:, cols],
+                                rhs=w_codes[:, 2 * n0:2 * (n0 + BANK)].bitcast(E2M1), rhs_scale=w_plane[:, n0:n0 + BANK], start=True, stop=True)
+
+        def add_bias(n, i):
+            n0 = BANK * (n % 3)
+            z = new("z%d_%d" % (n, i), [P, BANK], F32, tag="z%d" % ((4 * n + i) % 8))
+            z_tiles[n, i] = z
+            nc.vector.tensor_tensor(out=z[:], in0=banks["y", n, i][:], in1=bias[:, n0:n0 + BANK], op=ALU.add)
+
+        def silu(n, i):
+            nc.scalar.activation(out=act[n][:, i, :], in_=z_tiles[n, i][:], func=ACT.Silu)
+
+        def store(n, lo, hi):
+            a, n0 = n // 3, BANK * (n % 3)
+            nc.sync.dma_start(out=out_v[a, :, lo:hi, n0:n0 + BANK], in_=act[n][:, lo:hi, :])
+
+        out_codes = [new("out_codes%d" % n, [P, BANK], U32) for n in range(6)]
+
+        def planes(n):
+            a, n0 = n // 3, BANK * (n % 3)
+            quantize(out_codes[n][:], out_scales[a][:, n0:n0 + BANK], staged["o%d" % n][:], E4M3)
+
+        def store_codes(n):
+            a, n0 = n // 3, BANK * (n % 3)
+            nc.sync.dma_start(out=out_1[a, :, n0:n0 + BANK, :].rearrange("p n i -> p (n i)").bitcast(I32), in_=out_codes[n][:].bitcast(I32))
+
+        def store_scales(a, queues):
+            for q in range(4):
+                queues[q].dma_start(out=out_2[a, 4 * q:4 * q + 4, :].bitcast(I32), in_=out_scales[a][32 * q:32 * q + 4, :].bitcast(I32))
+
+        cast_dealt("V", "wc", wc_raw, 0, 512)
+        quantize_cols("wc", (wc_q, wc_s), E4M3, 0, 512)
+        cast_rows("V", "c0", c_raw[0], 0, 336)
+        cast_rows("S", "c0", c_raw[0], 336, 512)
+        quantize_cols("c0", c_mx[0], E5M2, 0, 512)
+        pc_matmul(0, 0)
+        cast_dealt("V", "wx", wx_raw, 0, 352)
+        cast_dealt("S", "wx", wx_raw, 352, 512)
+        pc_matmul(0, 1)
+        pc_copy(0, 0)
+        pc_matmul(0, 2)
+        quantize_cols("wx", (wx_q, wx_s), E4M3, 0, 512)
+        pc_copy(0, 1)
+        pc_matmul(0, 3)
+        pc_copy(0, 2)
+        cast_dealt("V", "x0", x_raw[0], 0, 400)
+        cast_dealt("S", "x0", x_raw[0], 400, 512)
+        pc_copy(0, 3)
+        quantize_cols("x0", x_mx[0], E4M3, 0, 128)
+        quantize_cols("x0", x_mx[0], E4M3, 128, 256)
+        quantize_cols("x0", x_mx[0], E4M3, 256, 384)
+        px_matmul(0, 0)
+        quantize_cols("x0", x_mx[0], E4M3, 384, 512)
+        px_matmul(0, 1)
+        product(0, 0)
+        px_matmul(0, 2)
+        product(0, 1)
+        px_matmul(0, 3)
+        cast_rows("S", "c1", c_raw[1], 0, 320)
+        cast_rows("G", "c1", c_raw[1], 320, 512)
+        product(0, 2)
+        product(0, 3)
+        quantize_cols("h0", h_mx[0], E4M3, 0, 128)
+        quantize_cols("h0", h_mx[0], E4M3, 128, 256)
+        quantize_cols("h0", h_mx[0], E4M3, 256, 384)
+        y_matmul(0, 0)
+        quantize_cols("h0", h_mx[0], E4M3, 384, 512)
+        quantize_cols("c1", c_mx[1], E5M2, 0, 512)
+        y_matmul(0, 1)
+        add_bias(0, 0)
+        cast_dealt("G", "x1", x_raw[1], 0, 512)
+        y_matmul(0, 2)
+        add_bias(0, 1)
+        pc_matmul(1, 0)
+        silu(0, 0)
+        y_matmul(0, 3)
+        add_bias(0, 2)
+        pc_matmul(1, 1)
+        silu(0, 1)
+        store(0, 0, 1)
+        y_matmul(1, 0)
+        add_bias(0, 3)
+        pc_matmul(1, 2)
+        pc_copy(1, 0)
+        store(0, 1, 2)
+        y_matmul(1, 1)
+        add_bias(1, 0)
+        pc_matmul(1, 3)
+        silu(0, 2)
+        y_matmul(1, 2)
+        add_bias(1, 1)
+        y_matmul(1, 3)
+        pc_copy(1, 1)
+        store(0, 2, 3)
+        y_matmul(2, 0)
+        quantize_cols("x1", x_mx[1], E4M3, 0, 512)
+        silu(0, 3)
+        y_matmul(2, 1)
+        add_bias(1, 2)
+        pc_copy(1, 2)
+        px_matmul(1, 0)
+        store(0, 3, 4)
+        cast_rows("G", "o0", act[0], 128, 512)
+        px_matmul(1, 1)
+        add_bias(1, 3)
+        pc_copy(1, 3)
+        px_matmul(1, 2)
+        add_bias(2, 0)
+        silu(1, 0)
+        px_matmul(1, 3)
+        product(1, 0)
+        y_matmul(2, 2)
+        silu(1, 1)
+        y_matmul(2, 3)
+        product(1, 1)
+        silu(1, 2)
+        store(1, 0, 2)
+        product(1, 2)
+        silu(1, 3)
+        product(1, 3)
+        silu(2, 0)
+        store(1, 2, 4)
+        cast_rows("S", "o0", act[0], 0, 128)
+        quantize_cols("h1", h_mx[1], E4M3, 0, 128)
+        quantize_cols("h1", h_mx[1], E4M3, 128, 256)
+        add_bias(2, 1)
+        y_matmul(3, 0)
+        quantize_cols("h1", h_mx[1], E4M3, 256, 384)
+        quantize_cols("h1", h_mx[1], E4M3, 384, 512)
+        silu(2, 1)
+        y_matmul(3, 1)
+        add_bias(2, 2)
+        cast_rows("G", "o1", act[1], 0, 512)
+        add_bias(2, 3)
+        store(2, 0, 2)
+        silu(2, 2)
+        y_matmul(3, 2)
+        add_bias(3, 0)
+        silu(2, 3)
+        y_matmul(3, 3)
+        add_bias(3, 1)
+        silu(3, 0)
+        y_matmul(4, 0)
+        store(2, 2, 4)
+        add_bias(3, 2)
+        silu(3, 1)
+        y_matmul(4, 1)
+        store(3, 0, 1)
+        add_bias(3, 3)
+        cast_rows("G", "o2", act[2], 0, 512)
+        silu(3, 2)
+        y_matmul(4, 2)
+        store(3, 1, 2)
+        add_bias(4, 0)
+        silu(3, 3)
+        y_matmul(4, 3)
+        store(3, 2, 3)
+        add_bias(4, 1)
+        silu(4, 0)
+        y_matmul(5, 0)
+        store(3, 3, 4)
+        add_bias(4, 2)
+        silu(4, 1)
+        y_matmul(5, 1)
+        add_bias(4, 3)
+        silu(4, 2)
+        y_matmul(5, 2)
+        store(4, 0, 2)
+        add_bias(5, 0)
+        cast_rows("G", "o3", act[3], 128, 512)
+        silu(4, 3)
+        y_matmul(5, 3)
+        add_bias(5, 1)
+        silu(5, 0)
+        store(4, 2, 4)
+        add_bias(5, 2)
+        silu(5, 1)
+        add_bias(5, 3)
+        silu(5, 2)
+        store(5, 0, 2)
+        planes(0)
+        silu(5, 3)
+        planes(1)
+        cast_rows("S", "o4", act[4], 192, 512)
+        store(5, 2, 4)
+        store_codes(0)
+        planes(2)
+        store_codes(1)
+        cast_rows("V", "o3", act[3], 0, 128)
+        store_codes(2)
+        store_scales(0, [nc.sync] * 4)
+        cast_rows("V", "o4", act[4], 0, 192)
+        cast_rows("S", "o5", act[5], 384, 512)
+        planes(3)
+        cast_rows("V", "o5", act[5], 0, 384)
+        store_codes(3)
+        planes(4)
+        planes(5)
+        store_codes(4)
+        store_codes(5)
+        store_scales(1, [nc.sync, nc.sync, nc.scalar, nc.scalar])

@@ -20,7 +20,7 @@ ACT = mybir.ActivationFunctionType
 P = 128
 HALF = 512
 BANK = 512
-STAGE_TAGS = {"c1": "stage_a", "x1": "stage_a", "o0": "stage_a", "h1": "stage_b", "o1": "stage_b"}
+STAGE_TAGS = {"h0": "stage_a", "c1": "stage_a", "o0": "stage_a", "h1": "stage_b", "o1": "stage_b"}
 
 
 def tile_mix_bilin_tm_pl_silu_kernel(tc, x, wx, c, wc, w_words, w_scales, b, out_0, out_1, out_2):
@@ -50,11 +50,14 @@ def tile_mix_bilin_tm_pl_silu_kernel(tc, x, wx, c, wc, w_words, w_scales, b, out
                 nc.gpsimd.tensor_scalar(out=out, in0=in_, scalar1=1.0, scalar2=-0.0, op0=ALU.mult, op1=ALU.add)
 
         def interleave(engine, dst, raw, lo, hi):
-            cast(engine, dst[:, lo:hi, :], raw[:, :, lo:hi].rearrange("p k t -> p t k"))
+            if engine == "G":
+                cast(engine, dst[:, lo:hi, :], raw[:, :, lo:hi].rearrange("p k t -> p t k"))
+                return
+            cast(engine, dst[:, lo:hi, :].rearrange("p (g e) k -> p g k e", e=4), raw[:, :, lo:hi].rearrange("p k (g e) -> p g k e", e=4))
 
         def deal(engine, dst, raw, lo, hi):
-            cast(engine, dst[:, :, lo:hi, :].rearrange("p j m k -> p m j k"),
-                 raw[:, :, 4 * lo:4 * hi].rearrange("p k (m j) -> p m j k", j=4))
+            cast(engine, dst[:, :, lo:hi, :].rearrange("p j m k -> p m k j"),
+                 raw[:, :, 4 * lo:4 * hi].rearrange("p k (m j) -> p m k j", j=4))
 
         def quantize(codes, scales, values, fmt):
             nc.vector.quantize_mx(out=codes.bitcast(fmt), scales=scales, in_=values)
@@ -74,8 +77,8 @@ def tile_mix_bilin_tm_pl_silu_kernel(tc, x, wx, c, wc, w_words, w_scales, b, out
         nc.vector.memset(w_plane[:].bitcast(I32), 0)
         for q in range(4):
             nc.sync.dma_start(out=w_plane[32 * q:32 * q + 4, :].bitcast(I32), in_=w_scales[0, 4 * q:4 * q + 4, :].bitcast(I32))
-        c_raw.append(load("c_raw1", c[:, HALF:]))
         x_raw.append(load("x_raw1", x[:, HALF:]))
+        c_raw.append(load("c_raw1", c[:, HALF:]))
 
         warm = new("warm", [P, 8], F32)
         nc.vector.memset(warm[:], 0.0)
@@ -145,8 +148,8 @@ def tile_mix_bilin_tm_pl_silu_kernel(tc, x, wx, c, wc, w_words, w_scales, b, out
 
         def product(a, i):
             h = stage("h%d" % a)[:].rearrange("p (i m j) -> p i m j", i=4, j=4)
-            nc.vector.tensor_tensor(out=h[:, i], in0=banks["px", a, i][:].rearrange("p (j m) -> p m j", j=4),
-                                    in1=pc_sb[a][:, :, i, :].rearrange("p j m -> p m j"), op=ALU.mult)
+            nc.vector.tensor_tensor(out=h[:, i].rearrange("p (g e) j -> p g j e", e=2), in0=banks["px", a, i][:].rearrange("p (j g e) -> p g j e", j=4, e=2),
+                                    in1=pc_sb[a][:, :, i, :].rearrange("p j (g e) -> p g j e", e=2), op=ALU.mult)
 
         act = [new("act%d" % n, [P, 4, BANK], F32) for n in range(6)]
         out_v = out_0.rearrange("(a p i) n -> a p i n", a=2, i=4)
@@ -215,62 +218,64 @@ def tile_mix_bilin_tm_pl_silu_kernel(tc, x, wx, c, wc, w_words, w_scales, b, out
         px_matmul(0, 2)
         product(0, 1)
         px_matmul(0, 3)
-        cast_rows("S", "c1", c_raw[1], 0, 320)
-        cast_rows("G", "c1", c_raw[1], 320, 512)
+        cast_dealt("S", "x1", x_raw[1], 128, 512)
         product(0, 2)
         product(0, 3)
+        cast_dealt("V", "x1", x_raw[1], 0, 128)
         quantize_cols("h0", h_mx[0], E4M3, 0, 128)
         quantize_cols("h0", h_mx[0], E4M3, 128, 256)
         quantize_cols("h0", h_mx[0], E4M3, 256, 384)
         y_matmul(0, 0)
         quantize_cols("h0", h_mx[0], E4M3, 384, 512)
-        quantize_cols("c1", c_mx[1], E5M2, 0, 512)
+        quantize_cols("x1", x_mx[1], E4M3, 0, 512)
+        cast_rows("S", "c1", c_raw[1], 0, 224)
         y_matmul(0, 1)
+        cast_rows("G", "c1", c_raw[1], 224, 512)
         add_bias(0, 0)
-        cast_dealt("G", "x1", x_raw[1], 0, 512)
         y_matmul(0, 2)
         add_bias(0, 1)
-        pc_matmul(1, 0)
-        silu(0, 0)
         y_matmul(0, 3)
+        silu(0, 0)
+        y_matmul(1, 0)
         add_bias(0, 2)
-        pc_matmul(1, 1)
+        y_matmul(1, 1)
         silu(0, 1)
         store(0, 0, 1)
-        y_matmul(1, 0)
-        add_bias(0, 3)
-        pc_matmul(1, 2)
-        pc_copy(1, 0)
-        store(0, 1, 2)
-        y_matmul(1, 1)
-        add_bias(1, 0)
-        pc_matmul(1, 3)
-        silu(0, 2)
+        quantize_cols("c1", c_mx[1], E5M2, 0, 512)
         y_matmul(1, 2)
+        silu(0, 2)
+        store(0, 1, 2)
+        add_bias(0, 3)
+        pc_matmul(1, 0)
+        store(0, 2, 3)
+        pc_matmul(1, 1)
+        add_bias(1, 0)
+        pc_matmul(1, 2)
+        silu(0, 3)
+        pc_matmul(1, 3)
         add_bias(1, 1)
         y_matmul(1, 3)
-        pc_copy(1, 1)
-        store(0, 2, 3)
-        y_matmul(2, 0)
-        quantize_cols("x1", x_mx[1], E4M3, 0, 512)
-        silu(0, 3)
-        y_matmul(2, 1)
-        add_bias(1, 2)
-        pc_copy(1, 2)
-        px_matmul(1, 0)
+        pc_copy(1, 0)
         store(0, 3, 4)
-        cast_rows("G", "o0", act[0], 128, 512)
-        px_matmul(1, 1)
+        cast_rows("G", "o0", act[0], 0, 512)
+        y_matmul(2, 0)
+        add_bias(1, 2)
+        pc_copy(1, 1)
+        y_matmul(2, 1)
+        px_matmul(1, 0)
         add_bias(1, 3)
-        pc_copy(1, 3)
-        px_matmul(1, 2)
+        pc_copy(1, 2)
+        px_matmul(1, 1)
         add_bias(2, 0)
+        y_matmul(2, 2)
+        pc_copy(1, 3)
+        y_matmul(2, 3)
+        add_bias(2, 1)
+        px_matmul(1, 2)
         silu(1, 0)
         px_matmul(1, 3)
         product(1, 0)
-        y_matmul(2, 2)
         silu(1, 1)
-        y_matmul(2, 3)
         product(1, 1)
         silu(1, 2)
         store(1, 0, 2)
@@ -279,20 +284,18 @@ def tile_mix_bilin_tm_pl_silu_kernel(tc, x, wx, c, wc, w_words, w_scales, b, out
         product(1, 3)
         silu(2, 0)
         store(1, 2, 4)
-        cast_rows("S", "o0", act[0], 0, 128)
+        silu(2, 1)
         quantize_cols("h1", h_mx[1], E4M3, 0, 128)
         quantize_cols("h1", h_mx[1], E4M3, 128, 256)
-        add_bias(2, 1)
-        y_matmul(3, 0)
-        quantize_cols("h1", h_mx[1], E4M3, 256, 384)
-        quantize_cols("h1", h_mx[1], E4M3, 384, 512)
-        silu(2, 1)
-        y_matmul(3, 1)
         add_bias(2, 2)
-        cast_rows("G", "o1", act[1], 0, 512)
-        add_bias(2, 3)
+        y_matmul(3, 0)
         store(2, 0, 2)
+        quantize_cols("h1", h_mx[1], E4M3, 256, 384)
+        y_matmul(3, 1)
+        quantize_cols("h1", h_mx[1], E4M3, 384, 512)
         silu(2, 2)
+        add_bias(2, 3)
+        cast_rows("G", "o1", act[1], 0, 512)
         y_matmul(3, 2)
         add_bias(3, 0)
         silu(2, 3)
@@ -306,11 +309,11 @@ def tile_mix_bilin_tm_pl_silu_kernel(tc, x, wx, c, wc, w_words, w_scales, b, out
         y_matmul(4, 1)
         store(3, 0, 1)
         add_bias(3, 3)
-        cast_rows("G", "o2", act[2], 0, 512)
         silu(3, 2)
         y_matmul(4, 2)
         store(3, 1, 2)
         add_bias(4, 0)
+        cast_rows("G", "o2", act[2], 0, 512)
         silu(3, 3)
         y_matmul(4, 3)
         store(3, 2, 3)
@@ -326,10 +329,10 @@ def tile_mix_bilin_tm_pl_silu_kernel(tc, x, wx, c, wc, w_words, w_scales, b, out
         y_matmul(5, 2)
         store(4, 0, 2)
         add_bias(5, 0)
-        cast_rows("G", "o3", act[3], 128, 512)
         silu(4, 3)
         y_matmul(5, 3)
         add_bias(5, 1)
+        cast_rows("G", "o3", act[3], 224, 512)
         silu(5, 0)
         store(4, 2, 4)
         add_bias(5, 2)
@@ -345,7 +348,7 @@ def tile_mix_bilin_tm_pl_silu_kernel(tc, x, wx, c, wc, w_words, w_scales, b, out
         store_codes(0)
         planes(2)
         store_codes(1)
-        cast_rows("V", "o3", act[3], 0, 128)
+        cast_rows("V", "o3", act[3], 0, 224)
         store_codes(2)
         store_scales(0, [nc.sync] * 4)
         cast_rows("V", "o4", act[4], 0, 192)

@@ -71,13 +71,13 @@ def tile_mix_bilin_tm_pl_silu_kernel(tc, x, wx, c, wc, w_words, w_scales, b, out
         c_raw = [load("c_raw0", c[:, :HALF])]
         wx_raw = load("wx_raw", wx)
         x_raw = [load("x_raw0", x[:, :HALF])]
+        x_raw.append(load("x_raw1", x[:, HALF:]))
         w_codes = new("w_codes", [P, 2 * M], U8)
         nc.sync.dma_start(out=w_codes[:].bitcast(I32), in_=w_words[0].bitcast(I32))
         w_plane = new("w_plane", [P, M], U8)
         nc.vector.memset(w_plane[:].bitcast(I32), 0)
         for q in range(4):
             nc.sync.dma_start(out=w_plane[32 * q:32 * q + 4, :].bitcast(I32), in_=w_scales[0, 4 * q:4 * q + 4, :].bitcast(I32))
-        x_raw.append(load("x_raw1", x[:, HALF:]))
         c_raw.append(load("c_raw1", c[:, HALF:]))
 
         warm = new("warm", [P, 8], F32)
@@ -103,7 +103,7 @@ def tile_mix_bilin_tm_pl_silu_kernel(tc, x, wx, c, wc, w_words, w_scales, b, out
         x_mx = [mx("x%d" % a, HALF) for a in range(2)]
         h_mx = [mx("h%d" % a, HALF) for a in range(2)]
         pc_sb = [new("pc%d" % a, [P, 4, 4, P], F32) for a in range(2)]
-        out_scales = [new("out_scales%d" % a, [P, M], U8) for a in range(2)]
+        out_scales = new("out_scales", [P, 2, M], U8)
 
         def flat(t):
             return t.rearrange("p a b -> p (a b)")
@@ -176,37 +176,46 @@ def tile_mix_bilin_tm_pl_silu_kernel(tc, x, wx, c, wc, w_words, w_scales, b, out
             a, n0 = n // 3, BANK * (n % 3)
             nc.sync.dma_start(out=out_v[a, :, lo:hi, n0:n0 + BANK], in_=act[n][:, lo:hi, :])
 
-        out_codes = [new("out_codes%d" % n, [P, BANK], U32) for n in range(6)]
+        pieces = [(0, 0, 512), (1, 0, 512), (2, 0, 512), (3, 0, 512), (4, 0, 512), (5, 0, 256), (5, 256, 256)]
+        out_codes = [new("out_codes%d" % n, [P, piece[2]], U32) for n, piece in enumerate(pieces)]
 
-        def planes(n):
-            a, n0 = n // 3, BANK * (n % 3)
-            quantize(out_codes[n][:], out_scales[a][:, n0:n0 + BANK], staged["o%d" % n][:], E4M3)
+        def cast_out(engine, k, lo, hi):
+            n, off, w = pieces[k]
+            cast_rows(engine, "o%d" % k, act[n][:, :, off:off + w], lo, hi)
 
-        def store_codes(n):
-            a, n0 = n // 3, BANK * (n % 3)
-            nc.sync.dma_start(out=out_1[a, :, n0:n0 + BANK, :].rearrange("p n i -> p (n i)").bitcast(I32), in_=out_codes[n][:].bitcast(I32))
+        def planes(k):
+            n, off, w = pieces[k]
+            a, n0 = n // 3, BANK * (n % 3) + off
+            quantize(out_codes[k][:], out_scales[:, a, n0:n0 + w], staged["o%d" % k][:, :4 * w], E4M3)
 
-        def store_scales(a, queues):
+        def store_codes(k):
+            n, off, w = pieces[k]
+            a, n0 = n // 3, BANK * (n % 3) + off
+            nc.sync.dma_start(out=out_1[a, :, n0:n0 + w, :].rearrange("p n i -> p (n i)").bitcast(I32), in_=out_codes[k][:].bitcast(I32))
+
+        def store_scales(queues):
             for q in range(4):
-                queues[q].dma_start(out=out_2[a, 4 * q:4 * q + 4, :].bitcast(I32), in_=out_scales[a][32 * q:32 * q + 4, :].bitcast(I32))
+                queues[q].dma_start(out=out_2[:, 4 * q:4 * q + 4, :].rearrange("a r n -> r a n").bitcast(I32),
+                                    in_=out_scales[32 * q:32 * q + 4].bitcast(I32))
 
-        cast_dealt("V", "wc", wc_raw, 0, 512)
+        cast_dealt("V", "wc", wc_raw, 0, 336)
+        cast_dealt("S", "wc", wc_raw, 336, 512)
         quantize_cols("wc", (wc_q, wc_s), E4M3, 0, 512)
         cast_rows("V", "c0", c_raw[0], 0, 336)
         cast_rows("S", "c0", c_raw[0], 336, 512)
         quantize_cols("c0", c_mx[0], E5M2, 0, 512)
         pc_matmul(0, 0)
-        cast_dealt("V", "wx", wx_raw, 0, 352)
-        cast_dealt("S", "wx", wx_raw, 352, 512)
+        cast_dealt("V", "wx", wx_raw, 0, 336)
+        cast_dealt("S", "wx", wx_raw, 336, 512)
         pc_matmul(0, 1)
-        pc_copy(0, 0)
         pc_matmul(0, 2)
+        pc_copy(0, 0)
         quantize_cols("wx", (wx_q, wx_s), E4M3, 0, 512)
-        pc_copy(0, 1)
         pc_matmul(0, 3)
+        pc_copy(0, 1)
         pc_copy(0, 2)
-        cast_dealt("V", "x0", x_raw[0], 0, 400)
-        cast_dealt("S", "x0", x_raw[0], 400, 512)
+        cast_dealt("V", "x0", x_raw[0], 0, 352)
+        cast_dealt("S", "x0", x_raw[0], 352, 512)
         pc_copy(0, 3)
         quantize_cols("x0", x_mx[0], E4M3, 0, 128)
         quantize_cols("x0", x_mx[0], E4M3, 128, 256)
@@ -215,111 +224,112 @@ def tile_mix_bilin_tm_pl_silu_kernel(tc, x, wx, c, wc, w_words, w_scales, b, out
         quantize_cols("x0", x_mx[0], E4M3, 384, 512)
         px_matmul(0, 1)
         product(0, 0)
+        cast_dealt("S", "x1", x_raw[1], 0, 512)
         px_matmul(0, 2)
         product(0, 1)
         px_matmul(0, 3)
-        cast_dealt("S", "x1", x_raw[1], 128, 512)
-        product(0, 2)
-        product(0, 3)
-        cast_dealt("V", "x1", x_raw[1], 0, 128)
         quantize_cols("h0", h_mx[0], E4M3, 0, 128)
-        quantize_cols("h0", h_mx[0], E4M3, 128, 256)
-        quantize_cols("h0", h_mx[0], E4M3, 256, 384)
+        product(0, 2)
         y_matmul(0, 0)
-        quantize_cols("h0", h_mx[0], E4M3, 384, 512)
-        quantize_cols("x1", x_mx[1], E4M3, 0, 512)
-        cast_rows("S", "c1", c_raw[1], 0, 224)
+        quantize_cols("h0", h_mx[0], E4M3, 128, 256)
+        product(0, 3)
         y_matmul(0, 1)
-        cast_rows("G", "c1", c_raw[1], 224, 512)
         add_bias(0, 0)
-        y_matmul(0, 2)
-        add_bias(0, 1)
-        y_matmul(0, 3)
+        quantize_cols("h0", h_mx[0], E4M3, 256, 384)
+        quantize_cols("h0", h_mx[0], E4M3, 384, 512)
         silu(0, 0)
+        quantize_cols("x1", x_mx[1], E4M3, 0, 512)
+        y_matmul(0, 2)
+        cast_rows("S", "c1", c_raw[1], 0, 272)
+        add_bias(0, 1)
+        cast_rows("G", "c1", c_raw[1], 272, 512)
+        y_matmul(0, 3)
+        store(0, 0, 1)
         y_matmul(1, 0)
         add_bias(0, 2)
         y_matmul(1, 1)
-        silu(0, 1)
-        store(0, 0, 1)
-        quantize_cols("c1", c_mx[1], E5M2, 0, 512)
-        y_matmul(1, 2)
-        silu(0, 2)
-        store(0, 1, 2)
         add_bias(0, 3)
+        silu(0, 1)
+        y_matmul(1, 2)
+        quantize_cols("c1", c_mx[1], E5M2, 0, 512)
+        silu(0, 2)
+        y_matmul(1, 3)
+        store(0, 1, 2)
+        add_bias(1, 0)
+        silu(0, 3)
         pc_matmul(1, 0)
         store(0, 2, 3)
         pc_matmul(1, 1)
-        add_bias(1, 0)
-        pc_matmul(1, 2)
-        silu(0, 3)
-        pc_matmul(1, 3)
         add_bias(1, 1)
-        y_matmul(1, 3)
-        pc_copy(1, 0)
-        store(0, 3, 4)
-        cast_rows("G", "o0", act[0], 0, 512)
-        y_matmul(2, 0)
-        add_bias(1, 2)
-        pc_copy(1, 1)
-        y_matmul(2, 1)
-        px_matmul(1, 0)
-        add_bias(1, 3)
-        pc_copy(1, 2)
-        px_matmul(1, 1)
-        add_bias(2, 0)
-        y_matmul(2, 2)
-        pc_copy(1, 3)
-        y_matmul(2, 3)
-        add_bias(2, 1)
-        px_matmul(1, 2)
+        pc_matmul(1, 2)
         silu(1, 0)
+        store(0, 3, 4)
+        cast_out("G", 0, 0, 512)
+        pc_matmul(1, 3)
+        add_bias(1, 2)
+        y_matmul(2, 0)
+        pc_copy(1, 0)
+        y_matmul(2, 1)
+        add_bias(1, 3)
+        pc_copy(1, 1)
+        y_matmul(2, 2)
+        px_matmul(1, 0)
+        add_bias(2, 0)
+        pc_copy(1, 2)
+        y_matmul(2, 3)
+        px_matmul(1, 1)
+        add_bias(2, 1)
+        pc_copy(1, 3)
+        px_matmul(1, 2)
+        add_bias(2, 2)
+        silu(1, 1)
         px_matmul(1, 3)
         product(1, 0)
-        silu(1, 1)
-        product(1, 1)
         silu(1, 2)
         store(1, 0, 2)
-        product(1, 2)
+        product(1, 1)
         silu(1, 3)
-        product(1, 3)
-        silu(2, 0)
-        store(1, 2, 4)
-        silu(2, 1)
         quantize_cols("h1", h_mx[1], E4M3, 0, 128)
-        quantize_cols("h1", h_mx[1], E4M3, 128, 256)
-        add_bias(2, 2)
+        silu(2, 0)
+        product(1, 2)
+        store(1, 2, 4)
         y_matmul(3, 0)
-        store(2, 0, 2)
-        quantize_cols("h1", h_mx[1], E4M3, 256, 384)
+        silu(2, 1)
+        quantize_cols("h1", h_mx[1], E4M3, 128, 256)
+        product(1, 3)
         y_matmul(3, 1)
-        quantize_cols("h1", h_mx[1], E4M3, 384, 512)
         silu(2, 2)
+        store(2, 0, 2)
         add_bias(2, 3)
-        cast_rows("G", "o1", act[1], 0, 512)
-        y_matmul(3, 2)
-        add_bias(3, 0)
+        planes(0)
         silu(2, 3)
-        y_matmul(3, 3)
-        add_bias(3, 1)
-        silu(3, 0)
-        y_matmul(4, 0)
+        quantize_cols("h1", h_mx[1], E4M3, 256, 384)
+        quantize_cols("h1", h_mx[1], E4M3, 384, 512)
+        store_codes(0)
+        add_bias(3, 0)
+        y_matmul(3, 2)
         store(2, 2, 4)
+        cast_out("G", 1, 0, 512)
+        add_bias(3, 1)
+        y_matmul(3, 3)
+        silu(3, 0)
         add_bias(3, 2)
+        y_matmul(4, 0)
         silu(3, 1)
-        y_matmul(4, 1)
         store(3, 0, 1)
         add_bias(3, 3)
+        y_matmul(4, 1)
         silu(3, 2)
         y_matmul(4, 2)
         store(3, 1, 2)
         add_bias(4, 0)
-        cast_rows("G", "o2", act[2], 0, 512)
         silu(3, 3)
         y_matmul(4, 3)
         store(3, 2, 3)
         add_bias(4, 1)
         silu(4, 0)
         y_matmul(5, 0)
+        cast_out("G", 2, 0, 512)
         store(3, 3, 4)
         add_bias(4, 2)
         silu(4, 1)
@@ -332,7 +342,6 @@ def tile_mix_bilin_tm_pl_silu_kernel(tc, x, wx, c, wc, w_words, w_scales, b, out
         silu(4, 3)
         y_matmul(5, 3)
         add_bias(5, 1)
-        cast_rows("G", "o3", act[3], 224, 512)
         silu(5, 0)
         store(4, 2, 4)
         add_bias(5, 2)
@@ -340,24 +349,25 @@ def tile_mix_bilin_tm_pl_silu_kernel(tc, x, wx, c, wc, w_words, w_scales, b, out
         add_bias(5, 3)
         silu(5, 2)
         store(5, 0, 2)
-        planes(0)
-        silu(5, 3)
         planes(1)
-        cast_rows("S", "o4", act[4], 192, 512)
-        store(5, 2, 4)
-        store_codes(0)
+        silu(5, 3)
         planes(2)
+        cast_out("S", 4, 48, 512)
+        store(5, 2, 4)
         store_codes(1)
-        cast_rows("V", "o3", act[3], 0, 224)
+        cast_out("V", 3, 0, 512)
         store_codes(2)
-        store_scales(0, [nc.sync] * 4)
-        cast_rows("V", "o4", act[4], 0, 192)
-        cast_rows("S", "o5", act[5], 384, 512)
+        cast_out("V", 4, 0, 48)
         planes(3)
-        cast_rows("V", "o5", act[5], 0, 384)
+        cast_out("S", 5, 96, 256)
+        cast_out("V", 5, 0, 96)
         store_codes(3)
         planes(4)
-        planes(5)
+        cast_out("S", 6, 128, 256)
+        cast_out("V", 6, 0, 128)
         store_codes(4)
+        planes(5)
+        planes(6)
         store_codes(5)
-        store_scales(1, [nc.sync, nc.sync, nc.scalar, nc.scalar])
+        store_codes(6)
+        store_scales([nc.sync, nc.sync, nc.scalar, nc.scalar])

@@ -18,356 +18,256 @@ ALU = mybir.AluOpType
 ACT = mybir.ActivationFunctionType
 
 P = 128
-HALF = 512
-BANK = 512
-STAGE_TAGS = {"h0": "stage_a", "c1": "stage_a", "o0": "stage_a", "h1": "stage_b", "o1": "stage_b"}
+PACK = 4
+HALF = P * PACK
+COLS = 512
+CHUNKS = M // COLS
+
+TILE_ORDER = [(0, i) for i in range(PACK)] + [(chunk, i) for i in range(PACK) for chunk in (1, 2)]
+Y_BANKS = 4
+Z_BUFS = 8
+
+C0_SPLIT = 336
+WX_SPLIT = 336
+X0_SPLIT = 352
+OUT_02_SPLIT = 224
+OUT_10_SPLIT = 272
+OUT_11_SPLIT = 192
+OUT_12_SPLITS = (96, 96)
 
 
 def tile_mix_bilin_tm_pl_silu_kernel(tc, x, wx, c, wc, w_words, w_scales, b, out_0, out_1, out_2):
     nc = tc.nc
     with ExitStack() as ctx:
-        sb = ctx.enter_context(tc.tile_pool(name="sb", bufs=1))
+        sbuf = ctx.enter_context(tc.tile_pool(name="sbuf", bufs=1))
         psum = ctx.enter_context(tc.psum_pool(name="psum", bufs=1))
         ctx.enter_context(tc.manual_schedule())
 
-        def new(name, shape, dtype, tag=None, bufs=1):
-            return sb.tile(shape, dtype, name=name, tag=tag or name, bufs=bufs, align_bytes=64)
+        def new_tile(name, shape, dtype, tag=None):
+            return sbuf.tile(shape, dtype, name=name, tag=tag or name, align_bytes=64)
 
-        def new_bank(name, n):
-            return psum.tile([P, BANK], F32, name=name, tag="bank%d" % n)
+        def new_bank(name, bank):
+            return psum.tile([P, COLS], F32, name=name, tag="bank%d" % bank)
 
-        def load(name, src):
-            raw = new(name, [P, 4, src.shape[1]], F32)
-            nc.sync.dma_start(out=raw[:], in_=src.rearrange("(p k) t -> p k t", k=4))
+        def new_mx(name, width):
+            return new_tile(name + "_codes", [P, width], U32), new_tile(name + "_scales", [P, width], U8)
+
+        def new_rounded(name, width=HALF, tag=None):
+            return new_tile(name + "_bf16", [P, PACK * width], BF16, tag)
+
+        def load_rows(name, rows):
+            raw = new_tile(name, [P, PACK, rows.shape[1]], F32)
+            nc.sync.dma_start(out=raw[:], in_=rows.rearrange("(p e) n -> p e n", e=PACK))
             return raw
 
-        def cast(engine, out, in_):
-            if engine == "V":
-                nc.vector.tensor_copy(out=out, in_=in_)
-            elif engine == "S":
-                nc.scalar.copy(out=out, in_=in_)
-            else:
-                nc.gpsimd.tensor_scalar(out=out, in0=in_, scalar1=1.0, scalar2=-0.0, op0=ALU.mult, op1=ALU.add)
+        def interleave(copy, rounded, raw, lo, hi):
+            out = rounded[:, PACK * lo:PACK * hi].rearrange("p (g u e) -> p g e u", u=4, e=PACK)
+            copy(out=out, in_=raw[:, :, lo:hi].rearrange("p e (g u) -> p g e u", u=4))
 
-        def interleave(engine, dst, raw, lo, hi):
-            if engine == "G":
-                cast(engine, dst[:, lo:hi, :], raw[:, :, lo:hi].rearrange("p k t -> p t k"))
-                return
-            cast(engine, dst[:, lo:hi, :].rearrange("p (g e) k -> p g k e", e=4), raw[:, :, lo:hi].rearrange("p k (g e) -> p g k e", e=4))
+        def interleave_on_gpsimd(rounded, raw, lo, hi):
+            out = rounded[:, PACK * lo:PACK * hi].rearrange("p (n e) -> p n e", e=PACK)
+            nc.gpsimd.tensor_scalar(out=out, in0=raw[:, :, lo:hi].rearrange("p e n -> p n e"),
+                                    scalar1=1.0, scalar2=-0.0, op0=ALU.mult, op1=ALU.add)
 
-        def deal(engine, dst, raw, lo, hi):
-            cast(engine, dst[:, :, lo:hi, :].rearrange("p j m k -> p m k j"),
-                 raw[:, :, 4 * lo:4 * hi].rearrange("p k (m j) -> p m k j", j=4))
+        def deal(copy, rounded, raw, lo, hi):
+            out = rounded[:].rearrange("p (j m e) -> p m e j", j=PACK, e=PACK)[:, lo // PACK:hi // PACK]
+            copy(out=out, in_=raw[:, :, lo:hi].rearrange("p e (m j) -> p m e j", j=PACK))
 
-        def quantize(codes, scales, values, fmt):
-            nc.vector.quantize_mx(out=codes.bitcast(fmt), scales=scales, in_=values)
+        def quantize(mx, rounded, fmt, lo=0, hi=HALF):
+            codes, scales = mx
+            nc.vector.quantize_mx(out=codes[:, lo:hi].bitcast(fmt), scales=scales[:, lo:hi], in_=rounded[:, PACK * lo:PACK * hi])
 
-        def mx(name, width):
-            return new(name + "_codes", [P, width], U32), new(name + "_scales", [P, width], U8)
+        def dealt_cols(j):
+            return slice(P * j, P * (j + 1))
 
-        b_cols = new("b_cols", [P, M // P], F32)
-        nc.scalar.dma_start(out=b_cols[:], in_=b.rearrange("(p c) -> p c", p=P))
-        wc_raw = load("wc_raw", wc)
-        c_raw = [load("c_raw0", c[:, :HALF])]
-        wx_raw = load("wx_raw", wx)
-        x_raw = [load("x_raw0", x[:, :HALF])]
-        x_raw.append(load("x_raw1", x[:, HALF:]))
-        w_codes = new("w_codes", [P, 2 * M], U8)
+        on_vector, on_scalar = nc.vector.tensor_copy, nc.scalar.copy
+
+        b_per_row = M // P
+        b_rows = new_tile("b_rows", [P, b_per_row], F32)
+        nc.sync.dma_start(out=b_rows[:], in_=b.rearrange("(p s) -> p s", p=P))
+        wc_raw = load_rows("wc_raw", wc)
+        c0_raw = load_rows("c0_raw", c[:, :HALF])
+        wx_raw = load_rows("wx_raw", wx)
+        x0_raw = load_rows("x0_raw", x[:, :HALF])
+        x1_raw = load_rows("x1_raw", x[:, HALF:])
+        w_codes = new_tile("w_codes", [P, 2 * M], U8)
         nc.sync.dma_start(out=w_codes[:].bitcast(I32), in_=w_words[0].bitcast(I32))
-        w_plane = new("w_plane", [P, M], U8)
+        w_plane = new_tile("w_plane", [P, M], U8)
         nc.vector.memset(w_plane[:].bitcast(I32), 0)
-        for q in range(4):
-            nc.sync.dma_start(out=w_plane[32 * q:32 * q + 4, :].bitcast(I32), in_=w_scales[0, 4 * q:4 * q + 4, :].bitcast(I32))
-        c_raw.append(load("c_raw1", c[:, HALF:]))
+        for quad in range(4):
+            nc.sync.dma_start(out=w_plane[32 * quad:32 * quad + 4, :].bitcast(I32),
+                              in_=w_scales[0, 4 * quad:4 * quad + 4, :].bitcast(I32))
+        c1_raw = load_rows("c1_raw", c[:, HALF:])
 
-        warm = new("warm", [P, 8], F32)
-        nc.vector.memset(warm[:], 0.0)
-        warm_out = new("warm_out", [P, 8], F32)
-        nc.scalar.activation(out=warm_out[:], in_=warm[:], func=ACT.Silu)
-
-        ident = new("ident", [P, P], F32)
+        ident = new_tile("ident", [P, P], F32)
         make_identity(nc, ident[:])
+        bias = new_tile("bias", [P, M], F32)
+        bias_ns = bias[:].rearrange("p (n s) -> p n s", s=b_per_row)
+        for group in range(b_per_row // 4):
+            bank = new_bank("bias%d" % group, group)
+            for u in range(4):
+                s = 4 * group + u
+                nc.tensor.transpose(bank[:, P * u:P * (u + 1)], b_rows[:, s:s + 1].to_broadcast([P, P]), ident[:])
+            nc.scalar.copy(out=bias_ns[:, :, 4 * group:4 * group + 4], in_=bank[:].rearrange("p (u n) -> p n u", u=4))
 
-        bias = new("bias", [P, M], F32)
-        bias_v = bias[:].rearrange("p (n c) -> p n c", c=M // P)
-        for g in range(3):
-            bank = new_bank("bias%d" % g, g)
-            for e in range(4):
-                col = 4 * g + e
-                nc.tensor.transpose(bank[:, P * e:P * (e + 1)], b_cols[:, col:col + 1].to_broadcast([P, P]), ident[:])
-            nc.scalar.copy(out=bias_v[:, :, 4 * g:4 * g + 4], in_=bank[:].rearrange("p (e n) -> p n e", e=4))
-
-        wc_q, wc_s = mx("wc", R)
-        wx_q, wx_s = mx("wx", R)
-        c_mx = [mx("c%d" % a, HALF) for a in range(2)]
-        x_mx = [mx("x%d" % a, HALF) for a in range(2)]
-        h_mx = [mx("h%d" % a, HALF) for a in range(2)]
-        pc_sb = [new("pc%d" % a, [P, 4, 4, P], F32) for a in range(2)]
-        out_scales = new("out_scales", [P, 2, M], U8)
-
-        def flat(t):
-            return t.rearrange("p a b -> p (a b)")
-
-        staged = {}
-
-        def stage(name):
-            if name not in staged:
-                staged[name] = new(name + "_bf", [P, 2048], BF16, tag=STAGE_TAGS.get(name, name + "_bf"))
-            return staged[name]
-
-        def cast_rows(engine, name, raw, lo, hi):
-            interleave(engine, stage(name)[:].rearrange("p (t k) -> p t k", k=4), raw, lo, hi)
-
-        def cast_dealt(engine, name, raw, lo, hi):
-            deal(engine, stage(name)[:].rearrange("p (j m k) -> p j m k", j=4, k=4), raw, lo // 4, hi // 4)
-
-        def quantize_cols(name, pair, fmt, lo, hi):
-            quantize(pair[0][:, lo:hi], pair[1][:, lo:hi], staged[name][:, 4 * lo:4 * hi], fmt)
-
-        banks = {}
+        wc_mx, wx_mx = new_mx("wc", R), new_mx("wx", R)
+        c_mx = [new_mx("c%d" % a, HALF) for a in range(2)]
+        x_mx = [new_mx("x%d" % a, HALF) for a in range(2)]
+        h_mx = [new_mx("h%d" % a, HALF) for a in range(2)]
+        pc_dealt = [new_tile("pc%d" % a, [P, PACK, PACK, P], F32) for a in range(2)]
+        result = [new_tile("result%d" % a, [P, PACK, M], F32) for a in range(2)]
+        out_scales = new_tile("out_scales", [P, 2, M], U8)
+        out_rows = out_0.rearrange("(a p i) n -> a p i n", a=2, i=PACK)
+        pc_banks, px_banks, y_banks, biased = {}, {}, {}, {}
 
         def pc_matmul(a, j):
-            bank = new_bank("pc%d_%d" % (a, j), 4 + j)
-            cols = slice(P * j, P * (j + 1))
-            nc.tensor.matmul_mx(out=bank[:], lhsT=wc_q[:, cols].bitcast(E4M3), lhsT_scale=wc_s[:, cols],
+            pc_banks[a, j] = new_bank("pc%d_%d" % (a, j), 4 + j)
+            cols = dealt_cols(j)
+            nc.tensor.matmul_mx(out=pc_banks[a, j][:], lhsT=wc_mx[0][:, cols].bitcast(E4M3), lhsT_scale=wc_mx[1][:, cols],
                                 rhs=c_mx[a][0][:].bitcast(E5M2), rhs_scale=c_mx[a][1][:], start=True, stop=True)
-            banks["pc", a, j] = bank
 
         def pc_copy(a, j):
-            bank = banks["pc", a, j]
-            nc.scalar.copy(out=pc_sb[a][:, j], in_=bank[:].rearrange("p (m i) -> p i m", i=4))
+            nc.scalar.copy(out=pc_dealt[a][:, j], in_=pc_banks[a, j][:].rearrange("p (m i) -> p i m", i=PACK))
 
-        def px_matmul(a, q):
-            bank = new_bank("px%d_%d" % (a, q), 4 * a + q)
-            tok = slice(P * q, P * (q + 1))
-            for j in range(4):
-                cols = slice(P * j, P * (j + 1))
-                nc.tensor.matmul_mx(out=bank[:, cols], lhsT=wx_q[:, cols].bitcast(E4M3), lhsT_scale=wx_s[:, cols],
-                                    rhs=x_mx[a][0][:, tok].bitcast(E4M3), rhs_scale=x_mx[a][1][:, tok], start=True, stop=True)
-            banks["px", a, q] = bank
+        def px_matmul(a, i):
+            px_banks[a, i] = new_bank("px%d_%d" % (a, i), 4 * a + i)
+            tokens = dealt_cols(i)
+            for j in range(PACK):
+                cols = dealt_cols(j)
+                nc.tensor.matmul_mx(out=px_banks[a, i][:, cols], lhsT=wx_mx[0][:, cols].bitcast(E4M3), lhsT_scale=wx_mx[1][:, cols],
+                                    rhs=x_mx[a][0][:, tokens].bitcast(E4M3), rhs_scale=x_mx[a][1][:, tokens], start=True, stop=True)
 
-        def product(a, i):
-            h = stage("h%d" % a)[:].rearrange("p (i m j) -> p i m j", i=4, j=4)
-            nc.vector.tensor_tensor(out=h[:, i].rearrange("p (g e) j -> p g j e", e=2), in0=banks["px", a, i][:].rearrange("p (j g e) -> p g j e", j=4, e=2),
-                                    in1=pc_sb[a][:, :, i, :].rearrange("p j (g e) -> p g j e", e=2), op=ALU.mult)
+        def product(h_rounded, a, i):
+            out = h_rounded[:, HALF * i:HALF * (i + 1)].rearrange("p (g u j) -> p g j u", u=2, j=PACK)
+            nc.vector.tensor_tensor(out=out, in0=px_banks[a, i][:].rearrange("p (j g u) -> p g j u", j=PACK, u=2),
+                                    in1=pc_dealt[a][:, :, i, :].rearrange("p j (g u) -> p g j u", u=2), op=ALU.mult)
 
-        act = [new("act%d" % n, [P, 4, BANK], F32) for n in range(6)]
-        out_v = out_0.rearrange("(a p i) n -> a p i n", a=2, i=4)
-        z_tiles = {}
+        def quantize_tokens(mx, rounded, i):
+            quantize(mx, rounded, E4M3, P * i, P * (i + 1))
 
-        def y_matmul(n, i):
-            a, n0 = n // 3, BANK * (n % 3)
-            bank = new_bank("y%d_%d" % (n, i), i)
-            banks["y", n, i] = bank
-            cols = slice(P * i, P * (i + 1))
-            nc.tensor.matmul_mx(out=bank[:], lhsT=h_mx[a][0][:, cols].bitcast(E4M3), lhsT_scale=h_mx[a][1][:, cols],
-                                rhs=w_codes[:, 2 * n0:2 * (n0 + BANK)].bitcast(E2M1), rhs_scale=w_plane[:, n0:n0 + BANK], start=True, stop=True)
+        def y_matmul(a, step):
+            chunk, i = TILE_ORDER[step]
+            y_banks[a, step] = new_bank("y%d_%d" % (a, step), step % Y_BANKS)
+            tokens, n0 = dealt_cols(i), COLS * chunk
+            nc.tensor.matmul_mx(out=y_banks[a, step][:], lhsT=h_mx[a][0][:, tokens].bitcast(E4M3), lhsT_scale=h_mx[a][1][:, tokens],
+                                rhs=w_codes[:, 2 * n0:2 * (n0 + COLS)].bitcast(E2M1), rhs_scale=w_plane[:, n0:n0 + COLS],
+                                start=True, stop=True)
 
-        def add_bias(n, i):
-            n0 = BANK * (n % 3)
-            z = new("z%d_%d" % (n, i), [P, BANK], F32, tag="z%d" % ((4 * n + i) % 8))
-            z_tiles[n, i] = z
-            nc.vector.tensor_tensor(out=z[:], in0=banks["y", n, i][:], in1=bias[:, n0:n0 + BANK], op=ALU.add)
+        def add_bias(a, step):
+            n0 = COLS * TILE_ORDER[step][0]
+            slot = (len(TILE_ORDER) * a + step) % Z_BUFS
+            biased[a, step] = new_tile("biased%d_%d" % (a, step), [P, COLS], F32, "biased%d" % slot)
+            nc.vector.tensor_tensor(out=biased[a, step][:], in0=y_banks[a, step][:], in1=bias[:, n0:n0 + COLS], op=ALU.add)
+            if step + Y_BANKS < len(TILE_ORDER):
+                y_matmul(a, step + Y_BANKS)
 
-        def silu(n, i):
-            nc.scalar.activation(out=act[n][:, i, :], in_=z_tiles[n, i][:], func=ACT.Silu)
+        def silu(a, step):
+            chunk, i = TILE_ORDER[step]
+            nc.scalar.activation(out=result[a][:, i, COLS * chunk:COLS * (chunk + 1)], in_=biased[a, step][:], func=ACT.Silu)
+            if chunk != 1:
+                cols = slice(0, COLS) if chunk == 0 else slice(COLS, M)
+                nc.sync.dma_start(out=out_rows[a, :, i, cols], in_=result[a][:, i, cols])
 
-        def store(n, lo, hi):
-            a, n0 = n // 3, BANK * (n % 3)
-            nc.sync.dma_start(out=out_v[a, :, lo:hi, n0:n0 + BANK], in_=act[n][:, lo:hi, :])
+        def result_cols(a, n0, width=COLS):
+            return result[a][:, :, n0:n0 + width]
 
-        pieces = [(0, 0, 512), (1, 0, 512), (2, 0, 512), (3, 0, 512), (4, 0, 512), (5, 0, 256), (5, 256, 256)]
-        out_codes = [new("out_codes%d" % n, [P, piece[2]], U32) for n, piece in enumerate(pieces)]
+        def hand_on(rounded, a, n0, width=COLS):
+            codes = new_tile("out_codes%d_%d" % (a, n0), [P, width], U32)
+            nc.vector.quantize_mx(out=codes[:].bitcast(E4M3), scales=out_scales[:, a, n0:n0 + width], in_=rounded[:])
+            nc.sync.dma_start(out=out_1[a, :, n0:n0 + width, :].rearrange("p n i -> p (n i)").bitcast(I32), in_=codes[:].bitcast(I32))
 
-        def cast_out(engine, k, lo, hi):
-            n, off, w = pieces[k]
-            cast_rows(engine, "o%d" % k, act[n][:, :, off:off + w], lo, hi)
+        wc_rounded = new_rounded("wc")
+        deal(on_vector, wc_rounded, wc_raw, 0, R)
+        quantize(wc_mx, wc_rounded, E4M3)
+        c0_rounded = new_rounded("c0")
+        interleave(on_vector, c0_rounded, c0_raw, 0, C0_SPLIT)
+        interleave(on_scalar, c0_rounded, c0_raw, C0_SPLIT, HALF)
+        quantize(c_mx[0], c0_rounded, E5M2)
+        for j in range(PACK):
+            pc_matmul(0, j)
+        wx_rounded = new_rounded("wx")
+        deal(on_vector, wx_rounded, wx_raw, 0, WX_SPLIT)
+        deal(on_scalar, wx_rounded, wx_raw, WX_SPLIT, R)
+        quantize(wx_mx, wx_rounded, E4M3)
+        for j in range(PACK - 1):
+            pc_copy(0, j)
+        x0_rounded = new_rounded("x0")
+        deal(on_vector, x0_rounded, x0_raw, 0, X0_SPLIT)
+        deal(on_scalar, x0_rounded, x0_raw, X0_SPLIT, HALF)
+        pc_copy(0, PACK - 1)
+        for i in range(PACK):
+            quantize_tokens(x_mx[0], x0_rounded, i)
+            px_matmul(0, i)
+        x1_rounded = new_rounded("x1")
+        deal(on_scalar, x1_rounded, x1_raw, 0, HALF)
 
-        def planes(k):
-            n, off, w = pieces[k]
-            a, n0 = n // 3, BANK * (n % 3) + off
-            quantize(out_codes[k][:], out_scales[:, a, n0:n0 + w], staged["o%d" % k][:, :4 * w], E4M3)
+        h0_rounded = new_rounded("h0", tag="turns_a")
+        product(h0_rounded, 0, 0)
+        for i in range(PACK - 1):
+            product(h0_rounded, 0, i + 1)
+            if i == PACK - 2:
+                quantize(x_mx[1], x1_rounded, E4M3)
+            quantize_tokens(h_mx[0], h0_rounded, i)
+            y_matmul(0, i)
+        quantize_tokens(h_mx[0], h0_rounded, PACK - 1)
+        y_matmul(0, PACK - 1)
 
-        def store_codes(k):
-            n, off, w = pieces[k]
-            a, n0 = n // 3, BANK * (n % 3) + off
-            nc.sync.dma_start(out=out_1[a, :, n0:n0 + w, :].rearrange("p n i -> p (n i)").bitcast(I32), in_=out_codes[k][:].bitcast(I32))
+        c1_rounded = new_rounded("c1", tag="turns_a")
+        interleave_on_gpsimd(c1_rounded, c1_raw, 0, HALF)
+        beside_c1 = 6
+        for step in range(beside_c1):
+            add_bias(0, step)
+            silu(0, step)
+        quantize(c_mx[1], c1_rounded, E5M2)
+        for j in range(PACK):
+            pc_matmul(1, j)
+        out_00 = new_rounded("out_00", tag="turns_a")
+        interleave_on_gpsimd(out_00, result_cols(0, 0), 0, COLS)
+        for step in range(beside_c1, len(TILE_ORDER)):
+            add_bias(0, step)
+        for j in range(PACK):
+            pc_copy(1, j)
+        for i in range(PACK):
+            px_matmul(1, i)
+        for step in range(beside_c1, len(TILE_ORDER)):
+            silu(0, step)
+        out_02 = new_rounded("out_02")
+        interleave(on_scalar, out_02, result_cols(0, 2 * COLS), 0, OUT_02_SPLIT)
 
-        def store_scales(queues):
-            for q in range(4):
-                queues[q].dma_start(out=out_2[:, 4 * q:4 * q + 4, :].rearrange("a r n -> r a n").bitcast(I32),
-                                    in_=out_scales[32 * q:32 * q + 4].bitcast(I32))
+        h1_rounded = new_rounded("h1", tag="turns_b")
+        for i in range(PACK - 1):
+            product(h1_rounded, 1, i)
+        for i in range(2):
+            quantize_tokens(h_mx[1], h1_rounded, i)
+            y_matmul(1, i)
+        product(h1_rounded, 1, PACK - 1)
+        hand_on(out_00, 0, 0)
+        for i in range(2, PACK):
+            quantize_tokens(h_mx[1], h1_rounded, i)
+            y_matmul(1, i)
 
-        cast_dealt("V", "wc", wc_raw, 0, 336)
-        cast_dealt("S", "wc", wc_raw, 336, 512)
-        quantize_cols("wc", (wc_q, wc_s), E4M3, 0, 512)
-        cast_rows("V", "c0", c_raw[0], 0, 336)
-        cast_rows("S", "c0", c_raw[0], 336, 512)
-        quantize_cols("c0", c_mx[0], E5M2, 0, 512)
-        pc_matmul(0, 0)
-        cast_dealt("V", "wx", wx_raw, 0, 336)
-        cast_dealt("S", "wx", wx_raw, 336, 512)
-        pc_matmul(0, 1)
-        pc_matmul(0, 2)
-        pc_copy(0, 0)
-        quantize_cols("wx", (wx_q, wx_s), E4M3, 0, 512)
-        pc_matmul(0, 3)
-        pc_copy(0, 1)
-        pc_copy(0, 2)
-        cast_dealt("V", "x0", x_raw[0], 0, 352)
-        cast_dealt("S", "x0", x_raw[0], 352, 512)
-        pc_copy(0, 3)
-        quantize_cols("x0", x_mx[0], E4M3, 0, 128)
-        quantize_cols("x0", x_mx[0], E4M3, 128, 256)
-        quantize_cols("x0", x_mx[0], E4M3, 256, 384)
-        px_matmul(0, 0)
-        quantize_cols("x0", x_mx[0], E4M3, 384, 512)
-        px_matmul(0, 1)
-        product(0, 0)
-        cast_dealt("S", "x1", x_raw[1], 0, 512)
-        px_matmul(0, 2)
-        product(0, 1)
-        px_matmul(0, 3)
-        quantize_cols("h0", h_mx[0], E4M3, 0, 128)
-        product(0, 2)
-        y_matmul(0, 0)
-        quantize_cols("h0", h_mx[0], E4M3, 128, 256)
-        product(0, 3)
-        y_matmul(0, 1)
-        add_bias(0, 0)
-        quantize_cols("h0", h_mx[0], E4M3, 256, 384)
-        quantize_cols("h0", h_mx[0], E4M3, 384, 512)
-        silu(0, 0)
-        quantize_cols("x1", x_mx[1], E4M3, 0, 512)
-        y_matmul(0, 2)
-        cast_rows("S", "c1", c_raw[1], 0, 272)
-        add_bias(0, 1)
-        cast_rows("G", "c1", c_raw[1], 272, 512)
-        y_matmul(0, 3)
-        store(0, 0, 1)
-        y_matmul(1, 0)
-        add_bias(0, 2)
-        y_matmul(1, 1)
-        add_bias(0, 3)
-        silu(0, 1)
-        y_matmul(1, 2)
-        quantize_cols("c1", c_mx[1], E5M2, 0, 512)
-        silu(0, 2)
-        y_matmul(1, 3)
-        store(0, 1, 2)
-        add_bias(1, 0)
-        silu(0, 3)
-        pc_matmul(1, 0)
-        store(0, 2, 3)
-        pc_matmul(1, 1)
-        add_bias(1, 1)
-        pc_matmul(1, 2)
-        silu(1, 0)
-        store(0, 3, 4)
-        cast_out("G", 0, 0, 512)
-        pc_matmul(1, 3)
-        add_bias(1, 2)
-        y_matmul(2, 0)
-        pc_copy(1, 0)
-        y_matmul(2, 1)
-        add_bias(1, 3)
-        pc_copy(1, 1)
-        y_matmul(2, 2)
-        px_matmul(1, 0)
-        add_bias(2, 0)
-        pc_copy(1, 2)
-        y_matmul(2, 3)
-        px_matmul(1, 1)
-        add_bias(2, 1)
-        pc_copy(1, 3)
-        px_matmul(1, 2)
-        add_bias(2, 2)
-        silu(1, 1)
-        px_matmul(1, 3)
-        product(1, 0)
-        silu(1, 2)
-        store(1, 0, 2)
-        product(1, 1)
-        silu(1, 3)
-        quantize_cols("h1", h_mx[1], E4M3, 0, 128)
-        silu(2, 0)
-        product(1, 2)
-        store(1, 2, 4)
-        y_matmul(3, 0)
-        silu(2, 1)
-        quantize_cols("h1", h_mx[1], E4M3, 128, 256)
-        product(1, 3)
-        y_matmul(3, 1)
-        silu(2, 2)
-        store(2, 0, 2)
-        add_bias(2, 3)
-        planes(0)
-        silu(2, 3)
-        quantize_cols("h1", h_mx[1], E4M3, 256, 384)
-        quantize_cols("h1", h_mx[1], E4M3, 384, 512)
-        store_codes(0)
-        add_bias(3, 0)
-        y_matmul(3, 2)
-        store(2, 2, 4)
-        cast_out("G", 1, 0, 512)
-        add_bias(3, 1)
-        y_matmul(3, 3)
-        silu(3, 0)
-        add_bias(3, 2)
-        y_matmul(4, 0)
-        silu(3, 1)
-        store(3, 0, 1)
-        add_bias(3, 3)
-        y_matmul(4, 1)
-        silu(3, 2)
-        y_matmul(4, 2)
-        store(3, 1, 2)
-        add_bias(4, 0)
-        silu(3, 3)
-        y_matmul(4, 3)
-        store(3, 2, 3)
-        add_bias(4, 1)
-        silu(4, 0)
-        y_matmul(5, 0)
-        cast_out("G", 2, 0, 512)
-        store(3, 3, 4)
-        add_bias(4, 2)
-        silu(4, 1)
-        y_matmul(5, 1)
-        add_bias(4, 3)
-        silu(4, 2)
-        y_matmul(5, 2)
-        store(4, 0, 2)
-        add_bias(5, 0)
-        silu(4, 3)
-        y_matmul(5, 3)
-        add_bias(5, 1)
-        silu(5, 0)
-        store(4, 2, 4)
-        add_bias(5, 2)
-        silu(5, 1)
-        add_bias(5, 3)
-        silu(5, 2)
-        store(5, 0, 2)
-        planes(1)
-        silu(5, 3)
-        planes(2)
-        cast_out("S", 4, 48, 512)
-        store(5, 2, 4)
-        store_codes(1)
-        cast_out("V", 3, 0, 512)
-        store_codes(2)
-        cast_out("V", 4, 0, 48)
-        planes(3)
-        cast_out("S", 5, 96, 256)
-        cast_out("V", 5, 0, 96)
-        store_codes(3)
-        planes(4)
-        cast_out("S", 6, 128, 256)
-        cast_out("V", 6, 0, 128)
-        store_codes(4)
-        planes(5)
-        planes(6)
-        store_codes(5)
-        store_codes(6)
-        store_scales([nc.sync, nc.sync, nc.scalar, nc.scalar])
+        out_01 = new_rounded("out_01", tag="turns_b")
+        interleave_on_gpsimd(out_01, result_cols(0, COLS), 0, COLS)
+        interleave_on_gpsimd(out_02, result_cols(0, 2 * COLS), OUT_02_SPLIT, COLS)
+        for step in range(len(TILE_ORDER)):
+            add_bias(1, step)
+            silu(1, step)
+        out_10 = new_rounded("out_10")
+        interleave_on_gpsimd(out_10, result_cols(1, 0), OUT_10_SPLIT, COLS)
+
+        hand_on(out_01, 0, COLS)
+        hand_on(out_02, 0, 2 * COLS)
+        interleave(on_vector, out_10, result_cols(1, 0), 0, OUT_10_SPLIT)
+        pieces = [(COLS, COLS, OUT_11_SPLIT), (2 * COLS, COLS // 2, OUT_12_SPLITS[0]), (2 * COLS + COLS // 2, COLS // 2, OUT_12_SPLITS[1])]
+        waiting = (out_10, 1, 0, COLS)
+        for n0, width, split in pieces:
+            rounded = new_rounded("out_1_%d" % n0, width)
+            interleave(on_vector, rounded, result_cols(1, n0, width), 0, split)
+            interleave(on_scalar, rounded, result_cols(1, n0, width), split, width)
+            hand_on(*waiting)
+            waiting = (rounded, 1, n0, width)
+        hand_on(*waiting)
+
+        for quad, queue in enumerate([nc.sync, nc.sync, nc.scalar, nc.scalar]):
+            queue.dma_start(out=out_2[:, 4 * quad:4 * quad + 4, :].rearrange("a r n -> r a n").bitcast(I32),
+                            in_=out_scales[32 * quad:32 * quad + 4].bitcast(I32))

@@ -30,9 +30,10 @@ Z_BUFS = 8
 C0_SPLIT = 336
 WX_SPLIT = 336
 X0_SPLIT = 352
+C1_SPLIT = 448
 OUT_02_SPLIT = 224
-OUT_10_SPLIT = 272
-OUT_11_SPLIT = 192
+OUT_10_SPLIT = 336
+OUT_11_SPLIT = 176
 OUT_12_SPLITS = (96, 96)
 
 
@@ -92,15 +93,15 @@ def tile_mix_bilin_tm_pl_silu_kernel(tc, x, wx, c, wc, w_words, w_scales, b, out
         x1_raw = load_rows("x1_raw", x[:, HALF:])
         w_codes = new_tile("w_codes", [P, 2 * M], U8)
         nc.sync.dma_start(out=w_codes[:].bitcast(I32), in_=w_words[0].bitcast(I32))
-        w_plane = new_tile("w_plane", [P, M], U8)
-        nc.vector.memset(w_plane[:].bitcast(I32), 0)
-        for quad in range(4):
-            nc.sync.dma_start(out=w_plane[32 * quad:32 * quad + 4, :].bitcast(I32),
-                              in_=w_scales[0, 4 * quad:4 * quad + 4, :].bitcast(I32))
         c1_raw = load_rows("c1_raw", c[:, HALF:])
-
         ident = new_tile("ident", [P, P], F32)
         make_identity(nc, ident[:])
+        w_scale_tile = new_tile("w_scale_tile", [P, M], U8)
+        nc.gpsimd.memset(w_scale_tile[:].bitcast(I32), 0)
+        for quad in range(4):
+            nc.gpsimd.dma_start(out=w_scale_tile[32 * quad:32 * quad + 4, :].bitcast(I32),
+                                in_=w_scales[0, 4 * quad:4 * quad + 4, :].bitcast(I32))
+
         bias = new_tile("bias", [P, M], F32)
         bias_ns = bias[:].rearrange("p (n s) -> p n s", s=b_per_row)
         for group in range(b_per_row // 4):
@@ -150,7 +151,7 @@ def tile_mix_bilin_tm_pl_silu_kernel(tc, x, wx, c, wc, w_words, w_scales, b, out
             y_banks[a, step] = new_bank("y%d_%d" % (a, step), step % Y_BANKS)
             tokens, n0 = dealt_cols(i), COLS * chunk
             nc.tensor.matmul_mx(out=y_banks[a, step][:], lhsT=h_mx[a][0][:, tokens].bitcast(E4M3), lhsT_scale=h_mx[a][1][:, tokens],
-                                rhs=w_codes[:, 2 * n0:2 * (n0 + COLS)].bitcast(E2M1), rhs_scale=w_plane[:, n0:n0 + COLS],
+                                rhs=w_codes[:, 2 * n0:2 * (n0 + COLS)].bitcast(E2M1), rhs_scale=w_scale_tile[:, n0:n0 + COLS],
                                 start=True, stop=True)
 
         def add_bias(a, step):
@@ -213,11 +214,13 @@ def tile_mix_bilin_tm_pl_silu_kernel(tc, x, wx, c, wc, w_words, w_scales, b, out
         y_matmul(0, PACK - 1)
 
         c1_rounded = new_rounded("c1", tag="turns_a")
-        interleave_on_gpsimd(c1_rounded, c1_raw, 0, HALF)
+        interleave_on_gpsimd(c1_rounded, c1_raw, 0, C1_SPLIT)
         beside_c1 = 6
         for step in range(beside_c1):
             add_bias(0, step)
             silu(0, step)
+            if step == 0:
+                interleave(on_scalar, c1_rounded, c1_raw, C1_SPLIT, HALF)
         quantize(c_mx[1], c1_rounded, E5M2)
         for j in range(PACK):
             pc_matmul(1, j)
@@ -268,6 +271,6 @@ def tile_mix_bilin_tm_pl_silu_kernel(tc, x, wx, c, wc, w_words, w_scales, b, out
             waiting = (rounded, 1, n0, width)
         hand_on(*waiting)
 
-        for quad, queue in enumerate([nc.sync, nc.sync, nc.scalar, nc.scalar]):
-            queue.dma_start(out=out_2[:, 4 * quad:4 * quad + 4, :].rearrange("a r n -> r a n").bitcast(I32),
-                            in_=out_scales[32 * quad:32 * quad + 4].bitcast(I32))
+        for quad in range(4):
+            nc.scalar.dma_start(out=out_2[:, 4 * quad:4 * quad + 4, :].rearrange("a r n -> r a n").bitcast(I32),
+                                in_=out_scales[32 * quad:32 * quad + 4].bitcast(I32))

@@ -23,18 +23,20 @@ HALF = P * PACK
 COLS = 512
 CHUNKS = M // COLS
 
-TILE_ORDER = [(0, i) for i in range(PACK)] + [(chunk, i) for i in range(PACK) for chunk in (1, 2)]
+UNITS = M // P
 Y_BANKS = 4
 Z_BUFS = 8
-
-C0_SPLIT = 336
-WX_SPLIT = 336
-X0_SPLIT = 352
-C1_SPLIT = 448
-OUT_02_SPLIT = 224
-OUT_10_SPLIT = 336
-OUT_11_SPLIT = 176
-OUT_12_SPLITS = (96, 96)
+PIECE = 256
+WC_SPLIT = 352
+C0_SPLIT = 160
+WXA_SPLIT = 96
+X0A_SPLIT = 160
+X0B_SPLIT = 160
+ROW_GROUPS = 4
+S1, S2, S3 = 4, 10, 19
+PC_AFTER = {0: (0, 1), 1: (2,), 2: (3,)}
+G1, G3, S4, V5 = 128, 448, 256, 128
+SINGLE = (0, 1, 2, 3)
 
 
 def tile_mix_bilin_tm_pl_silu_kernel(tc, x, wx, c, wc, w_words, w_scales, b, out_0, out_1, out_2):
@@ -83,24 +85,29 @@ def tile_mix_bilin_tm_pl_silu_kernel(tc, x, wx, c, wc, w_words, w_scales, b, out
 
         on_vector, on_scalar = nc.vector.tensor_copy, nc.scalar.copy
 
+        on_gpsimd = None
+        def load_halves(name, rows):
+            return [load_rows("%s%d" % (name, q), rows[:, PIECE * q:PIECE * (q + 1)]) for q in range(2)]
+
         b_per_row = M // P
         b_rows = new_tile("b_rows", [P, b_per_row], F32)
         nc.sync.dma_start(out=b_rows[:], in_=b.rearrange("(p s) -> p s", p=P))
         wc_raw = load_rows("wc_raw", wc)
-        c0_raw = load_rows("c0_raw", c[:, :HALF])
-        wx_raw = load_rows("wx_raw", wx)
-        x0_raw = load_rows("x0_raw", x[:, :HALF])
-        x1_raw = load_rows("x1_raw", x[:, HALF:])
-        w_codes = new_tile("w_codes", [P, 2 * M], U8)
-        nc.sync.dma_start(out=w_codes[:].bitcast(I32), in_=w_words[0].bitcast(I32))
-        c1_raw = load_rows("c1_raw", c[:, HALF:])
-        ident = new_tile("ident", [P, P], F32)
-        make_identity(nc, ident[:])
+        c0_raw = load_halves("c0_raw", c[:, :HALF])
+        wx_raw = load_halves("wx_raw", wx)
+        x0_raw = load_halves("x0_raw", x[:, :HALF])
+        c1_raw = [load_rows("c1_raw0", c[:, HALF:HALF + PIECE])]
         w_scale_tile = new_tile("w_scale_tile", [P, M], U8)
         nc.gpsimd.memset(w_scale_tile[:].bitcast(I32), 0)
-        for quad in range(4):
-            nc.gpsimd.dma_start(out=w_scale_tile[32 * quad:32 * quad + 4, :].bitcast(I32),
-                                in_=w_scales[0, 4 * quad:4 * quad + 4, :].bitcast(I32))
+        w_scale_rows = w_scales[0].rearrange("(q r) n -> r q n", r=4)
+        for r in range(4):
+            nc.sync.dma_start(out=w_scale_tile[r:P:32, :].bitcast(I32), in_=w_scale_rows[r].bitcast(I32))
+        w_codes = new_tile("w_codes", [P, 2 * M], U8)
+        nc.sync.dma_start(out=w_codes[:].bitcast(I32), in_=w_words[0].bitcast(I32))
+        c1_raw.append(load_rows("c1_raw1", c[:, HALF + PIECE:]))
+        x1_raw = load_rows("x1_raw", x[:, HALF:])
+        ident = new_tile("ident", [P, P], F32)
+        make_identity(nc, ident[:])
 
         bias = new_tile("bias", [P, M], F32)
         bias_ns = bias[:].rearrange("p (n s) -> p n s", s=b_per_row)
@@ -111,15 +118,28 @@ def tile_mix_bilin_tm_pl_silu_kernel(tc, x, wx, c, wc, w_words, w_scales, b, out
                 nc.tensor.transpose(bank[:, P * u:P * (u + 1)], b_rows[:, s:s + 1].to_broadcast([P, P]), ident[:])
             nc.scalar.copy(out=bias_ns[:, :, 4 * group:4 * group + 4], in_=bank[:].rearrange("p (u n) -> p n u", u=4))
 
+        pieces = (2, 1)
         wc_mx, wx_mx = new_mx("wc", R), new_mx("wx", R)
         c_mx = [new_mx("c%d" % a, HALF) for a in range(2)]
         x_mx = [new_mx("x%d" % a, HALF) for a in range(2)]
         h_mx = [new_mx("h%d" % a, HALF) for a in range(2)]
-        pc_dealt = [new_tile("pc%d" % a, [P, PACK, PACK, P], F32) for a in range(2)]
-        result = [new_tile("result%d" % a, [P, PACK, M], F32) for a in range(2)]
+        pc_dealt = [new_tile("pc%d" % a, [P, PACK, HALF], F32, "pc") for a in range(1)]
+        result = {}
         out_scales = new_tile("out_scales", [P, 2, M], U8)
         out_rows = out_0.rearrange("(a p i) n -> a p i n", a=2, i=PACK)
         pc_banks, px_banks, y_banks, biased = {}, {}, {}, {}
+
+        def deal_part(copy, dealt, raw, m0, lo, hi):
+            out = dealt[:, :, m0 + lo // PACK:m0 + hi // PACK, :].rearrange("p j m e -> p m e j")
+            copy(out=out, in_=raw[:, :, lo:hi].rearrange("p e (m j) -> p m e j", j=PACK))
+
+        def deal_on_gpsimd(rounded, raw, lo, hi):
+            out = rounded[:].rearrange("p (j m e) -> p m j e", j=PACK, e=PACK)[:, lo // PACK:hi // PACK]
+            nc.gpsimd.tensor_scalar(out=out, in0=raw[:, :, lo:hi].rearrange("p e (m j) -> p m j e", j=PACK),
+                                    scalar1=1.0, scalar2=-0.0, op0=ALU.mult, op1=ALU.add)
+
+        def dealt_view(rounded):
+            return rounded.rearrange("p (j m e) -> p j m e", j=PACK, e=PACK)
 
         def pc_matmul(a, j):
             pc_banks[a, j] = new_bank("pc%d_%d" % (a, j), 4 + j)
@@ -128,149 +148,200 @@ def tile_mix_bilin_tm_pl_silu_kernel(tc, x, wx, c, wc, w_words, w_scales, b, out
                                 rhs=c_mx[a][0][:].bitcast(E5M2), rhs_scale=c_mx[a][1][:], start=True, stop=True)
 
         def pc_copy(a, j):
-            nc.scalar.copy(out=pc_dealt[a][:, j], in_=pc_banks[a, j][:].rearrange("p (m i) -> p i m", i=PACK))
+            nc.scalar.copy(out=pc_dealt[a][:, j].rearrange("p (q i m) -> p q i m", q=pieces[a], i=PACK),
+                           in_=pc_banks[a, j][:].rearrange("p (q m i) -> p q i m", q=pieces[a], i=PACK))
 
-        def px_matmul(a, i):
-            px_banks[a, i] = new_bank("px%d_%d" % (a, i), 4 * a + i)
-            tokens = dealt_cols(i)
+        def px_matmul(a, part):
+            px_banks[a, part] = new_bank("px%d_%d" % (a, part), 4 * a + part)
+            tokens = dealt_cols(part)
             for j in range(PACK):
                 cols = dealt_cols(j)
-                nc.tensor.matmul_mx(out=px_banks[a, i][:, cols], lhsT=wx_mx[0][:, cols].bitcast(E4M3), lhsT_scale=wx_mx[1][:, cols],
+                nc.tensor.matmul_mx(out=px_banks[a, part][:, cols], lhsT=wx_mx[0][:, cols].bitcast(E4M3), lhsT_scale=wx_mx[1][:, cols],
                                     rhs=x_mx[a][0][:, tokens].bitcast(E4M3), rhs_scale=x_mx[a][1][:, tokens], start=True, stop=True)
 
-        def product(h_rounded, a, i):
-            out = h_rounded[:, HALF * i:HALF * (i + 1)].rearrange("p (g u j) -> p g j u", u=2, j=PACK)
-            nc.vector.tensor_tensor(out=out, in0=px_banks[a, i][:].rearrange("p (j g u) -> p g j u", j=PACK, u=2),
-                                    in1=pc_dealt[a][:, :, i, :].rearrange("p j (g u) -> p g j u", u=2), op=ALU.mult)
+        def product(h_rounded, a, part):
+            out = h_rounded[:, HALF * part:HALF * (part + 1)].rearrange("p (g u j) -> p g j u", u=2, j=PACK)
+            nc.vector.tensor_tensor(out=out, in0=px_banks[a, part][:].rearrange("p (j g u) -> p g j u", j=PACK, u=2),
+                                    in1=pc_dealt[a][:, :, dealt_cols(part)].rearrange("p j (g u) -> p g j u", u=2), op=ALU.mult)
 
-        def quantize_tokens(mx, rounded, i):
-            quantize(mx, rounded, E4M3, P * i, P * (i + 1))
+        def quantize_piece(mx, rounded, q, j):
+            src, dst = PIECE * q + 64 * j, P * j + 64 * q
+            codes, scales = mx
+            nc.vector.quantize_mx(out=codes[:, dst:dst + 64].bitcast(E4M3), scales=scales[:, dst:dst + 64],
+                                  in_=rounded[:, PACK * src:PACK * (src + 64)])
 
-        def y_matmul(a, step):
-            chunk, i = TILE_ORDER[step]
-            y_banks[a, step] = new_bank("y%d_%d" % (a, step), step % Y_BANKS)
-            tokens, n0 = dealt_cols(i), COLS * chunk
-            nc.tensor.matmul_mx(out=y_banks[a, step][:], lhsT=h_mx[a][0][:, tokens].bitcast(E4M3), lhsT_scale=h_mx[a][1][:, tokens],
-                                rhs=w_codes[:, 2 * n0:2 * (n0 + COLS)].bitcast(E2M1), rhs_scale=w_scale_tile[:, n0:n0 + COLS],
+        def y_pass(out, a, i, n0, width):
+            tokens = dealt_cols(i)
+            nc.tensor.matmul_mx(out=out, lhsT=h_mx[a][0][:, tokens].bitcast(E4M3), lhsT_scale=h_mx[a][1][:, tokens],
+                                rhs=w_codes[:, 2 * n0:2 * (n0 + width)].bitcast(E2M1), rhs_scale=w_scale_tile[:, n0:n0 + width],
                                 start=True, stop=True)
 
-        def add_bias(a, step):
-            n0 = COLS * TILE_ORDER[step][0]
-            slot = (len(TILE_ORDER) * a + step) % Z_BUFS
-            biased[a, step] = new_tile("biased%d_%d" % (a, step), [P, COLS], F32, "biased%d" % slot)
-            nc.vector.tensor_tensor(out=biased[a, step][:], in0=y_banks[a, step][:], in1=bias[:, n0:n0 + COLS], op=ALU.add)
-            if step + Y_BANKS < len(TILE_ORDER):
-                y_matmul(a, step + Y_BANKS)
+        def y_matmul(step):
+            group, k = divmod(step, PACK)
+            a, n0 = group // CHUNKS, COLS * (group % CHUNKS)
+            y_banks[step] = new_bank("y%d" % step, step % Y_BANKS)
+            if group < ROW_GROUPS:
+                y_pass(y_banks[step][:], a, k, n0, COLS)
+            else:
+                for i in range(PACK):
+                    y_pass(y_banks[step][:, dealt_cols(i)], a, i, n0 + P * k, P)
 
-        def silu(a, step):
-            chunk, i = TILE_ORDER[step]
-            nc.scalar.activation(out=result[a][:, i, COLS * chunk:COLS * (chunk + 1)], in_=biased[a, step][:], func=ACT.Silu)
-            if chunk != 1:
-                cols = slice(0, COLS) if chunk == 0 else slice(COLS, M)
-                nc.sync.dma_start(out=out_rows[a, :, i, cols], in_=result[a][:, i, cols])
+        def add_bias(step):
+            group, k = divmod(step, PACK)
+            n0 = COLS * (group % CHUNKS)
+            biased[step] = new_tile("biased%d" % step, [P, COLS], F32, "biased%d" % (step % Z_BUFS))
+            if group < ROW_GROUPS:
+                nc.vector.tensor_tensor(out=biased[step][:], in0=y_banks[step][:], in1=bias[:, n0:n0 + COLS], op=ALU.add)
+            else:
+                nc.vector.tensor_tensor(out=biased[step][:].rearrange("p (i n) -> p i n", i=PACK), in0=y_banks[step][:].rearrange("p (i n) -> p i n", i=PACK),
+                                        in1=bias[:, n0 + P * k:n0 + P * (k + 1)].unsqueeze(1).to_broadcast([P, PACK, P]), op=ALU.add)
+            if step % UNITS + Y_BANKS < UNITS:
+                y_matmul(step + Y_BANKS)
 
-        def result_cols(a, n0, width=COLS):
-            return result[a][:, :, n0:n0 + width]
+        def silu(step):
+            group, k = divmod(step, PACK)
+            a, n0 = group // CHUNKS, COLS * (group % CHUNKS)
+            if k == 0:
+                result[group] = new_tile("result%d" % group, [P, PACK, COLS], F32)
+            first = k if step in SINGLE else k - 1
+            if group < ROW_GROUPS:
+                nc.scalar.activation(out=result[group][:, k, :], in_=biased[step][:], func=ACT.Silu)
+                if step in SINGLE or k % 2:
+                    nc.sync.dma_start(out=out_rows[a, :, first:k + 1, n0:n0 + COLS], in_=result[group][:, first:k + 1, :])
+            else:
+                nc.scalar.activation(out=result[group][:, :, P * k:P * (k + 1)], in_=biased[step][:].rearrange("p (i n) -> p i n", i=PACK), func=ACT.Silu)
+                if step in SINGLE or k % 2:
+                    nc.sync.dma_start(out=out_rows[a, :, :, n0 + P * first:n0 + P * (k + 1)], in_=result[group][:, :, P * first:P * (k + 1)])
 
-        def hand_on(rounded, a, n0, width=COLS):
-            codes = new_tile("out_codes%d_%d" % (a, n0), [P, width], U32)
-            nc.vector.quantize_mx(out=codes[:].bitcast(E4M3), scales=out_scales[:, a, n0:n0 + width], in_=rounded[:])
-            nc.sync.dma_start(out=out_1[a, :, n0:n0 + width, :].rearrange("p n i -> p (n i)").bitcast(I32), in_=codes[:].bitcast(I32))
+        def steps(lo, hi):
+            for step in range(lo, hi):
+                add_bias(step)
+                silu(step)
+
+        def hand_on(group, lo, parts):
+            a, n0 = group // CHUNKS, COLS * (group % CHUNKS) + lo
+            total = sum(part.shape[1] for part in parts) // PACK
+            codes = new_tile("out_codes%d_%d" % (a, n0), [P, total], U32)
+            at = 0
+            for part in parts:
+                done, cols = 0, part.shape[1] // PACK
+                for width in (512, 256, 128, 64):
+                    if cols - done >= width:
+                        nc.vector.quantize_mx(out=codes[:, at:at + width].bitcast(E4M3), scales=out_scales[:, a, n0 + at:n0 + at + width],
+                                              in_=part[:, PACK * done:PACK * (done + width)])
+                        done, at = done + width, at + width
+            nc.sync.dma_start(out=out_1[a, :, n0:n0 + total, :].rearrange("p n i -> p (n i)").bitcast(I32), in_=codes[:].bitcast(I32))
+
+        def round_out(engine, group, lo, hi, tag=None):
+            rounded = new_rounded("out%d_%d" % (group, lo), hi - lo, tag)
+            if engine is on_gpsimd:
+                interleave_on_gpsimd(rounded, result[group][:, :, lo:hi], 0, hi - lo)
+            else:
+                interleave(engine, rounded, result[group][:, :, lo:hi], 0, hi - lo)
+            return rounded[:]
+
+        def store_scales(queue):
+            rows = out_2.rearrange("a (q r) n -> r q a n", r=4)
+            for r in range(4):
+                queue.dma_start(out=rows[r].bitcast(I32), in_=out_scales[r:P:32].bitcast(I32))
 
         wc_rounded = new_rounded("wc")
-        deal(on_vector, wc_rounded, wc_raw, 0, R)
+        deal(on_vector, wc_rounded, wc_raw, 0, WC_SPLIT)
+        deal(on_scalar, wc_rounded, wc_raw, WC_SPLIT, R)
         quantize(wc_mx, wc_rounded, E4M3)
-        c0_rounded = new_rounded("c0")
-        interleave(on_vector, c0_rounded, c0_raw, 0, C0_SPLIT)
-        interleave(on_scalar, c0_rounded, c0_raw, C0_SPLIT, HALF)
-        quantize(c_mx[0], c0_rounded, E5M2)
+        c0_rounded = [new_rounded("c0_%d" % q, PIECE) for q in range(2)]
+        interleave(on_scalar, c0_rounded[0], c0_raw[0], 0, PIECE)
+        interleave(on_vector, c0_rounded[1], c0_raw[1], 0, C0_SPLIT)
+        interleave(on_scalar, c0_rounded[1], c0_raw[1], C0_SPLIT, PIECE)
+        for q in range(2):
+            cols = slice(PIECE * q, PIECE * (q + 1))
+            nc.vector.quantize_mx(out=c_mx[0][0][:, cols].bitcast(E5M2), scales=c_mx[0][1][:, cols], in_=c0_rounded[q][:])
+        wx_rounded = new_rounded("wx")
+        x0_rounded = new_rounded("x0")
+        h0_rounded = new_rounded("h0")
+        width = PACK * PIECE
+        deal_part(on_scalar, dealt_view(wx_rounded[:, :width]), wx_raw[0], 0, WXA_SPLIT, PIECE)
         for j in range(PACK):
             pc_matmul(0, j)
-        wx_rounded = new_rounded("wx")
-        deal(on_vector, wx_rounded, wx_raw, 0, WX_SPLIT)
-        deal(on_scalar, wx_rounded, wx_raw, WX_SPLIT, R)
-        quantize(wx_mx, wx_rounded, E4M3)
         for j in range(PACK - 1):
             pc_copy(0, j)
-        x0_rounded = new_rounded("x0")
-        deal(on_vector, x0_rounded, x0_raw, 0, X0_SPLIT)
-        deal(on_scalar, x0_rounded, x0_raw, X0_SPLIT, HALF)
+        deal_part(on_scalar, dealt_view(x0_rounded[:, :width]), x0_raw[0], 0, X0A_SPLIT, PIECE)
         pc_copy(0, PACK - 1)
+        deal_part(on_vector, dealt_view(wx_rounded[:, :width]), wx_raw[0], 0, 0, WXA_SPLIT)
+        for j in range(PACK):
+            quantize_piece(wx_mx, wx_rounded, 0, j)
+        deal_part(on_vector, dealt_view(wx_rounded[:, width:]), wx_raw[1], 0, 0, PIECE)
+        deal_part(on_vector, dealt_view(x0_rounded[:, :width]), x0_raw[0], 0, 0, X0A_SPLIT)
+        for j in range(PACK):
+            quantize_piece(wx_mx, wx_rounded, 1, j)
+        quantize(x_mx[0], x0_rounded, E4M3, 0, PIECE)
+        px_matmul(0, 0)
+        px_matmul(0, 1)
+        deal_part(on_vector, dealt_view(x0_rounded[:, width:]), x0_raw[1], 0, 0, X0B_SPLIT)
+        deal_part(on_scalar, dealt_view(x0_rounded[:, width:]), x0_raw[1], 0, X0B_SPLIT, PIECE)
+        c1_rounded = [new_rounded("c1_0", PIECE)]
+        interleave(on_scalar, c1_rounded[0], c1_raw[0], 0, PIECE)
+        quantize(x_mx[0], x0_rounded, E4M3, PIECE, HALF)
+        px_matmul(0, 2)
+        px_matmul(0, 3)
+        for part in range(3):
+            product(h0_rounded, 0, part)
         for i in range(PACK):
-            quantize_tokens(x_mx[0], x0_rounded, i)
-            px_matmul(0, i)
-        x1_rounded = new_rounded("x1")
-        deal(on_scalar, x1_rounded, x1_raw, 0, HALF)
+            quantize_piece(h_mx[0], h0_rounded, 0, i)
+        for i in range(2):
+            quantize_piece(h_mx[0], h0_rounded, 1, i)
+        product(h0_rounded, 0, 3)
+        for i in range(2):
+            y_matmul(i)
+        add_bias(0)
+        for i in range(2, PACK):
+            quantize_piece(h_mx[0], h0_rounded, 1, i)
+            y_matmul(i)
+        silu(0)
 
-        h0_rounded = new_rounded("h0", tag="turns_a")
-        product(h0_rounded, 0, 0)
-        for i in range(PACK - 1):
-            product(h0_rounded, 0, i + 1)
-            if i == PACK - 2:
-                quantize(x_mx[1], x1_rounded, E4M3)
-            quantize_tokens(h_mx[0], h0_rounded, i)
-            y_matmul(0, i)
-        quantize_tokens(h_mx[0], h0_rounded, PACK - 1)
-        y_matmul(0, PACK - 1)
-
-        c1_rounded = new_rounded("c1", tag="turns_a")
-        interleave_on_gpsimd(c1_rounded, c1_raw, 0, C1_SPLIT)
-        beside_c1 = 6
-        for step in range(beside_c1):
-            add_bias(0, step)
-            silu(0, step)
-            if step == 0:
-                interleave(on_scalar, c1_rounded, c1_raw, C1_SPLIT, HALF)
-        quantize(c_mx[1], c1_rounded, E5M2)
+        c1_rounded.append(new_rounded("c1_1", PIECE, tag="h0_bf16"))
+        interleave_on_gpsimd(c1_rounded[1], c1_raw[1], 0, PIECE)
+        steps(1, S1)
+        for q in range(2):
+            cols = slice(PIECE * q, PIECE * (q + 1))
+            nc.vector.quantize_mx(out=c_mx[1][0][:, cols].bitcast(E5M2), scales=c_mx[1][1][:, cols], in_=c1_rounded[q][:])
+        x1_rounded = new_rounded("x1", tag="h0_bf16")
+        deal_on_gpsimd(x1_rounded, x1_raw, 0, HALF)
+        pc_dealt.append(new_tile("pc1", [P, PACK, HALF], F32, "pc"))
         for j in range(PACK):
             pc_matmul(1, j)
-        out_00 = new_rounded("out_00", tag="turns_a")
-        interleave_on_gpsimd(out_00, result_cols(0, 0), 0, COLS)
-        for step in range(beside_c1, len(TILE_ORDER)):
-            add_bias(0, step)
-        for j in range(PACK):
-            pc_copy(1, j)
+        for step in range(S1, S2):
+            add_bias(step)
+            silu(step)
+            for j in PC_AFTER.get(step - S1, ()):
+                pc_copy(1, j)
+        quantize(x_mx[1], x1_rounded, E4M3)
         for i in range(PACK):
             px_matmul(1, i)
-        for step in range(beside_c1, len(TILE_ORDER)):
-            silu(0, step)
-        out_02 = new_rounded("out_02")
-        interleave(on_scalar, out_02, result_cols(0, 2 * COLS), 0, OUT_02_SPLIT)
-
-        h1_rounded = new_rounded("h1", tag="turns_b")
-        for i in range(PACK - 1):
+        out0 = round_out(on_gpsimd, 0, 0, COLS, "h0_bf16")
+        steps(S2, UNITS)
+        h1_rounded = new_rounded("h1")
+        for i in range(PACK):
             product(h1_rounded, 1, i)
-        for i in range(2):
-            quantize_tokens(h_mx[1], h1_rounded, i)
-            y_matmul(1, i)
-        product(h1_rounded, 1, PACK - 1)
-        hand_on(out_00, 0, 0)
-        for i in range(2, PACK):
-            quantize_tokens(h_mx[1], h1_rounded, i)
-            y_matmul(1, i)
+        for i in range(PACK):
+            quantize(h_mx[1], h1_rounded, E4M3, P * i, P * (i + 1))
+            y_matmul(UNITS + i)
+        hand_on(0, 0, [out0])
+        out1s = round_out(on_scalar, 1, G1, COLS)
 
-        out_01 = new_rounded("out_01", tag="turns_b")
-        interleave_on_gpsimd(out_01, result_cols(0, COLS), 0, COLS)
-        interleave_on_gpsimd(out_02, result_cols(0, 2 * COLS), OUT_02_SPLIT, COLS)
-        for step in range(len(TILE_ORDER)):
-            add_bias(1, step)
-            silu(1, step)
-        out_10 = new_rounded("out_10")
-        interleave_on_gpsimd(out_10, result_cols(1, 0), OUT_10_SPLIT, COLS)
-
-        hand_on(out_01, 0, COLS)
-        hand_on(out_02, 0, 2 * COLS)
-        interleave(on_vector, out_10, result_cols(1, 0), 0, OUT_10_SPLIT)
-        pieces = [(COLS, COLS, OUT_11_SPLIT), (2 * COLS, COLS // 2, OUT_12_SPLITS[0]), (2 * COLS + COLS // 2, COLS // 2, OUT_12_SPLITS[1])]
-        waiting = (out_10, 1, 0, COLS)
-        for n0, width, split in pieces:
-            rounded = new_rounded("out_1_%d" % n0, width)
-            interleave(on_vector, rounded, result_cols(1, n0, width), 0, split)
-            interleave(on_scalar, rounded, result_cols(1, n0, width), split, width)
-            hand_on(*waiting)
-            waiting = (rounded, 1, n0, width)
-        hand_on(*waiting)
-
-        for quad in range(4):
-            nc.scalar.dma_start(out=out_2[:, 4 * quad:4 * quad + 4, :].rearrange("a r n -> r a n").bitcast(I32),
-                                in_=out_scales[32 * quad:32 * quad + 4].bitcast(I32))
+        out2 = round_out(on_gpsimd, 2, 0, COLS, "h0_bf16")
+        out1g = round_out(on_gpsimd, 1, 0, G1)
+        steps(UNITS, S3)
+        out4s = round_out(on_scalar, 4, 0, S4)
+        hand_on(1, 0, [out1g, out1s, out2])
+        out3g = round_out(on_gpsimd, 3, 0, G3, "h0_bf16")
+        steps(S3, 2 * UNITS)
+        out3v = round_out(on_vector, 3, G3, COLS)
+        out4v = round_out(on_vector, 4, S4, COLS)
+        hand_on(3, 0, [out3g, out3v])
+        out5v = round_out(on_vector, 5, 0, V5)
+        out5s = round_out(on_scalar, 5, V5, 2 * P)
+        out5t = round_out(on_scalar, 5, 2 * P, COLS)
+        hand_on(4, 0, [out4s, out4v, out5v, out5s])
+        hand_on(5, 2 * P, [out5t])
+        store_scales(nc.scalar)

@@ -68,8 +68,8 @@ def tile_mix_bilin_tm_pl_silu_kernel(tc, x, wx, c, wc, w_words, w_scales, b, out
             copy(out=out, in_=raw[:, :, lo:hi].rearrange("p e (g u) -> p g e u", u=4))
 
         def interleave_on_gpsimd(rounded, raw, lo, hi):
-            out = rounded[:, PACK * lo:PACK * hi].rearrange("p (n e) -> p n e", e=PACK)
-            nc.gpsimd.tensor_scalar(out=out, in0=raw[:, :, lo:hi].rearrange("p e n -> p n e"),
+            out = rounded[:, PACK * lo:PACK * hi].rearrange("p (g u e) -> p g e u", u=4, e=PACK)
+            nc.gpsimd.tensor_scalar(out=out, in0=raw[:, :, lo:hi].rearrange("p e (g u) -> p g e u", u=4),
                                     scalar1=1.0, scalar2=-0.0, op0=ALU.mult, op1=ALU.add)
 
         def deal(copy, rounded, raw, lo, hi):
@@ -134,8 +134,8 @@ def tile_mix_bilin_tm_pl_silu_kernel(tc, x, wx, c, wc, w_words, w_scales, b, out
             copy(out=out, in_=raw[:, :, lo:hi].rearrange("p e (m j) -> p m e j", j=PACK))
 
         def deal_on_gpsimd(rounded, raw, lo, hi):
-            out = rounded[:].rearrange("p (j m e) -> p m j e", j=PACK, e=PACK)[:, lo // PACK:hi // PACK]
-            nc.gpsimd.tensor_scalar(out=out, in0=raw[:, :, lo:hi].rearrange("p e (m j) -> p m j e", j=PACK),
+            out = rounded[:].rearrange("p (j m e) -> p m e j", j=PACK, e=PACK)[:, lo // PACK:hi // PACK]
+            nc.gpsimd.tensor_scalar(out=out, in0=raw[:, :, lo:hi].rearrange("p e (m j) -> p m e j", j=PACK),
                                     scalar1=1.0, scalar2=-0.0, op0=ALU.mult, op1=ALU.add)
 
         def dealt_view(rounded):

@@ -32,10 +32,10 @@ C0_SPLIT = 160
 WXA_SPLIT = 96
 X0A_SPLIT = 160
 X0B_SPLIT = 160
-ROW_GROUPS = 4
-S1, S2, S3 = 4, 10, 19
+ROW_GROUPS = 5
+S1, S2, S3 = 2, 9, 20
 PC_AFTER = {0: (0, 1), 1: (2,), 2: (3,)}
-G1, G3, S4, V5 = 128, 448, 256, 128
+S3W, V5 = 256, 128
 SINGLE = (0, 1, 2, 3)
 
 
@@ -96,18 +96,21 @@ def tile_mix_bilin_tm_pl_silu_kernel(tc, x, wx, c, wc, w_words, w_scales, b, out
         c0_raw = load_halves("c0_raw", c[:, :HALF])
         wx_raw = load_halves("wx_raw", wx)
         x0_raw = load_halves("x0_raw", x[:, :HALF])
-        c1_raw = [load_rows("c1_raw0", c[:, HALF:HALF + PIECE])]
+        w_codes = new_tile("w_codes", [P, 2 * M], U8)
+        nc.sync.dma_start(out=w_codes[:].bitcast(I32), in_=w_words[0].bitcast(I32))
+        c1_raw = load_halves("c1_raw", c[:, HALF:])
+        x1_raw = load_rows("x1_raw", x[:, HALF:])
+        ident = new_tile("ident", [P, P], F32)
+        make_identity(nc, ident[:])
+
         w_scale_tile = new_tile("w_scale_tile", [P, M], U8)
         nc.gpsimd.memset(w_scale_tile[:].bitcast(I32), 0)
         w_scale_rows = w_scales[0].rearrange("(q r) n -> r q n", r=4)
         for r in range(4):
-            nc.sync.dma_start(out=w_scale_tile[r:P:32, :].bitcast(I32), in_=w_scale_rows[r].bitcast(I32))
-        w_codes = new_tile("w_codes", [P, 2 * M], U8)
-        nc.sync.dma_start(out=w_codes[:].bitcast(I32), in_=w_words[0].bitcast(I32))
-        c1_raw.append(load_rows("c1_raw1", c[:, HALF + PIECE:]))
-        x1_raw = load_rows("x1_raw", x[:, HALF:])
-        ident = new_tile("ident", [P, P], F32)
-        make_identity(nc, ident[:])
+            nc.gpsimd.dma_start(out=w_scale_tile[r:P:32, :].bitcast(I32), in_=w_scale_rows[r].bitcast(I32))
+
+        warm = new_tile("warm", [P, 1], F32)
+        nc.scalar.activation(out=warm[:], in_=ident[:, 0:1], func=ACT.Silu)
 
         bias = new_tile("bias", [P, M], F32)
         bias_ns = bias[:].rearrange("p (n s) -> p n s", s=b_per_row)
@@ -279,8 +282,9 @@ def tile_mix_bilin_tm_pl_silu_kernel(tc, x, wx, c, wc, w_words, w_scales, b, out
         px_matmul(0, 1)
         deal_part(on_vector, dealt_view(x0_rounded[:, width:]), x0_raw[1], 0, 0, X0B_SPLIT)
         deal_part(on_scalar, dealt_view(x0_rounded[:, width:]), x0_raw[1], 0, X0B_SPLIT, PIECE)
-        c1_rounded = [new_rounded("c1_0", PIECE)]
-        interleave(on_scalar, c1_rounded[0], c1_raw[0], 0, PIECE)
+        c1_rounded = new_rounded("c1")
+        for q in range(2):
+            interleave(on_scalar, c1_rounded[:, width * q:width * (q + 1)], c1_raw[q], 0, PIECE)
         quantize(x_mx[0], x0_rounded, E4M3, PIECE, HALF)
         px_matmul(0, 2)
         px_matmul(0, 3)
@@ -299,13 +303,9 @@ def tile_mix_bilin_tm_pl_silu_kernel(tc, x, wx, c, wc, w_words, w_scales, b, out
             y_matmul(i)
         silu(0)
 
-        c1_rounded.append(new_rounded("c1_1", PIECE, tag="h0_bf16"))
-        interleave_on_gpsimd(c1_rounded[1], c1_raw[1], 0, PIECE)
         steps(1, S1)
-        for q in range(2):
-            cols = slice(PIECE * q, PIECE * (q + 1))
-            nc.vector.quantize_mx(out=c_mx[1][0][:, cols].bitcast(E5M2), scales=c_mx[1][1][:, cols], in_=c1_rounded[q][:])
-        x1_rounded = new_rounded("x1", tag="h0_bf16")
+        quantize(c_mx[1], c1_rounded, E5M2)
+        x1_rounded = new_rounded("x1", tag="c1_bf16")
         deal_on_gpsimd(x1_rounded, x1_raw, 0, HALF)
         pc_dealt.append(new_tile("pc1", [P, PACK, HALF], F32, "pc"))
         for j in range(PACK):
@@ -318,7 +318,7 @@ def tile_mix_bilin_tm_pl_silu_kernel(tc, x, wx, c, wc, w_words, w_scales, b, out
         quantize(x_mx[1], x1_rounded, E4M3)
         for i in range(PACK):
             px_matmul(1, i)
-        out0 = round_out(on_gpsimd, 0, 0, COLS, "h0_bf16")
+        out0 = round_out(on_gpsimd, 0, 0, COLS, "c1_bf16")
         steps(S2, UNITS)
         h1_rounded = new_rounded("h1")
         for i in range(PACK):
@@ -327,21 +327,18 @@ def tile_mix_bilin_tm_pl_silu_kernel(tc, x, wx, c, wc, w_words, w_scales, b, out
             quantize(h_mx[1], h1_rounded, E4M3, P * i, P * (i + 1))
             y_matmul(UNITS + i)
         hand_on(0, 0, [out0])
-        out1s = round_out(on_scalar, 1, G1, COLS)
+        out1 = round_out(on_scalar, 1, 0, COLS)
 
-        out2 = round_out(on_gpsimd, 2, 0, COLS, "h0_bf16")
-        out1g = round_out(on_gpsimd, 1, 0, G1)
+        out2 = round_out(on_gpsimd, 2, 0, COLS, "c1_bf16")
         steps(UNITS, S3)
-        out4s = round_out(on_scalar, 4, 0, S4)
-        hand_on(1, 0, [out1g, out1s, out2])
-        out3g = round_out(on_gpsimd, 3, 0, G3, "h0_bf16")
+        out3s = round_out(on_scalar, 3, 0, S3W)
+        hand_on(1, 0, [out1, out2])
+        out3g = round_out(on_gpsimd, 3, S3W, COLS, "c1_bf16")
         steps(S3, 2 * UNITS)
-        out3v = round_out(on_vector, 3, G3, COLS)
-        out4v = round_out(on_vector, 4, S4, COLS)
-        hand_on(3, 0, [out3g, out3v])
+        out4v = round_out(on_vector, 4, 0, COLS)
+        hand_on(3, 0, [out3s, out3g])
         out5v = round_out(on_vector, 5, 0, V5)
-        out5s = round_out(on_scalar, 5, V5, 2 * P)
-        out5t = round_out(on_scalar, 5, 2 * P, COLS)
-        hand_on(4, 0, [out4s, out4v, out5v, out5s])
-        hand_on(5, 2 * P, [out5t])
+        out5s = round_out(on_scalar, 5, V5, COLS)
+        hand_on(4, 0, [out4v, out5v])
+        hand_on(5, V5, [out5s])
         store_scales(nc.scalar)

@@ -27,16 +27,23 @@ UNITS = M // P
 Y_BANKS = 4
 Z_BUFS = 8
 PIECE = 256
-WC_SPLIT = 352
-C0_SPLIT = 160
-WXA_SPLIT = 96
-X0A_SPLIT = 160
+BY_CHUNK = [(chunk, i) for chunk in range(CHUNKS) for i in range(PACK)]
+ONE_TWO = [(0, i) for i in range(PACK)] + [(chunk, i) for i in range(PACK) for chunk in (1, 2)]
+TWO_ONE = [(chunk, i) for i in range(PACK) for chunk in (0, 1)] + [(2, i) for i in range(PACK)]
+BY_ROW = [(chunk, i) for i in range(PACK) for chunk in range(CHUNKS)]
+FIRST_THEN_ROWS = [(0, 0), (0, 1), (1, 0), (2, 0), (1, 1), (2, 1)] + BY_ROW[6:]
+ORDER = (BY_CHUNK, ONE_TWO)
+SPLIT = ('x0_raw',)
+WC_SPLIT = 384
+C0_SPLIT = 352
+WX_SPLIT = 352
+PC_BEFORE_WX, PC_BEFORE_X = 0, 3
+X0A_SPLIT = 256
 X0B_SPLIT = 160
-ROW_GROUPS = 5
 S1, S2, S3 = 2, 9, 20
-PC_AFTER = {0: (0, 1), 1: (2,), 2: (3,)}
-S3W, V5 = 256, 128
-SINGLE = (0, 1, 2, 3)
+PC_AT = 3
+A1, A2, B1 = 512, 768, 128
+CUTS, SHARES = (640, 1152), (384, 256, 128)
 
 
 def tile_mix_bilin_tm_pl_silu_kernel(tc, x, wx, c, wc, w_words, w_scales, b, out_0, out_1, out_2):
@@ -87,18 +94,21 @@ def tile_mix_bilin_tm_pl_silu_kernel(tc, x, wx, c, wc, w_words, w_scales, b, out
 
         on_gpsimd = None
         def load_halves(name, rows):
+            if name not in SPLIT:
+                raw = load_rows(name, rows)
+                return [raw[:, :, PIECE * q:PIECE * (q + 1)] for q in range(2)]
             return [load_rows("%s%d" % (name, q), rows[:, PIECE * q:PIECE * (q + 1)]) for q in range(2)]
 
         b_per_row = M // P
         b_rows = new_tile("b_rows", [P, b_per_row], F32)
         nc.sync.dma_start(out=b_rows[:], in_=b.rearrange("(p s) -> p s", p=P))
         wc_raw = load_rows("wc_raw", wc)
-        c0_raw = load_halves("c0_raw", c[:, :HALF])
-        wx_raw = load_halves("wx_raw", wx)
+        c0_raw = load_rows("c0_raw", c[:, :HALF])
+        wx_raw = load_rows("wx_raw", wx)
         x0_raw = load_halves("x0_raw", x[:, :HALF])
+        c1_raw = load_halves("c1_raw", c[:, HALF:])
         w_codes = new_tile("w_codes", [P, 2 * M], U8)
         nc.sync.dma_start(out=w_codes[:].bitcast(I32), in_=w_words[0].bitcast(I32))
-        c1_raw = load_halves("c1_raw", c[:, HALF:])
         x1_raw = load_rows("x1_raw", x[:, HALF:])
         ident = new_tile("ident", [P, P], F32)
         make_identity(nc, ident[:])
@@ -127,8 +137,8 @@ def tile_mix_bilin_tm_pl_silu_kernel(tc, x, wx, c, wc, w_words, w_scales, b, out
         x_mx = [new_mx("x%d" % a, HALF) for a in range(2)]
         h_mx = [new_mx("h%d" % a, HALF) for a in range(2)]
         pc_dealt = [new_tile("pc%d" % a, [P, PACK, HALF], F32, "pc") for a in range(1)]
-        result = {}
-        out_scales = new_tile("out_scales", [P, 2, M], U8)
+        result = [(new_tile("result%d_0" % a, [P, PACK, COLS], F32), new_tile("result%d_12" % a, [P, PACK, 2 * COLS], F32)) for a in range(2)]
+        out_scales = new_tile("out_scales", [P, M], U8)
         out_rows = out_0.rearrange("(a p i) n -> a p i n", a=2, i=PACK)
         pc_banks, px_banks, y_banks, biased = {}, {}, {}, {}
 
@@ -179,42 +189,31 @@ def tile_mix_bilin_tm_pl_silu_kernel(tc, x, wx, c, wc, w_words, w_scales, b, out
                                 rhs=w_codes[:, 2 * n0:2 * (n0 + width)].bitcast(E2M1), rhs_scale=w_scale_tile[:, n0:n0 + width],
                                 start=True, stop=True)
 
+        def result_cols(a, lo, hi):
+            return result[a][0][:, :, lo:hi] if hi <= COLS else result[a][1][:, :, lo - COLS:hi - COLS]
+
         def y_matmul(step):
-            group, k = divmod(step, PACK)
-            a, n0 = group // CHUNKS, COLS * (group % CHUNKS)
+            a, (chunk, i) = step // UNITS, ORDER[step // UNITS][step % UNITS]
             y_banks[step] = new_bank("y%d" % step, step % Y_BANKS)
-            if group < ROW_GROUPS:
-                y_pass(y_banks[step][:], a, k, n0, COLS)
-            else:
-                for i in range(PACK):
-                    y_pass(y_banks[step][:, dealt_cols(i)], a, i, n0 + P * k, P)
+            y_pass(y_banks[step][:], a, i, COLS * chunk, COLS)
 
         def add_bias(step):
-            group, k = divmod(step, PACK)
-            n0 = COLS * (group % CHUNKS)
+            n0 = COLS * ORDER[step // UNITS][step % UNITS][0]
             biased[step] = new_tile("biased%d" % step, [P, COLS], F32, "biased%d" % (step % Z_BUFS))
-            if group < ROW_GROUPS:
-                nc.vector.tensor_tensor(out=biased[step][:], in0=y_banks[step][:], in1=bias[:, n0:n0 + COLS], op=ALU.add)
-            else:
-                nc.vector.tensor_tensor(out=biased[step][:].rearrange("p (i n) -> p i n", i=PACK), in0=y_banks[step][:].rearrange("p (i n) -> p i n", i=PACK),
-                                        in1=bias[:, n0 + P * k:n0 + P * (k + 1)].unsqueeze(1).to_broadcast([P, PACK, P]), op=ALU.add)
+            nc.vector.tensor_tensor(out=biased[step][:], in0=y_banks[step][:], in1=bias[:, n0:n0 + COLS], op=ALU.add)
             if step % UNITS + Y_BANKS < UNITS:
                 y_matmul(step + Y_BANKS)
 
         def silu(step):
-            group, k = divmod(step, PACK)
-            a, n0 = group // CHUNKS, COLS * (group % CHUNKS)
-            if k == 0:
-                result[group] = new_tile("result%d" % group, [P, PACK, COLS], F32)
-            first = k if step in SINGLE else k - 1
-            if group < ROW_GROUPS:
-                nc.scalar.activation(out=result[group][:, k, :], in_=biased[step][:], func=ACT.Silu)
-                if step in SINGLE or k % 2:
-                    nc.sync.dma_start(out=out_rows[a, :, first:k + 1, n0:n0 + COLS], in_=result[group][:, first:k + 1, :])
-            else:
-                nc.scalar.activation(out=result[group][:, :, P * k:P * (k + 1)], in_=biased[step][:].rearrange("p (i n) -> p i n", i=PACK), func=ACT.Silu)
-                if step in SINGLE or k % 2:
-                    nc.sync.dma_start(out=out_rows[a, :, :, n0 + P * first:n0 + P * (k + 1)], in_=result[group][:, :, P * first:P * (k + 1)])
+            a, place = divmod(step, UNITS)
+            chunk, i = ORDER[a][place]
+            nc.scalar.activation(out=result_cols(a, COLS * chunk, COLS * (chunk + 1))[:, i, :], in_=biased[step][:], func=ACT.Silu)
+            if place + 1 == UNITS or ORDER[a][place + 1][1] != i:
+                first = place
+                while first > 0 and ORDER[a][first - 1][1] == i:
+                    first -= 1
+                lo, hi = COLS * ORDER[a][first][0], COLS * (chunk + 1)
+                nc.sync.dma_start(out=out_rows[a, :, i, lo:hi], in_=result_cols(a, lo, hi)[:, i, :])
 
         def steps(lo, hi):
             for step in range(lo, hi):
@@ -228,61 +227,61 @@ def tile_mix_bilin_tm_pl_silu_kernel(tc, x, wx, c, wc, w_words, w_scales, b, out
             at = 0
             for part in parts:
                 done, cols = 0, part.shape[1] // PACK
-                for width in (512, 256, 128, 64):
-                    if cols - done >= width:
-                        nc.vector.quantize_mx(out=codes[:, at:at + width].bitcast(E4M3), scales=out_scales[:, a, n0 + at:n0 + at + width],
+                for width in (512, 256, 128):
+                    while cols - done >= width:
+                        nc.vector.quantize_mx(out=codes[:, at:at + width].bitcast(E4M3), scales=out_scales[4 * a:, n0 + at:n0 + at + width],
                                               in_=part[:, PACK * done:PACK * (done + width)])
                         done, at = done + width, at + width
             nc.sync.dma_start(out=out_1[a, :, n0:n0 + total, :].rearrange("p n i -> p (n i)").bitcast(I32), in_=codes[:].bitcast(I32))
 
         def round_out(engine, group, lo, hi, tag=None):
             rounded = new_rounded("out%d_%d" % (group, lo), hi - lo, tag)
+            n0 = COLS * (group % CHUNKS)
+            source = result_cols(group // CHUNKS, n0 + lo, n0 + hi)
             if engine is on_gpsimd:
-                interleave_on_gpsimd(rounded, result[group][:, :, lo:hi], 0, hi - lo)
+                interleave_on_gpsimd(rounded, source, 0, hi - lo)
             else:
-                interleave(engine, rounded, result[group][:, :, lo:hi], 0, hi - lo)
+                interleave(engine, rounded, source, 0, hi - lo)
             return rounded[:]
 
         def store_scales(queue):
-            rows = out_2.rearrange("a (q r) n -> r q a n", r=4)
-            for r in range(4):
-                queue.dma_start(out=rows[r].bitcast(I32), in_=out_scales[r:P:32].bitcast(I32))
+            rows = out_2.rearrange("a (q r) n -> q a r n", r=4)
+            for q in (0, 2, 1, 3):
+                queue.dma_start(out=rows[q].bitcast(I32), in_=out_scales[32 * q:32 * q + 8, :].bitcast(I32))
 
         wc_rounded = new_rounded("wc")
         deal(on_vector, wc_rounded, wc_raw, 0, WC_SPLIT)
         deal(on_scalar, wc_rounded, wc_raw, WC_SPLIT, R)
         quantize(wc_mx, wc_rounded, E4M3)
-        c0_rounded = [new_rounded("c0_%d" % q, PIECE) for q in range(2)]
-        interleave(on_scalar, c0_rounded[0], c0_raw[0], 0, PIECE)
-        interleave(on_vector, c0_rounded[1], c0_raw[1], 0, C0_SPLIT)
-        interleave(on_scalar, c0_rounded[1], c0_raw[1], C0_SPLIT, PIECE)
-        for q in range(2):
-            cols = slice(PIECE * q, PIECE * (q + 1))
-            nc.vector.quantize_mx(out=c_mx[0][0][:, cols].bitcast(E5M2), scales=c_mx[0][1][:, cols], in_=c0_rounded[q][:])
+        c0_rounded = new_rounded("c0")
+        interleave(on_vector, c0_rounded, c0_raw, 0, C0_SPLIT)
+        interleave(on_scalar, c0_rounded, c0_raw, C0_SPLIT, HALF)
+        quantize(c_mx[0], c0_rounded, E5M2)
+        for j in range(PACK):
+            pc_matmul(0, j)
         wx_rounded = new_rounded("wx")
         x0_rounded = new_rounded("x0")
         h0_rounded = new_rounded("h0")
         width = PACK * PIECE
-        deal_part(on_scalar, dealt_view(wx_rounded[:, :width]), wx_raw[0], 0, WXA_SPLIT, PIECE)
-        for j in range(PACK):
-            pc_matmul(0, j)
-        for j in range(PACK - 1):
+        for j in range(PC_BEFORE_WX):
             pc_copy(0, j)
-        deal_part(on_scalar, dealt_view(x0_rounded[:, :width]), x0_raw[0], 0, X0A_SPLIT, PIECE)
-        pc_copy(0, PACK - 1)
-        deal_part(on_vector, dealt_view(wx_rounded[:, :width]), wx_raw[0], 0, 0, WXA_SPLIT)
-        for j in range(PACK):
-            quantize_piece(wx_mx, wx_rounded, 0, j)
-        deal_part(on_vector, dealt_view(wx_rounded[:, width:]), wx_raw[1], 0, 0, PIECE)
+        deal(on_vector, wx_rounded, wx_raw, 0, WX_SPLIT)
+        if WX_SPLIT < R:
+            deal(on_scalar, wx_rounded, wx_raw, WX_SPLIT, R)
+        quantize(wx_mx, wx_rounded, E4M3)
+        for j in range(PC_BEFORE_WX, PC_BEFORE_X):
+            pc_copy(0, j)
         deal_part(on_vector, dealt_view(x0_rounded[:, :width]), x0_raw[0], 0, 0, X0A_SPLIT)
-        for j in range(PACK):
-            quantize_piece(wx_mx, wx_rounded, 1, j)
+        if X0A_SPLIT < PIECE:
+            deal_part(on_scalar, dealt_view(x0_rounded[:, :width]), x0_raw[0], 0, X0A_SPLIT, PIECE)
         quantize(x_mx[0], x0_rounded, E4M3, 0, PIECE)
         px_matmul(0, 0)
         px_matmul(0, 1)
         deal_part(on_vector, dealt_view(x0_rounded[:, width:]), x0_raw[1], 0, 0, X0B_SPLIT)
         deal_part(on_scalar, dealt_view(x0_rounded[:, width:]), x0_raw[1], 0, X0B_SPLIT, PIECE)
-        c1_rounded = new_rounded("c1")
+        for j in range(PC_BEFORE_X, PACK):
+            pc_copy(0, j)
+        c1_rounded = new_rounded("c1", tag="turns")
         for q in range(2):
             interleave(on_scalar, c1_rounded[:, width * q:width * (q + 1)], c1_raw[q], 0, PIECE)
         quantize(x_mx[0], x0_rounded, E4M3, PIECE, HALF)
@@ -305,40 +304,43 @@ def tile_mix_bilin_tm_pl_silu_kernel(tc, x, wx, c, wc, w_words, w_scales, b, out
 
         steps(1, S1)
         quantize(c_mx[1], c1_rounded, E5M2)
-        x1_rounded = new_rounded("x1", tag="c1_bf16")
-        deal_on_gpsimd(x1_rounded, x1_raw, 0, HALF)
-        pc_dealt.append(new_tile("pc1", [P, PACK, HALF], F32, "pc"))
         for j in range(PACK):
             pc_matmul(1, j)
+        x1_rounded = new_rounded("x1", tag="turns")
+        deal_on_gpsimd(x1_rounded, x1_raw, 0, HALF)
+        pc_dealt.append(new_tile("pc1", [P, PACK, HALF], F32, "pc"))
         for step in range(S1, S2):
             add_bias(step)
             silu(step)
-            for j in PC_AFTER.get(step - S1, ()):
-                pc_copy(1, j)
+            if 0 <= step - PC_AT < PACK:
+                pc_copy(1, step - PC_AT)
         quantize(x_mx[1], x1_rounded, E4M3)
         for i in range(PACK):
             px_matmul(1, i)
-        out0 = round_out(on_gpsimd, 0, 0, COLS, "c1_bf16")
+        out0g = round_out(on_gpsimd, 0, 0, A1, "turns")
         steps(S2, UNITS)
+        out0s = [round_out(on_scalar, 0, A1, A2)] if A2 > A1 else []
         h1_rounded = new_rounded("h1")
         for i in range(PACK):
             product(h1_rounded, 1, i)
         for i in range(PACK):
             quantize(h_mx[1], h1_rounded, E4M3, P * i, P * (i + 1))
             y_matmul(UNITS + i)
-        hand_on(0, 0, [out0])
-        out1 = round_out(on_scalar, 1, 0, COLS)
+        hand_on(0, 0, [out0g])
 
-        out2 = round_out(on_gpsimd, 2, 0, COLS, "c1_bf16")
-        steps(UNITS, S3)
-        out3s = round_out(on_scalar, 3, 0, S3W)
-        hand_on(1, 0, [out1, out2])
-        out3g = round_out(on_gpsimd, 3, S3W, COLS, "c1_bf16")
-        steps(S3, 2 * UNITS)
-        out4v = round_out(on_vector, 4, 0, COLS)
-        hand_on(3, 0, [out3s, out3g])
-        out5v = round_out(on_vector, 5, 0, V5)
-        out5s = round_out(on_scalar, 5, V5, COLS)
-        hand_on(4, 0, [out4v, out5v])
-        hand_on(5, V5, [out5s])
+        out0h = round_out(on_gpsimd, 0, A2, M, "turns")
+        steps(UNITS, UNITS + PACK)
+        early = [round_out(on_gpsimd, 3, 0, B1)]
+        steps(UNITS + PACK, 2 * UNITS)
+        hand_on(0, A1, out0s + [out0h])
+        cuts = [B1] + list(CUTS) + [M]
+        waiting = None
+        for lo, hi, split in zip(cuts, cuts[1:], SHARES):
+            parts = [round_out(on_vector, 3, lo, lo + split)]
+            if lo + split < hi:
+                parts.append(round_out(on_scalar, 3, lo + split, hi))
+            if waiting:
+                hand_on(3, *waiting)
+            waiting = (lo, parts) if waiting else (0, early + parts)
+        hand_on(3, *waiting)
         store_scales(nc.scalar)

@@ -31,7 +31,6 @@ BY_CHUNK = [(chunk, i) for chunk in range(CHUNKS) for i in range(PACK)]
 ONE_TWO = [(0, i) for i in range(PACK)] + [(chunk, i) for i in range(PACK) for chunk in (1, 2)]
 TWO_ONE = [(chunk, i) for i in range(PACK) for chunk in (0, 1)] + [(2, i) for i in range(PACK)]
 BY_ROW = [(chunk, i) for i in range(PACK) for chunk in range(CHUNKS)]
-FIRST_THEN_ROWS = [(0, 0), (0, 1), (1, 0), (2, 0), (1, 1), (2, 1)] + BY_ROW[6:]
 ORDER = (BY_CHUNK, ONE_TWO)
 SPLIT = ('x0_raw',)
 WC_SPLIT = 384
@@ -40,10 +39,9 @@ WX_SPLIT = 352
 PC_BEFORE_WX, PC_BEFORE_X = 0, 3
 X0A_SPLIT = 256
 X0B_SPLIT = 160
-S1, S2, S3 = 2, 9, 20
+S1, S2 = 2, 9
 PC_AT = 3
-A1, A2, B1 = 512, 768, 128
-CUTS, SHARES = (640, 1152), (384, 256, 128)
+G1, G3, V4, V5 = 128, 512, 320, (128, 0)
 
 
 def tile_mix_bilin_tm_pl_silu_kernel(tc, x, wx, c, wc, w_words, w_scales, b, out_0, out_1, out_2):
@@ -92,7 +90,6 @@ def tile_mix_bilin_tm_pl_silu_kernel(tc, x, wx, c, wc, w_words, w_scales, b, out
 
         on_vector, on_scalar = nc.vector.tensor_copy, nc.scalar.copy
 
-        on_gpsimd = None
         def load_halves(name, rows):
             if name not in SPLIT:
                 raw = load_rows(name, rows)
@@ -106,7 +103,7 @@ def tile_mix_bilin_tm_pl_silu_kernel(tc, x, wx, c, wc, w_words, w_scales, b, out
         c0_raw = load_rows("c0_raw", c[:, :HALF])
         wx_raw = load_rows("wx_raw", wx)
         x0_raw = load_halves("x0_raw", x[:, :HALF])
-        c1_raw = load_halves("c1_raw", c[:, HALF:])
+        c1_raw = load_rows("c1_raw", c[:, HALF:])
         w_codes = new_tile("w_codes", [P, 2 * M], U8)
         nc.sync.dma_start(out=w_codes[:].bitcast(I32), in_=w_words[0].bitcast(I32))
         x1_raw = load_rows("x1_raw", x[:, HALF:])
@@ -172,16 +169,15 @@ def tile_mix_bilin_tm_pl_silu_kernel(tc, x, wx, c, wc, w_words, w_scales, b, out
                 nc.tensor.matmul_mx(out=px_banks[a, part][:, cols], lhsT=wx_mx[0][:, cols].bitcast(E4M3), lhsT_scale=wx_mx[1][:, cols],
                                     rhs=x_mx[a][0][:, tokens].bitcast(E4M3), rhs_scale=x_mx[a][1][:, tokens], start=True, stop=True)
 
-        def product(h_rounded, a, part):
-            out = h_rounded[:, HALF * part:HALF * (part + 1)].rearrange("p (g u j) -> p g j u", u=2, j=PACK)
-            nc.vector.tensor_tensor(out=out, in0=px_banks[a, part][:].rearrange("p (j g u) -> p g j u", j=PACK, u=2),
-                                    in1=pc_dealt[a][:, :, dealt_cols(part)].rearrange("p j (g u) -> p g j u", u=2), op=ALU.mult)
-
-        def quantize_piece(mx, rounded, q, j):
-            src, dst = PIECE * q + 64 * j, P * j + 64 * q
-            codes, scales = mx
-            nc.vector.quantize_mx(out=codes[:, dst:dst + 64].bitcast(E4M3), scales=scales[:, dst:dst + 64],
-                                  in_=rounded[:, PACK * src:PACK * (src + 64)])
+        def product(h_rounded, a, q, i):
+            count = P // pieces[a]
+            place = PACK * count * q + count * i
+            part, lo = divmod(place, P)
+            first = PACK * (P * i + count * q)
+            out = h_rounded[:, first:first + PACK * count].rearrange("p (g u j) -> p g j u", u=2, j=PACK)
+            px = px_banks[a, part][:].rearrange("p (j t) -> p j t", j=PACK)[:, :, lo:lo + count]
+            nc.vector.tensor_tensor(out=out, in0=px.rearrange("p j (g u) -> p g j u", u=2),
+                                    in1=pc_dealt[a][:, :, place:place + count].rearrange("p j (g u) -> p g j u", u=2), op=ALU.mult)
 
         def y_pass(out, a, i, n0, width):
             tokens = dealt_cols(i)
@@ -220,29 +216,15 @@ def tile_mix_bilin_tm_pl_silu_kernel(tc, x, wx, c, wc, w_words, w_scales, b, out
                 add_bias(step)
                 silu(step)
 
-        def hand_on(group, lo, parts):
-            a, n0 = group // CHUNKS, COLS * (group % CHUNKS) + lo
-            total = sum(part.shape[1] for part in parts) // PACK
+        def hand_on(a, n0, tiles):
+            total = sum(t.shape[1] for t in tiles) // PACK
             codes = new_tile("out_codes%d_%d" % (a, n0), [P, total], U32)
             at = 0
-            for part in parts:
-                done, cols = 0, part.shape[1] // PACK
-                for width in (512, 256, 128):
-                    while cols - done >= width:
-                        nc.vector.quantize_mx(out=codes[:, at:at + width].bitcast(E4M3), scales=out_scales[4 * a:, n0 + at:n0 + at + width],
-                                              in_=part[:, PACK * done:PACK * (done + width)])
-                        done, at = done + width, at + width
+            for t in tiles:
+                cols = t.shape[1] // PACK
+                nc.vector.quantize_mx(out=codes[:, at:at + cols].bitcast(E4M3), scales=out_scales[4 * a:, n0 + at:n0 + at + cols], in_=t[:])
+                at += cols
             nc.sync.dma_start(out=out_1[a, :, n0:n0 + total, :].rearrange("p n i -> p (n i)").bitcast(I32), in_=codes[:].bitcast(I32))
-
-        def round_out(engine, group, lo, hi, tag=None):
-            rounded = new_rounded("out%d_%d" % (group, lo), hi - lo, tag)
-            n0 = COLS * (group % CHUNKS)
-            source = result_cols(group // CHUNKS, n0 + lo, n0 + hi)
-            if engine is on_gpsimd:
-                interleave_on_gpsimd(rounded, source, 0, hi - lo)
-            else:
-                interleave(engine, rounded, source, 0, hi - lo)
-            return rounded[:]
 
         def store_scales(queue):
             rows = out_2.rearrange("a (q r) n -> q a r n", r=4)
@@ -282,27 +264,23 @@ def tile_mix_bilin_tm_pl_silu_kernel(tc, x, wx, c, wc, w_words, w_scales, b, out
         for j in range(PC_BEFORE_X, PACK):
             pc_copy(0, j)
         c1_rounded = new_rounded("c1", tag="turns")
-        for q in range(2):
-            interleave(on_scalar, c1_rounded[:, width * q:width * (q + 1)], c1_raw[q], 0, PIECE)
+        interleave(on_scalar, c1_rounded, c1_raw, 0, HALF)
         quantize(x_mx[0], x0_rounded, E4M3, PIECE, HALF)
         px_matmul(0, 2)
         px_matmul(0, 3)
-        for part in range(3):
-            product(h0_rounded, 0, part)
         for i in range(PACK):
-            quantize_piece(h_mx[0], h0_rounded, 0, i)
-        for i in range(2):
-            quantize_piece(h_mx[0], h0_rounded, 1, i)
-        product(h0_rounded, 0, 3)
-        for i in range(2):
-            y_matmul(i)
-        add_bias(0)
-        for i in range(2, PACK):
-            quantize_piece(h_mx[0], h0_rounded, 1, i)
-            y_matmul(i)
-        silu(0)
+            product(h0_rounded, 0, 0, i)
+        for i in range(3):
+            product(h0_rounded, 0, 1, i)
+        quantize(h_mx[0], h0_rounded, E4M3, 0, 2 * P)
+        y_matmul(0)
+        y_matmul(1)
+        product(h0_rounded, 0, 1, 3)
+        quantize(h_mx[0], h0_rounded, E4M3, 2 * P, HALF)
+        y_matmul(2)
+        y_matmul(3)
 
-        steps(1, S1)
+        steps(0, S1)
         quantize(c_mx[1], c1_rounded, E5M2)
         for j in range(PACK):
             pc_matmul(1, j)
@@ -317,30 +295,45 @@ def tile_mix_bilin_tm_pl_silu_kernel(tc, x, wx, c, wc, w_words, w_scales, b, out
         quantize(x_mx[1], x1_rounded, E4M3)
         for i in range(PACK):
             px_matmul(1, i)
-        out0g = round_out(on_gpsimd, 0, 0, A1, "turns")
+        rounded = [new_rounded("out0", tag="turns")]
+        interleave_on_gpsimd(rounded[0], result_cols(0, 0, COLS), 0, COLS)
         steps(S2, UNITS)
-        out0s = [round_out(on_scalar, 0, A1, A2)] if A2 > A1 else []
+        rounded.append(new_rounded("out1"))
+        if G1:
+            interleave_on_gpsimd(rounded[1], result_cols(0, COLS, 2 * COLS), 0, G1)
+        interleave(on_scalar, rounded[1], result_cols(0, COLS, 2 * COLS), G1, COLS)
         h1_rounded = new_rounded("h1")
         for i in range(PACK):
-            product(h1_rounded, 1, i)
-        for i in range(PACK):
-            quantize(h_mx[1], h1_rounded, E4M3, P * i, P * (i + 1))
-            y_matmul(UNITS + i)
-        hand_on(0, 0, [out0g])
+            product(h1_rounded, 1, 0, i)
+        for half in range(2):
+            quantize(h_mx[1], h1_rounded, E4M3, 2 * P * half, 2 * P * (half + 1))
+            y_matmul(UNITS + 2 * half)
+            y_matmul(UNITS + 2 * half + 1)
+        hand_on(0, 0, rounded[:1])
 
-        out0h = round_out(on_gpsimd, 0, A2, M, "turns")
-        steps(UNITS, UNITS + PACK)
-        early = [round_out(on_gpsimd, 3, 0, B1)]
-        steps(UNITS + PACK, 2 * UNITS)
-        hand_on(0, A1, out0s + [out0h])
-        cuts = [B1] + list(CUTS) + [M]
-        waiting = None
-        for lo, hi, split in zip(cuts, cuts[1:], SHARES):
-            parts = [round_out(on_vector, 3, lo, lo + split)]
-            if lo + split < hi:
-                parts.append(round_out(on_scalar, 3, lo + split, hi))
-            if waiting:
-                hand_on(3, *waiting)
-            waiting = (lo, parts) if waiting else (0, early + parts)
-        hand_on(3, *waiting)
+        rounded.append(new_rounded("out2", tag="turns"))
+        interleave_on_gpsimd(rounded[2], result_cols(0, 2 * COLS, M), 0, COLS)
+        steps(UNITS, 2 * UNITS)
+        rounded.append(new_rounded("out3"))
+        interleave_on_gpsimd(rounded[3], result_cols(1, 0, COLS), 0, G3)
+        hand_on(0, COLS, rounded[1:3])
+        if G3 < COLS:
+            interleave(on_vector, rounded[3], result_cols(1, 0, COLS), G3, COLS)
+        else:
+            hand_on(1, 0, rounded[3:4])
+        rounded.append(new_rounded("out4"))
+        interleave(on_vector, rounded[4], result_cols(1, COLS, 2 * COLS), 0, V4)
+        if V4 < COLS:
+            interleave(on_scalar, rounded[4], result_cols(1, COLS, 2 * COLS), V4, COLS)
+        if G3 < COLS:
+            hand_on(1, 0, rounded[3:4])
+        last = [new_rounded("out5_%d" % q, PIECE) for q in range(2)]
+        for q in range(2):
+            source = result_cols(1, 2 * COLS + PIECE * q, 2 * COLS + PIECE * (q + 1))
+            if V5[q]:
+                interleave(on_vector, last[q], source, 0, V5[q])
+            if V5[q] < PIECE:
+                interleave(on_scalar, last[q], source, V5[q], PIECE)
+        hand_on(1, COLS, [rounded[4], last[0]])
+        hand_on(1, 2 * COLS + PIECE, last[1:])
         store_scales(nc.scalar)

@@ -38,10 +38,12 @@ C0_SPLIT = 352
 WX_SPLIT = 352
 PC_BEFORE_WX, PC_BEFORE_X = 0, 3
 X0A_SPLIT = 256
-X0B_SPLIT = 160
-S1, S2 = 2, 9
-PC_AT = 3
-G1, G3, V4, V5 = 128, 512, 320, (128, 0)
+X0B_SPLIT = 96
+S2 = 8
+PC_AT = 2
+G1, G3, V4, V5 = 128, 512, 384, (128, 0)
+
+C1_SPLIT = 192
 
 
 def tile_mix_bilin_tm_pl_silu_kernel(tc, x, wx, c, wc, w_words, w_scales, b, out_0, out_1, out_2):
@@ -115,9 +117,6 @@ def tile_mix_bilin_tm_pl_silu_kernel(tc, x, wx, c, wc, w_words, w_scales, b, out
         w_scale_rows = w_scales[0].rearrange("(q r) n -> r q n", r=4)
         for r in range(4):
             nc.gpsimd.dma_start(out=w_scale_tile[r:P:32, :].bitcast(I32), in_=w_scale_rows[r].bitcast(I32))
-
-        warm = new_tile("warm", [P, 1], F32)
-        nc.scalar.activation(out=warm[:], in_=ident[:, 0:1], func=ACT.Silu)
 
         bias = new_tile("bias", [P, M], F32)
         bias_ns = bias[:].rearrange("p (n s) -> p n s", s=b_per_row)
@@ -243,19 +242,15 @@ def tile_mix_bilin_tm_pl_silu_kernel(tc, x, wx, c, wc, w_words, w_scales, b, out
             pc_matmul(0, j)
         wx_rounded = new_rounded("wx")
         x0_rounded = new_rounded("x0")
-        h0_rounded = new_rounded("h0")
+        h0_rounded = new_rounded("h0", tag="turns")
         width = PACK * PIECE
-        for j in range(PC_BEFORE_WX):
-            pc_copy(0, j)
         deal(on_vector, wx_rounded, wx_raw, 0, WX_SPLIT)
         if WX_SPLIT < R:
             deal(on_scalar, wx_rounded, wx_raw, WX_SPLIT, R)
-        quantize(wx_mx, wx_rounded, E4M3)
-        for j in range(PC_BEFORE_WX, PC_BEFORE_X):
+        for j in range(PC_BEFORE_X):
             pc_copy(0, j)
-        deal_part(on_vector, dealt_view(x0_rounded[:, :width]), x0_raw[0], 0, 0, X0A_SPLIT)
-        if X0A_SPLIT < PIECE:
-            deal_part(on_scalar, dealt_view(x0_rounded[:, :width]), x0_raw[0], 0, X0A_SPLIT, PIECE)
+        deal_part(on_vector, dealt_view(x0_rounded[:, :width]), x0_raw[0], 0, 0, PIECE)
+        quantize(wx_mx, wx_rounded, E4M3)
         quantize(x_mx[0], x0_rounded, E4M3, 0, PIECE)
         px_matmul(0, 0)
         px_matmul(0, 1)
@@ -263,11 +258,12 @@ def tile_mix_bilin_tm_pl_silu_kernel(tc, x, wx, c, wc, w_words, w_scales, b, out
         deal_part(on_scalar, dealt_view(x0_rounded[:, width:]), x0_raw[1], 0, X0B_SPLIT, PIECE)
         for j in range(PC_BEFORE_X, PACK):
             pc_copy(0, j)
-        c1_rounded = new_rounded("c1", tag="turns")
-        interleave(on_scalar, c1_rounded, c1_raw, 0, HALF)
         quantize(x_mx[0], x0_rounded, E4M3, PIECE, HALF)
         px_matmul(0, 2)
         px_matmul(0, 3)
+        c1_rounded = new_rounded("c1", tag="x0_bf16")
+        interleave_on_gpsimd(c1_rounded, c1_raw, 0, C1_SPLIT)
+        interleave(on_scalar, c1_rounded, c1_raw, C1_SPLIT, HALF)
         for i in range(PACK):
             product(h0_rounded, 0, 0, i)
         for i in range(3):
@@ -276,18 +272,17 @@ def tile_mix_bilin_tm_pl_silu_kernel(tc, x, wx, c, wc, w_words, w_scales, b, out
         y_matmul(0)
         y_matmul(1)
         product(h0_rounded, 0, 1, 3)
+        quantize(c_mx[1], c1_rounded, E5M2)
         quantize(h_mx[0], h0_rounded, E4M3, 2 * P, HALF)
         y_matmul(2)
         y_matmul(3)
-
-        steps(0, S1)
-        quantize(c_mx[1], c1_rounded, E5M2)
         for j in range(PACK):
             pc_matmul(1, j)
+
         x1_rounded = new_rounded("x1", tag="turns")
         deal_on_gpsimd(x1_rounded, x1_raw, 0, HALF)
         pc_dealt.append(new_tile("pc1", [P, PACK, HALF], F32, "pc"))
-        for step in range(S1, S2):
+        for step in range(S2):
             add_bias(step)
             silu(step)
             if 0 <= step - PC_AT < PACK:

@@ -22,28 +22,23 @@ PACK = 4
 HALF = P * PACK
 COLS = 512
 CHUNKS = M // COLS
+PIECE = HALF // 2
+PIECES = (2, 1)
 
-UNITS = M // P
+STEPS = CHUNKS * PACK
+ORDER = ([(chunk, i) for chunk in range(CHUNKS) for i in range(PACK)],
+         [(0, i) for i in range(PACK)] + [(chunk, i) for i in range(PACK) for chunk in (1, 2)])
 Y_BANKS = 4
-Z_BUFS = 8
-PIECE = 256
-BY_CHUNK = [(chunk, i) for chunk in range(CHUNKS) for i in range(PACK)]
-ONE_TWO = [(0, i) for i in range(PACK)] + [(chunk, i) for i in range(PACK) for chunk in (1, 2)]
-TWO_ONE = [(chunk, i) for i in range(PACK) for chunk in (0, 1)] + [(2, i) for i in range(PACK)]
-BY_ROW = [(chunk, i) for i in range(PACK) for chunk in range(CHUNKS)]
-ORDER = (BY_CHUNK, ONE_TWO)
-SPLIT = ('x0_raw',)
+BIASED_BUFS = 8
+BESIDE_C1 = 7
+
 WC_SPLIT = 384
 C0_SPLIT = 352
 WX_SPLIT = 352
-PC_BEFORE_WX, PC_BEFORE_X = 0, 3
-X0A_SPLIT = 256
-X0B_SPLIT = 96
-S2 = 8
-PC_AT = 2
-G1, G3, V4, V5 = 128, 512, 384, (128, 0)
-
-C1_SPLIT = 192
+X0_SPLIT = 160
+OUT_01_SPLIT = 224
+OUT_11_SPLIT = 320
+OUT_12_SPLIT = 128
 
 
 def tile_mix_bilin_tm_pl_silu_kernel(tc, x, wx, c, wc, w_words, w_scales, b, out_0, out_1, out_2):
@@ -70,18 +65,24 @@ def tile_mix_bilin_tm_pl_silu_kernel(tc, x, wx, c, wc, w_words, w_scales, b, out
             nc.sync.dma_start(out=raw[:], in_=rows.rearrange("(p e) n -> p e n", e=PACK))
             return raw
 
+        def load_pieces(name, rows):
+            return [load_rows("%s%d" % (name, q), rows[:, PIECE * q:PIECE * (q + 1)]) for q in range(2)]
+
+        def on_gpsimd(out, in_):
+            nc.gpsimd.tensor_scalar(out=out, in0=in_, scalar1=1.0, scalar2=-0.0, op0=ALU.mult, op1=ALU.add)
+
+        on_vector, on_scalar = nc.vector.tensor_copy, nc.scalar.copy
+
         def interleave(copy, rounded, raw, lo, hi):
             out = rounded[:, PACK * lo:PACK * hi].rearrange("p (g u e) -> p g e u", u=4, e=PACK)
             copy(out=out, in_=raw[:, :, lo:hi].rearrange("p e (g u) -> p g e u", u=4))
 
-        def interleave_on_gpsimd(rounded, raw, lo, hi):
-            out = rounded[:, PACK * lo:PACK * hi].rearrange("p (g u e) -> p g e u", u=4, e=PACK)
-            nc.gpsimd.tensor_scalar(out=out, in0=raw[:, :, lo:hi].rearrange("p e (g u) -> p g e u", u=4),
-                                    scalar1=1.0, scalar2=-0.0, op0=ALU.mult, op1=ALU.add)
-
-        def deal(copy, rounded, raw, lo, hi):
-            out = rounded[:].rearrange("p (j m e) -> p m e j", j=PACK, e=PACK)[:, lo // PACK:hi // PACK]
+        def deal(copy, rounded, raw, lo, hi, m0=0):
+            out = rounded.rearrange("p (j m e) -> p m e j", j=PACK, e=PACK)[:, m0 + lo // PACK:m0 + hi // PACK]
             copy(out=out, in_=raw[:, :, lo:hi].rearrange("p e (m j) -> p m e j", j=PACK))
+
+        def piece_of(rounded, q):
+            return rounded[:, PACK * PIECE * q:PACK * PIECE * (q + 1)]
 
         def quantize(mx, rounded, fmt, lo=0, hi=HALF):
             codes, scales = mx
@@ -90,28 +91,19 @@ def tile_mix_bilin_tm_pl_silu_kernel(tc, x, wx, c, wc, w_words, w_scales, b, out
         def dealt_cols(j):
             return slice(P * j, P * (j + 1))
 
-        on_vector, on_scalar = nc.vector.tensor_copy, nc.scalar.copy
-
-        def load_halves(name, rows):
-            if name not in SPLIT:
-                raw = load_rows(name, rows)
-                return [raw[:, :, PIECE * q:PIECE * (q + 1)] for q in range(2)]
-            return [load_rows("%s%d" % (name, q), rows[:, PIECE * q:PIECE * (q + 1)]) for q in range(2)]
-
         b_per_row = M // P
         b_rows = new_tile("b_rows", [P, b_per_row], F32)
         nc.sync.dma_start(out=b_rows[:], in_=b.rearrange("(p s) -> p s", p=P))
         wc_raw = load_rows("wc_raw", wc)
         c0_raw = load_rows("c0_raw", c[:, :HALF])
         wx_raw = load_rows("wx_raw", wx)
-        x0_raw = load_halves("x0_raw", x[:, :HALF])
-        c1_raw = load_rows("c1_raw", c[:, HALF:])
+        x0_raw = load_pieces("x0_raw", x[:, :HALF])
+        x1_raw = load_pieces("x1_raw", x[:, HALF:])
         w_codes = new_tile("w_codes", [P, 2 * M], U8)
         nc.sync.dma_start(out=w_codes[:].bitcast(I32), in_=w_words[0].bitcast(I32))
-        x1_raw = load_rows("x1_raw", x[:, HALF:])
+        c1_raw = load_pieces("c1_raw", c[:, HALF:])
         ident = new_tile("ident", [P, P], F32)
         make_identity(nc, ident[:])
-
         w_scale_tile = new_tile("w_scale_tile", [P, M], U8)
         nc.gpsimd.memset(w_scale_tile[:].bitcast(I32), 0)
         w_scale_rows = w_scales[0].rearrange("(q r) n -> r q n", r=4)
@@ -127,28 +119,16 @@ def tile_mix_bilin_tm_pl_silu_kernel(tc, x, wx, c, wc, w_words, w_scales, b, out
                 nc.tensor.transpose(bank[:, P * u:P * (u + 1)], b_rows[:, s:s + 1].to_broadcast([P, P]), ident[:])
             nc.scalar.copy(out=bias_ns[:, :, 4 * group:4 * group + 4], in_=bank[:].rearrange("p (u n) -> p n u", u=4))
 
-        pieces = (2, 1)
         wc_mx, wx_mx = new_mx("wc", R), new_mx("wx", R)
         c_mx = [new_mx("c%d" % a, HALF) for a in range(2)]
         x_mx = [new_mx("x%d" % a, HALF) for a in range(2)]
         h_mx = [new_mx("h%d" % a, HALF) for a in range(2)]
-        pc_dealt = [new_tile("pc%d" % a, [P, PACK, HALF], F32, "pc") for a in range(1)]
-        result = [(new_tile("result%d_0" % a, [P, PACK, COLS], F32), new_tile("result%d_12" % a, [P, PACK, 2 * COLS], F32)) for a in range(2)]
+        pc_dealt = {0: new_tile("pc0", [P, PACK, HALF], F32, "pc")}
+        result = [[new_tile("result0_%d" % chunk, [P, PACK, COLS], F32) for chunk in range(CHUNKS)],
+                  [new_tile("result1_0", [P, PACK, COLS], F32), new_tile("result1_12", [P, PACK, 2 * COLS], F32)]]
         out_scales = new_tile("out_scales", [P, M], U8)
         out_rows = out_0.rearrange("(a p i) n -> a p i n", a=2, i=PACK)
         pc_banks, px_banks, y_banks, biased = {}, {}, {}, {}
-
-        def deal_part(copy, dealt, raw, m0, lo, hi):
-            out = dealt[:, :, m0 + lo // PACK:m0 + hi // PACK, :].rearrange("p j m e -> p m e j")
-            copy(out=out, in_=raw[:, :, lo:hi].rearrange("p e (m j) -> p m e j", j=PACK))
-
-        def deal_on_gpsimd(rounded, raw, lo, hi):
-            out = rounded[:].rearrange("p (j m e) -> p m e j", j=PACK, e=PACK)[:, lo // PACK:hi // PACK]
-            nc.gpsimd.tensor_scalar(out=out, in0=raw[:, :, lo:hi].rearrange("p e (m j) -> p m e j", j=PACK),
-                                    scalar1=1.0, scalar2=-0.0, op0=ALU.mult, op1=ALU.add)
-
-        def dealt_view(rounded):
-            return rounded.rearrange("p (j m e) -> p j m e", j=PACK, e=PACK)
 
         def pc_matmul(a, j):
             pc_banks[a, j] = new_bank("pc%d_%d" % (a, j), 4 + j)
@@ -157,8 +137,8 @@ def tile_mix_bilin_tm_pl_silu_kernel(tc, x, wx, c, wc, w_words, w_scales, b, out
                                 rhs=c_mx[a][0][:].bitcast(E5M2), rhs_scale=c_mx[a][1][:], start=True, stop=True)
 
         def pc_copy(a, j):
-            nc.scalar.copy(out=pc_dealt[a][:, j].rearrange("p (q i m) -> p q i m", q=pieces[a], i=PACK),
-                           in_=pc_banks[a, j][:].rearrange("p (q m i) -> p q i m", q=pieces[a], i=PACK))
+            nc.scalar.copy(out=pc_dealt[a][:, j].rearrange("p (q i m) -> p q i m", q=PIECES[a], i=PACK),
+                           in_=pc_banks[a, j][:].rearrange("p (q m i) -> p q i m", q=PIECES[a], i=PACK))
 
         def px_matmul(a, part):
             px_banks[a, part] = new_bank("px%d_%d" % (a, part), 4 * a + part)
@@ -169,7 +149,7 @@ def tile_mix_bilin_tm_pl_silu_kernel(tc, x, wx, c, wc, w_words, w_scales, b, out
                                     rhs=x_mx[a][0][:, tokens].bitcast(E4M3), rhs_scale=x_mx[a][1][:, tokens], start=True, stop=True)
 
         def product(h_rounded, a, q, i):
-            count = P // pieces[a]
+            count = P // PIECES[a]
             place = PACK * count * q + count * i
             part, lo = divmod(place, P)
             first = PACK * (P * i + count * q)
@@ -178,36 +158,36 @@ def tile_mix_bilin_tm_pl_silu_kernel(tc, x, wx, c, wc, w_words, w_scales, b, out
             nc.vector.tensor_tensor(out=out, in0=px.rearrange("p j (g u) -> p g j u", u=2),
                                     in1=pc_dealt[a][:, :, place:place + count].rearrange("p j (g u) -> p g j u", u=2), op=ALU.mult)
 
-        def y_pass(out, a, i, n0, width):
-            tokens = dealt_cols(i)
-            nc.tensor.matmul_mx(out=out, lhsT=h_mx[a][0][:, tokens].bitcast(E4M3), lhsT_scale=h_mx[a][1][:, tokens],
-                                rhs=w_codes[:, 2 * n0:2 * (n0 + width)].bitcast(E2M1), rhs_scale=w_scale_tile[:, n0:n0 + width],
-                                start=True, stop=True)
+        def tile_of(step):
+            return (step // STEPS,) + ORDER[step // STEPS][step % STEPS]
 
         def result_cols(a, lo, hi):
-            return result[a][0][:, :, lo:hi] if hi <= COLS else result[a][1][:, :, lo - COLS:hi - COLS]
+            index = min(lo // COLS, len(result[a]) - 1)
+            return result[a][index][:, :, lo - COLS * index:hi - COLS * index]
+
+        def result_chunk(a, chunk):
+            return result_cols(a, COLS * chunk, COLS * (chunk + 1))
 
         def y_matmul(step):
-            a, (chunk, i) = step // UNITS, ORDER[step // UNITS][step % UNITS]
+            a, chunk, i = tile_of(step)
             y_banks[step] = new_bank("y%d" % step, step % Y_BANKS)
-            y_pass(y_banks[step][:], a, i, COLS * chunk, COLS)
+            tokens, n0 = dealt_cols(i), COLS * chunk
+            nc.tensor.matmul_mx(out=y_banks[step][:], lhsT=h_mx[a][0][:, tokens].bitcast(E4M3), lhsT_scale=h_mx[a][1][:, tokens],
+                                rhs=w_codes[:, 2 * n0:2 * (n0 + COLS)].bitcast(E2M1), rhs_scale=w_scale_tile[:, n0:n0 + COLS],
+                                start=True, stop=True)
 
         def add_bias(step):
-            n0 = COLS * ORDER[step // UNITS][step % UNITS][0]
-            biased[step] = new_tile("biased%d" % step, [P, COLS], F32, "biased%d" % (step % Z_BUFS))
+            n0 = COLS * tile_of(step)[1]
+            biased[step] = new_tile("biased%d" % step, [P, COLS], F32, "biased%d" % (step % BIASED_BUFS))
             nc.vector.tensor_tensor(out=biased[step][:], in0=y_banks[step][:], in1=bias[:, n0:n0 + COLS], op=ALU.add)
-            if step % UNITS + Y_BANKS < UNITS:
+            if step % STEPS + Y_BANKS < STEPS:
                 y_matmul(step + Y_BANKS)
 
         def silu(step):
-            a, place = divmod(step, UNITS)
-            chunk, i = ORDER[a][place]
-            nc.scalar.activation(out=result_cols(a, COLS * chunk, COLS * (chunk + 1))[:, i, :], in_=biased[step][:], func=ACT.Silu)
-            if place + 1 == UNITS or ORDER[a][place + 1][1] != i:
-                first = place
-                while first > 0 and ORDER[a][first - 1][1] == i:
-                    first -= 1
-                lo, hi = COLS * ORDER[a][first][0], COLS * (chunk + 1)
+            a, chunk, i = tile_of(step)
+            nc.scalar.activation(out=result_chunk(a, chunk)[:, i, :], in_=biased[step][:], func=ACT.Silu)
+            if (a, chunk) != (1, 1):
+                lo, hi = COLS * (1 if (a, chunk) == (1, 2) else chunk), COLS * (chunk + 1)
                 nc.sync.dma_start(out=out_rows[a, :, i, lo:hi], in_=result_cols(a, lo, hi)[:, i, :])
 
         def steps(lo, hi):
@@ -225,14 +205,9 @@ def tile_mix_bilin_tm_pl_silu_kernel(tc, x, wx, c, wc, w_words, w_scales, b, out
                 at += cols
             nc.sync.dma_start(out=out_1[a, :, n0:n0 + total, :].rearrange("p n i -> p (n i)").bitcast(I32), in_=codes[:].bitcast(I32))
 
-        def store_scales(queue):
-            rows = out_2.rearrange("a (q r) n -> q a r n", r=4)
-            for q in (0, 2, 1, 3):
-                queue.dma_start(out=rows[q].bitcast(I32), in_=out_scales[32 * q:32 * q + 8, :].bitcast(I32))
-
         wc_rounded = new_rounded("wc")
-        deal(on_vector, wc_rounded, wc_raw, 0, WC_SPLIT)
-        deal(on_scalar, wc_rounded, wc_raw, WC_SPLIT, R)
+        deal(on_vector, wc_rounded[:], wc_raw, 0, WC_SPLIT)
+        deal(on_scalar, wc_rounded[:], wc_raw, WC_SPLIT, R)
         quantize(wc_mx, wc_rounded, E4M3)
         c0_rounded = new_rounded("c0")
         interleave(on_vector, c0_rounded, c0_raw, 0, C0_SPLIT)
@@ -243,92 +218,86 @@ def tile_mix_bilin_tm_pl_silu_kernel(tc, x, wx, c, wc, w_words, w_scales, b, out
         wx_rounded = new_rounded("wx")
         x0_rounded = new_rounded("x0")
         h0_rounded = new_rounded("h0", tag="turns")
-        width = PACK * PIECE
-        deal(on_vector, wx_rounded, wx_raw, 0, WX_SPLIT)
-        if WX_SPLIT < R:
-            deal(on_scalar, wx_rounded, wx_raw, WX_SPLIT, R)
-        for j in range(PC_BEFORE_X):
+        deal(on_vector, wx_rounded[:], wx_raw, 0, WX_SPLIT)
+        deal(on_scalar, wx_rounded[:], wx_raw, WX_SPLIT, R)
+        for j in range(PACK - 1):
             pc_copy(0, j)
-        deal_part(on_vector, dealt_view(x0_rounded[:, :width]), x0_raw[0], 0, 0, PIECE)
+        deal(on_vector, piece_of(x0_rounded, 0), x0_raw[0], 0, PIECE)
         quantize(wx_mx, wx_rounded, E4M3)
         quantize(x_mx[0], x0_rounded, E4M3, 0, PIECE)
         px_matmul(0, 0)
         px_matmul(0, 1)
-        deal_part(on_vector, dealt_view(x0_rounded[:, width:]), x0_raw[1], 0, 0, X0B_SPLIT)
-        deal_part(on_scalar, dealt_view(x0_rounded[:, width:]), x0_raw[1], 0, X0B_SPLIT, PIECE)
-        for j in range(PC_BEFORE_X, PACK):
-            pc_copy(0, j)
+        deal(on_vector, piece_of(x0_rounded, 1), x0_raw[1], 0, X0_SPLIT)
+        deal(on_scalar, piece_of(x0_rounded, 1), x0_raw[1], X0_SPLIT, PIECE)
+        pc_copy(0, PACK - 1)
         quantize(x_mx[0], x0_rounded, E4M3, PIECE, HALF)
         px_matmul(0, 2)
         px_matmul(0, 3)
-        c1_rounded = new_rounded("c1", tag="x0_bf16")
-        interleave_on_gpsimd(c1_rounded, c1_raw, 0, C1_SPLIT)
-        interleave(on_scalar, c1_rounded, c1_raw, C1_SPLIT, HALF)
+        x1_rounded = new_rounded("x1")
+        for q in range(2):
+            deal(on_scalar, x1_rounded[:], x1_raw[q], 0, PIECE, m0=q * PIECE // PACK)
+
         for i in range(PACK):
             product(h0_rounded, 0, 0, i)
-        for i in range(3):
+        for i in range(PACK - 1):
             product(h0_rounded, 0, 1, i)
-        quantize(h_mx[0], h0_rounded, E4M3, 0, 2 * P)
+        quantize(h_mx[0], h0_rounded, E4M3, 0, PIECE)
         y_matmul(0)
         y_matmul(1)
-        product(h0_rounded, 0, 1, 3)
-        quantize(c_mx[1], c1_rounded, E5M2)
-        quantize(h_mx[0], h0_rounded, E4M3, 2 * P, HALF)
+        product(h0_rounded, 0, 1, PACK - 1)
+        quantize(x_mx[1], x1_rounded, E4M3)
+        quantize(h_mx[0], h0_rounded, E4M3, PIECE, HALF)
         y_matmul(2)
         y_matmul(3)
+
+        c1_rounded = new_rounded("c1", tag="turns")
+        for q in range(2):
+            interleave(on_gpsimd, piece_of(c1_rounded, q), c1_raw[q], 0, PIECE)
+        steps(0, BESIDE_C1)
+        quantize(c_mx[1], c1_rounded, E5M2)
         for j in range(PACK):
             pc_matmul(1, j)
-
-        x1_rounded = new_rounded("x1", tag="turns")
-        deal_on_gpsimd(x1_rounded, x1_raw, 0, HALF)
-        pc_dealt.append(new_tile("pc1", [P, PACK, HALF], F32, "pc"))
-        for step in range(S2):
+        out_00 = new_rounded("out_00", tag="turns")
+        interleave(on_gpsimd, out_00, result_chunk(0, 0), 0, COLS)
+        pc_dealt[1] = new_tile("pc1", [P, PACK, HALF], F32, "pc")
+        for step in range(BESIDE_C1, STEPS):
             add_bias(step)
+        for j in range(PACK):
+            pc_copy(1, j)
+            px_matmul(1, j)
+        for step in range(BESIDE_C1, STEPS):
             silu(step)
-            if 0 <= step - PC_AT < PACK:
-                pc_copy(1, step - PC_AT)
-        quantize(x_mx[1], x1_rounded, E4M3)
-        for i in range(PACK):
-            px_matmul(1, i)
-        rounded = [new_rounded("out0", tag="turns")]
-        interleave_on_gpsimd(rounded[0], result_cols(0, 0, COLS), 0, COLS)
-        steps(S2, UNITS)
-        rounded.append(new_rounded("out1"))
-        if G1:
-            interleave_on_gpsimd(rounded[1], result_cols(0, COLS, 2 * COLS), 0, G1)
-        interleave(on_scalar, rounded[1], result_cols(0, COLS, 2 * COLS), G1, COLS)
+        out_01 = new_rounded("out_01")
+        interleave(on_gpsimd, out_01, result_chunk(0, 1), 0, OUT_01_SPLIT)
+        interleave(on_scalar, out_01, result_chunk(0, 1), OUT_01_SPLIT, COLS)
+
         h1_rounded = new_rounded("h1")
         for i in range(PACK):
             product(h1_rounded, 1, 0, i)
-        for half in range(2):
-            quantize(h_mx[1], h1_rounded, E4M3, 2 * P * half, 2 * P * (half + 1))
-            y_matmul(UNITS + 2 * half)
-            y_matmul(UNITS + 2 * half + 1)
-        hand_on(0, 0, rounded[:1])
-
-        rounded.append(new_rounded("out2", tag="turns"))
-        interleave_on_gpsimd(rounded[2], result_cols(0, 2 * COLS, M), 0, COLS)
-        steps(UNITS, 2 * UNITS)
-        rounded.append(new_rounded("out3"))
-        interleave_on_gpsimd(rounded[3], result_cols(1, 0, COLS), 0, G3)
-        hand_on(0, COLS, rounded[1:3])
-        if G3 < COLS:
-            interleave(on_vector, rounded[3], result_cols(1, 0, COLS), G3, COLS)
-        else:
-            hand_on(1, 0, rounded[3:4])
-        rounded.append(new_rounded("out4"))
-        interleave(on_vector, rounded[4], result_cols(1, COLS, 2 * COLS), 0, V4)
-        if V4 < COLS:
-            interleave(on_scalar, rounded[4], result_cols(1, COLS, 2 * COLS), V4, COLS)
-        if G3 < COLS:
-            hand_on(1, 0, rounded[3:4])
-        last = [new_rounded("out5_%d" % q, PIECE) for q in range(2)]
         for q in range(2):
-            source = result_cols(1, 2 * COLS + PIECE * q, 2 * COLS + PIECE * (q + 1))
-            if V5[q]:
-                interleave(on_vector, last[q], source, 0, V5[q])
-            if V5[q] < PIECE:
-                interleave(on_scalar, last[q], source, V5[q], PIECE)
-        hand_on(1, COLS, [rounded[4], last[0]])
-        hand_on(1, 2 * COLS + PIECE, last[1:])
-        store_scales(nc.scalar)
+            quantize(h_mx[1], h1_rounded, E4M3, PIECE * q, PIECE * (q + 1))
+            y_matmul(STEPS + 2 * q)
+            y_matmul(STEPS + 2 * q + 1)
+        hand_on(0, 0, [out_00])
+
+        out_02 = new_rounded("out_02", tag="turns")
+        interleave(on_gpsimd, out_02, result_chunk(0, 2), 0, COLS)
+        steps(STEPS, 2 * STEPS)
+        out_10 = new_rounded("out_10")
+        interleave(on_gpsimd, out_10, result_chunk(1, 0), 0, COLS)
+
+        hand_on(0, COLS, [out_01, out_02])
+        hand_on(1, 0, [out_10])
+        out_11 = new_rounded("out_11")
+        interleave(on_vector, out_11, result_chunk(1, 1), 0, OUT_11_SPLIT)
+        interleave(on_scalar, out_11, result_chunk(1, 1), OUT_11_SPLIT, COLS)
+        out_12 = [new_rounded("out_12_%d" % q, PIECE) for q in range(2)]
+        interleave(on_vector, out_12[0], result_chunk(1, 2), 0, OUT_12_SPLIT)
+        interleave(on_scalar, out_12[0], result_chunk(1, 2), OUT_12_SPLIT, PIECE)
+        interleave(on_scalar, out_12[1], result_chunk(1, 2)[:, :, PIECE:], 0, PIECE)
+        hand_on(1, COLS, [out_11, out_12[0]])
+        hand_on(1, 2 * COLS + PIECE, [out_12[1]])
+
+        scale_rows = out_2.rearrange("a (q r) n -> q a r n", r=4)
+        for q in (0, 2, 1, 3):
+            nc.scalar.dma_start(out=scale_rows[q].bitcast(I32), in_=out_scales[32 * q:32 * q + 8, :].bitcast(I32))

@@ -30,7 +30,11 @@ ORDER = ([(chunk, i) for chunk in range(CHUNKS) for i in range(PACK)],
          [(0, i) for i in range(PACK)] + [(chunk, i) for i in range(PACK) for chunk in (1, 2)])
 Y_BANKS = 4
 BIASED_BUFS = 8
-BESIDE_C1 = 7
+S01 = 128
+S11 = 320
+X0A_SPLIT = 256
+BESIDE_C1 = 9
+PC_AFTER = [2, 3, 5, 6]
 
 WC_SPLIT = 384
 C0_SPLIT = 352
@@ -98,14 +102,25 @@ def tile_mix_bilin_tm_pl_silu_kernel(tc, x, wx, c, wc, w_words, w_scales, b, out
         c0_raw = load_rows("c0_raw", c[:, :HALF])
         wx_raw = load_rows("wx_raw", wx)
         x0_raw = load_pieces("x0_raw", x[:, :HALF])
-        x1_raw = load_pieces("x1_raw", x[:, HALF:])
-        w_codes = new_tile("w_codes", [P, 2 * M], U8)
-        nc.sync.dma_start(out=w_codes[:].bitcast(I32), in_=w_words[0].bitcast(I32))
-        c1_raw = load_pieces("c1_raw", c[:, HALF:])
+        c1_raw = [load_rows("c1_raw0", c[:, HALF:HALF + PIECE])]
+
+        def load_w(lo, hi):
+            words = new_tile("w_codes%d" % lo, [P, 2 * COLS * (hi - lo)], U8)
+            nc.sync.dma_start(out=words[:].bitcast(I32), in_=w_words[0, :, 2 * COLS * lo:2 * COLS * hi].bitcast(I32))
+            return [words[:, 2 * COLS * u:2 * COLS * (u + 1)] for u in range(hi - lo)]
+
+        w_codes = load_w(0, 1)
+        c1_raw.append(load_rows("c1_raw1", c[:, HALF + PIECE:]))
+        x1_raw = [load_rows("x1_raw0", x[:, HALF:HALF + PIECE])]
+        w_codes.extend(load_w(1, 2))
+        x1_raw.append(load_rows("x1_raw1", x[:, HALF + PIECE:]))
+        w_codes.extend(load_w(2, 3))
         ident = new_tile("ident", [P, P], F32)
         make_identity(nc, ident[:])
+        warm = new_tile("warm", [P, 1], F32)
+        nc.scalar.activation(out=warm[:], in_=ident[:, 0:1], func=ACT.Silu)
         w_scale_tile = new_tile("w_scale_tile", [P, M], U8)
-        nc.gpsimd.memset(w_scale_tile[:].bitcast(I32), 0)
+        nc.vector.memset(w_scale_tile[:].bitcast(I32), 0)
         w_scale_rows = w_scales[0].rearrange("(q r) n -> r q n", r=4)
         for r in range(4):
             nc.gpsimd.dma_start(out=w_scale_tile[r:P:32, :].bitcast(I32), in_=w_scale_rows[r].bitcast(I32))
@@ -131,7 +146,7 @@ def tile_mix_bilin_tm_pl_silu_kernel(tc, x, wx, c, wc, w_words, w_scales, b, out
         pc_banks, px_banks, y_banks, biased = {}, {}, {}, {}
 
         def pc_matmul(a, j):
-            pc_banks[a, j] = new_bank("pc%d_%d" % (a, j), 4 + j)
+            pc_banks[a, j] = new_bank("pc%d_%d" % (a, j), 4 * (1 - a) + j)
             cols = dealt_cols(j)
             nc.tensor.matmul_mx(out=pc_banks[a, j][:], lhsT=wc_mx[0][:, cols].bitcast(E4M3), lhsT_scale=wc_mx[1][:, cols],
                                 rhs=c_mx[a][0][:].bitcast(E5M2), rhs_scale=c_mx[a][1][:], start=True, stop=True)
@@ -141,7 +156,7 @@ def tile_mix_bilin_tm_pl_silu_kernel(tc, x, wx, c, wc, w_words, w_scales, b, out
                            in_=pc_banks[a, j][:].rearrange("p (q m i) -> p q i m", q=PIECES[a], i=PACK))
 
         def px_matmul(a, part):
-            px_banks[a, part] = new_bank("px%d_%d" % (a, part), 4 * a + part)
+            px_banks[a, part] = new_bank("px%d_%d" % (a, part), part)
             tokens = dealt_cols(part)
             for j in range(PACK):
                 cols = dealt_cols(j)
@@ -158,6 +173,13 @@ def tile_mix_bilin_tm_pl_silu_kernel(tc, x, wx, c, wc, w_words, w_scales, b, out
             nc.vector.tensor_tensor(out=out, in0=px.rearrange("p j (g u) -> p g j u", u=2),
                                     in1=pc_dealt[a][:, :, place:place + count].rearrange("p j (g u) -> p g j u", u=2), op=ALU.mult)
 
+        def product_plain(h_rounded, part, i):
+            count = P // PACK
+            place = P * i + count * part
+            out = h_rounded[:, PACK * place:PACK * (place + count)].rearrange("p (g u j) -> p g j u", u=2, j=PACK)
+            px = px_banks[1, part][:].rearrange("p (j g u i) -> p i g j u", j=PACK, u=2, i=PACK)[:, i]
+            nc.vector.tensor_tensor(out=out, in0=px, in1=pc_dealt[1][:, :, place:place + count].rearrange("p j (g u) -> p g j u", u=2), op=ALU.mult)
+
         def tile_of(step):
             return (step // STEPS,) + ORDER[step // STEPS][step % STEPS]
 
@@ -170,17 +192,17 @@ def tile_mix_bilin_tm_pl_silu_kernel(tc, x, wx, c, wc, w_words, w_scales, b, out
 
         def y_matmul(step):
             a, chunk, i = tile_of(step)
-            y_banks[step] = new_bank("y%d" % step, step % Y_BANKS)
+            y_banks[step] = new_bank("y%d" % step, 4 + step % Y_BANKS)
             tokens, n0 = dealt_cols(i), COLS * chunk
             nc.tensor.matmul_mx(out=y_banks[step][:], lhsT=h_mx[a][0][:, tokens].bitcast(E4M3), lhsT_scale=h_mx[a][1][:, tokens],
-                                rhs=w_codes[:, 2 * n0:2 * (n0 + COLS)].bitcast(E2M1), rhs_scale=w_scale_tile[:, n0:n0 + COLS],
+                                rhs=w_codes[chunk].bitcast(E2M1), rhs_scale=w_scale_tile[:, n0:n0 + COLS],
                                 start=True, stop=True)
 
-        def add_bias(step):
+        def add_bias(step, ahead=True):
             n0 = COLS * tile_of(step)[1]
             biased[step] = new_tile("biased%d" % step, [P, COLS], F32, "biased%d" % (step % BIASED_BUFS))
             nc.vector.tensor_tensor(out=biased[step][:], in0=y_banks[step][:], in1=bias[:, n0:n0 + COLS], op=ALU.add)
-            if step % STEPS + Y_BANKS < STEPS:
+            if ahead and step % STEPS + Y_BANKS < STEPS:
                 y_matmul(step + Y_BANKS)
 
         def silu(step):
@@ -205,99 +227,114 @@ def tile_mix_bilin_tm_pl_silu_kernel(tc, x, wx, c, wc, w_words, w_scales, b, out
                 at += cols
             nc.sync.dma_start(out=out_1[a, :, n0:n0 + total, :].rearrange("p n i -> p (n i)").bitcast(I32), in_=codes[:].bitcast(I32))
 
-        wc_rounded = new_rounded("wc")
-        deal(on_vector, wc_rounded[:], wc_raw, 0, WC_SPLIT)
-        deal(on_scalar, wc_rounded[:], wc_raw, WC_SPLIT, R)
+        def shared(walk, rounded, raw, split, width):
+            if split > 0:
+                walk(on_vector, rounded, raw, 0, split)
+            if split < width:
+                walk(on_scalar, rounded, raw, split, width)
+
+        wc_rounded = new_rounded("wc", tag="r0")
+        shared(deal, wc_rounded[:], wc_raw, WC_SPLIT, R)
         quantize(wc_mx, wc_rounded, E4M3)
-        c0_rounded = new_rounded("c0")
-        interleave(on_vector, c0_rounded, c0_raw, 0, C0_SPLIT)
-        interleave(on_scalar, c0_rounded, c0_raw, C0_SPLIT, HALF)
+        c0_rounded = new_rounded("c0", tag="r1")
+        shared(interleave, c0_rounded, c0_raw, C0_SPLIT, HALF)
         quantize(c_mx[0], c0_rounded, E5M2)
         for j in range(PACK):
             pc_matmul(0, j)
-        wx_rounded = new_rounded("wx")
-        x0_rounded = new_rounded("x0")
-        h0_rounded = new_rounded("h0", tag="turns")
-        deal(on_vector, wx_rounded[:], wx_raw, 0, WX_SPLIT)
-        deal(on_scalar, wx_rounded[:], wx_raw, WX_SPLIT, R)
+        wx_rounded = new_rounded("wx", tag="r2")
+        x0_rounded = new_rounded("x0", tag="r3")
+        h0_rounded = new_rounded("h0", tag="r4")
+        shared(deal, wx_rounded[:], wx_raw, WX_SPLIT, R)
         for j in range(PACK - 1):
             pc_copy(0, j)
-        deal(on_vector, piece_of(x0_rounded, 0), x0_raw[0], 0, PIECE)
         quantize(wx_mx, wx_rounded, E4M3)
+        shared(deal, piece_of(x0_rounded, 0), x0_raw[0], X0A_SPLIT, PIECE)
+        pc_copy(0, PACK - 1)
         quantize(x_mx[0], x0_rounded, E4M3, 0, PIECE)
         px_matmul(0, 0)
         px_matmul(0, 1)
-        deal(on_vector, piece_of(x0_rounded, 1), x0_raw[1], 0, X0_SPLIT)
-        deal(on_scalar, piece_of(x0_rounded, 1), x0_raw[1], X0_SPLIT, PIECE)
-        pc_copy(0, PACK - 1)
+        shared(deal, piece_of(x0_rounded, 1), x0_raw[1], X0_SPLIT, PIECE)
+        product(h0_rounded, 0, 0, 0)
         quantize(x_mx[0], x0_rounded, E4M3, PIECE, HALF)
         px_matmul(0, 2)
         px_matmul(0, 3)
-        x1_rounded = new_rounded("x1")
+        c1_rounded = new_rounded("c1", tag="r0")
         for q in range(2):
-            deal(on_scalar, x1_rounded[:], x1_raw[q], 0, PIECE, m0=q * PIECE // PACK)
-
-        for i in range(PACK):
-            product(h0_rounded, 0, 0, i)
-        for i in range(PACK - 1):
-            product(h0_rounded, 0, 1, i)
-        quantize(h_mx[0], h0_rounded, E4M3, 0, PIECE)
+            interleave(on_scalar, piece_of(c1_rounded, q), c1_raw[q], 0, PIECE)
+        product(h0_rounded, 0, 0, 1)
+        product(h0_rounded, 0, 0, 2)
+        product(h0_rounded, 0, 0, 3)
+        product(h0_rounded, 0, 1, 0)
+        product(h0_rounded, 0, 1, 1)
+        quantize(h_mx[0], h0_rounded, E4M3, 0, P)
         y_matmul(0)
+        product(h0_rounded, 0, 1, 2)
+        quantize(h_mx[0], h0_rounded, E4M3, P, 2 * P)
         y_matmul(1)
-        product(h0_rounded, 0, 1, PACK - 1)
-        quantize(x_mx[1], x1_rounded, E4M3)
+        product(h0_rounded, 0, 1, 3)
+        add_bias(0, ahead=False)
         quantize(h_mx[0], h0_rounded, E4M3, PIECE, HALF)
-        y_matmul(2)
-        y_matmul(3)
-
-        c1_rounded = new_rounded("c1", tag="turns")
-        for q in range(2):
-            interleave(on_gpsimd, piece_of(c1_rounded, q), c1_raw[q], 0, PIECE)
-        steps(0, BESIDE_C1)
+        for step in range(2, 5):
+            y_matmul(step)
+        silu(0)
+        steps(1, 2)
         quantize(c_mx[1], c1_rounded, E5M2)
         for j in range(PACK):
             pc_matmul(1, j)
-        out_00 = new_rounded("out_00", tag="turns")
-        interleave(on_gpsimd, out_00, result_chunk(0, 0), 0, COLS)
+        x1_rounded = new_rounded("x1", tag="r0")
+        for q in range(2):
+            interleave(on_gpsimd, piece_of(x1_rounded, q), x1_raw[q], 0, PIECE)
         pc_dealt[1] = new_tile("pc1", [P, PACK, HALF], F32, "pc")
-        for step in range(BESIDE_C1, STEPS):
-            add_bias(step)
+        for step in range(2, BESIDE_C1):
+            steps(step, step + 1)
+            if step in PC_AFTER:
+                pc_copy(1, PC_AFTER.index(step))
+        quantize(x_mx[1], x1_rounded, E4M3)
+        rounded = {}
+
+        def round_out(a, chunk, copy, lo, hi, tag=None):
+            if (a, chunk) not in rounded:
+                rounded[a, chunk] = new_rounded("out_%d%d" % (a, chunk), tag=tag)
+            interleave(copy, rounded[a, chunk], result_chunk(a, chunk), lo, hi)
+
+        def hand(a, chunk):
+            hand_on(a, COLS * chunk, [rounded[a, chunk]])
+
+        round_out(0, 0, on_gpsimd, 0, COLS, tag="r0")
         for j in range(PACK):
-            pc_copy(1, j)
             px_matmul(1, j)
         for step in range(BESIDE_C1, STEPS):
-            silu(step)
-        out_01 = new_rounded("out_01")
-        interleave(on_gpsimd, out_01, result_chunk(0, 1), 0, OUT_01_SPLIT)
-        interleave(on_scalar, out_01, result_chunk(0, 1), OUT_01_SPLIT, COLS)
-
-        h1_rounded = new_rounded("h1")
+            steps(step, step + 1)
+            if step in PC_AFTER:
+                pc_copy(1, PC_AFTER.index(step))
+        round_out(0, 1, on_gpsimd, 0, S01, tag="r1")
+        round_out(0, 1, on_scalar, S01, COLS)
+        h1_rounded = new_rounded("h1", tag="r2")
         for i in range(PACK):
-            product(h1_rounded, 1, 0, i)
+            for part in range(PACK):
+                product_plain(h1_rounded, part, i)
         for q in range(2):
             quantize(h_mx[1], h1_rounded, E4M3, PIECE * q, PIECE * (q + 1))
             y_matmul(STEPS + 2 * q)
             y_matmul(STEPS + 2 * q + 1)
-        hand_on(0, 0, [out_00])
+        hand(0, 0)
+        round_out(0, 2, on_gpsimd, 0, COLS, tag="r0")
+        steps(12, 24)
+        round_out(1, 0, on_gpsimd, 0, COLS, tag="r3")
+        hand_on(0, COLS, [rounded[0, 1], rounded[0, 2]])
+        hand(1, 0)
+        scale_rows = out_2.rearrange("a (q r) n -> q a r n", r=4)
 
-        out_02 = new_rounded("out_02", tag="turns")
-        interleave(on_gpsimd, out_02, result_chunk(0, 2), 0, COLS)
-        steps(STEPS, 2 * STEPS)
-        out_10 = new_rounded("out_10")
-        interleave(on_gpsimd, out_10, result_chunk(1, 0), 0, COLS)
+        def store_scales(lo, hi):
+            for q in (0, 2, 1, 3):
+                nc.scalar.dma_start(out=scale_rows[q, :, :, lo:hi].bitcast(I32), in_=out_scales[32 * q:32 * q + 8, lo:hi].bitcast(I32))
 
-        hand_on(0, COLS, [out_01, out_02])
-        hand_on(1, 0, [out_10])
-        out_11 = new_rounded("out_11")
-        interleave(on_vector, out_11, result_chunk(1, 1), 0, OUT_11_SPLIT)
-        interleave(on_scalar, out_11, result_chunk(1, 1), OUT_11_SPLIT, COLS)
+        round_out(1, 1, on_vector, 0, S11, tag="r2")
+        round_out(1, 1, on_scalar, S11, COLS)
         out_12 = [new_rounded("out_12_%d" % q, PIECE) for q in range(2)]
         interleave(on_vector, out_12[0], result_chunk(1, 2), 0, OUT_12_SPLIT)
         interleave(on_scalar, out_12[0], result_chunk(1, 2), OUT_12_SPLIT, PIECE)
         interleave(on_scalar, out_12[1], result_chunk(1, 2)[:, :, PIECE:], 0, PIECE)
-        hand_on(1, COLS, [out_11, out_12[0]])
+        hand_on(1, COLS, [rounded[1, 1], out_12[0]])
         hand_on(1, 2 * COLS + PIECE, [out_12[1]])
-
-        scale_rows = out_2.rearrange("a (q r) n -> q a r n", r=4)
-        for q in (0, 2, 1, 3):
-            nc.scalar.dma_start(out=scale_rows[q].bitcast(I32), in_=out_scales[32 * q:32 * q + 8, :].bitcast(I32))
+        store_scales(0, M)

@@ -31,8 +31,9 @@ ORDER = ([(chunk, i) for chunk in range(CHUNKS) for i in range(PACK)],
 Y_BANKS = 4
 BIASED_BUFS = 8
 S01 = 128
-S11 = 320
+S11 = 384
 X0A_SPLIT = 256
+Y_BANK = [4, 5, 6, 7] * 4 + [0, 1, 2, 3, 4, 5, 6, 7]
 BESIDE_C1 = 9
 PC_AFTER = [2, 3, 5, 6]
 
@@ -109,8 +110,8 @@ def tile_mix_bilin_tm_pl_silu_kernel(tc, x, wx, c, wc, w_words, w_scales, b, out
             nc.sync.dma_start(out=words[:].bitcast(I32), in_=w_words[0, :, 2 * COLS * lo:2 * COLS * hi].bitcast(I32))
             return [words[:, 2 * COLS * u:2 * COLS * (u + 1)] for u in range(hi - lo)]
 
-        w_codes = load_w(0, 1)
         c1_raw.append(load_rows("c1_raw1", c[:, HALF + PIECE:]))
+        w_codes = load_w(0, 1)
         x1_raw = [load_rows("x1_raw0", x[:, HALF:HALF + PIECE])]
         w_codes.extend(load_w(1, 2))
         x1_raw.append(load_rows("x1_raw1", x[:, HALF + PIECE:]))
@@ -192,30 +193,33 @@ def tile_mix_bilin_tm_pl_silu_kernel(tc, x, wx, c, wc, w_words, w_scales, b, out
 
         def y_matmul(step):
             a, chunk, i = tile_of(step)
-            y_banks[step] = new_bank("y%d" % step, 4 + step % Y_BANKS)
+            y_banks[step] = new_bank("y%d" % step, Y_BANK[step])
             tokens, n0 = dealt_cols(i), COLS * chunk
             nc.tensor.matmul_mx(out=y_banks[step][:], lhsT=h_mx[a][0][:, tokens].bitcast(E4M3), lhsT_scale=h_mx[a][1][:, tokens],
                                 rhs=w_codes[chunk].bitcast(E2M1), rhs_scale=w_scale_tile[:, n0:n0 + COLS],
                                 start=True, stop=True)
 
-        def add_bias(step, ahead=True):
-            n0 = COLS * tile_of(step)[1]
-            biased[step] = new_tile("biased%d" % step, [P, COLS], F32, "biased%d" % (step % BIASED_BUFS))
-            nc.vector.tensor_tensor(out=biased[step][:], in0=y_banks[step][:], in1=bias[:, n0:n0 + COLS], op=ALU.add)
-            if ahead and step % STEPS + Y_BANKS < STEPS:
-                y_matmul(step + Y_BANKS)
+        def y_group(lo, hi):
+            for step in reversed(range(lo, hi)):
+                y_matmul(step)
 
-        def silu(step):
-            a, chunk, i = tile_of(step)
-            nc.scalar.activation(out=result_chunk(a, chunk)[:, i, :], in_=biased[step][:], func=ACT.Silu)
-            if (a, chunk) != (1, 1):
-                lo, hi = COLS * (1 if (a, chunk) == (1, 2) else chunk), COLS * (chunk + 1)
-                nc.sync.dma_start(out=out_rows[a, :, i, lo:hi], in_=result_cols(a, lo, hi)[:, i, :])
-
-        def steps(lo, hi):
+        def adds(lo, hi):
             for step in range(lo, hi):
-                add_bias(step)
-                silu(step)
+                a, chunk, i = tile_of(step)
+                n0 = COLS * chunk
+                nc.vector.tensor_tensor(out=result_chunk(a, chunk)[:, i, :], in0=y_banks[step][:], in1=bias[:, n0:n0 + COLS], op=ALU.add)
+
+        def silu(lo, hi):
+            a, chunk, i = tile_of(lo)
+            last, i_last = tile_of(hi - 1)[1:]
+            n0, n1 = COLS * chunk, COLS * (last + 1)
+            rows = result_cols(a, n0, n1)[:, i:i_last + 1, :]
+            nc.scalar.activation(out=rows, in_=rows, func=ACT.Silu)
+            nc.sync.dma_start(out=out_rows[a, :, i:i_last + 1, n0:n1], in_=rows)
+
+        def silus(lo, hi, width):
+            for step in range(lo, hi, width):
+                silu(step, step + width)
 
         def hand_on(a, n0, tiles):
             total = sum(t.shape[1] for t in tiles) // PACK
@@ -266,75 +270,76 @@ def tile_mix_bilin_tm_pl_silu_kernel(tc, x, wx, c, wc, w_words, w_scales, b, out
         product(h0_rounded, 0, 0, 3)
         product(h0_rounded, 0, 1, 0)
         product(h0_rounded, 0, 1, 1)
-        quantize(h_mx[0], h0_rounded, E4M3, 0, P)
-        y_matmul(0)
         product(h0_rounded, 0, 1, 2)
-        quantize(h_mx[0], h0_rounded, E4M3, P, 2 * P)
-        y_matmul(1)
+        quantize(h_mx[0], h0_rounded, E4M3, 0, PIECE)
+        y_group(0, 2)
         product(h0_rounded, 0, 1, 3)
-        add_bias(0, ahead=False)
-        quantize(h_mx[0], h0_rounded, E4M3, PIECE, HALF)
-        for step in range(2, 5):
-            y_matmul(step)
-        silu(0)
-        steps(1, 2)
         quantize(c_mx[1], c1_rounded, E5M2)
-        for j in range(PACK):
-            pc_matmul(1, j)
-        x1_rounded = new_rounded("x1", tag="r0")
+        quantize(h_mx[0], h0_rounded, E4M3, PIECE, HALF)
+        y_group(2, 4)
+        x1_rounded = new_rounded("x1", tag="r4")
         for q in range(2):
             interleave(on_gpsimd, piece_of(x1_rounded, q), x1_raw[q], 0, PIECE)
         pc_dealt[1] = new_tile("pc1", [P, PACK, HALF], F32, "pc")
-        for step in range(2, BESIDE_C1):
-            steps(step, step + 1)
-            if step in PC_AFTER:
-                pc_copy(1, PC_AFTER.index(step))
+        pc_matmul(1, 1)
+        pc_matmul(1, 0)
+        adds(0, 2)
+        y_group(4, 6)
+        pc_matmul(1, 3)
+        pc_matmul(1, 2)
+        silus(0, 2, 1)
+        pc_copy(1, 0)
+        pc_copy(1, 1)
+        adds(2, 4)
+        y_group(6, 8)
+        silu(2, 4)
+        pc_copy(1, 2)
+        pc_copy(1, 3)
+        adds(4, 6)
+        y_group(8, 10)
+        adds(6, 8)
+        y_group(10, 12)
         quantize(x_mx[1], x1_rounded, E4M3)
-        rounded = {}
-
-        def round_out(a, chunk, copy, lo, hi, tag=None):
-            if (a, chunk) not in rounded:
-                rounded[a, chunk] = new_rounded("out_%d%d" % (a, chunk), tag=tag)
-            interleave(copy, rounded[a, chunk], result_chunk(a, chunk), lo, hi)
-
-        def hand(a, chunk):
-            hand_on(a, COLS * chunk, [rounded[a, chunk]])
-
-        round_out(0, 0, on_gpsimd, 0, COLS, tag="r0")
-        for j in range(PACK):
+        for j in reversed(range(PACK)):
             px_matmul(1, j)
-        for step in range(BESIDE_C1, STEPS):
-            steps(step, step + 1)
-            if step in PC_AFTER:
-                pc_copy(1, PC_AFTER.index(step))
-        round_out(0, 1, on_gpsimd, 0, S01, tag="r1")
-        round_out(0, 1, on_scalar, S01, COLS)
+        out_00 = new_rounded("out_00", tag="r4")
+        interleave(on_gpsimd, out_00, result_chunk(0, 0), 0, COLS)
+        adds(8, 12)
+        silus(4, 12, 2)
+        out_012 = new_rounded("out_012")
+        interleave(on_gpsimd, out_012, result_chunk(0, 1), 0, S01)
+        interleave(on_scalar, out_012, result_chunk(0, 1), S01, COLS)
         h1_rounded = new_rounded("h1", tag="r2")
         for i in range(PACK):
+            if i == PACK - 1:
+                quantize(h_mx[1], h1_rounded, E4M3, 0, PIECE)
+                y_group(12, 14)
             for part in range(PACK):
                 product_plain(h1_rounded, part, i)
-        for q in range(2):
-            quantize(h_mx[1], h1_rounded, E4M3, PIECE * q, PIECE * (q + 1))
-            y_matmul(STEPS + 2 * q)
-            y_matmul(STEPS + 2 * q + 1)
-        hand(0, 0)
-        round_out(0, 2, on_gpsimd, 0, COLS, tag="r0")
-        steps(12, 24)
-        round_out(1, 0, on_gpsimd, 0, COLS, tag="r3")
-        hand_on(0, COLS, [rounded[0, 1], rounded[0, 2]])
-        hand(1, 0)
-        scale_rows = out_2.rearrange("a (q r) n -> q a r n", r=4)
-
-        def store_scales(lo, hi):
-            for q in (0, 2, 1, 3):
-                nc.scalar.dma_start(out=scale_rows[q, :, :, lo:hi].bitcast(I32), in_=out_scales[32 * q:32 * q + 8, lo:hi].bitcast(I32))
-
-        round_out(1, 1, on_vector, 0, S11, tag="r2")
-        round_out(1, 1, on_scalar, S11, COLS)
+        hand_on(0, 0, [out_00])
+        quantize(h_mx[1], h1_rounded, E4M3, PIECE, HALF)
+        y_group(14, 16)
+        y_group(16, 20)
+        out_02 = new_rounded("out_02", tag="r2")
+        interleave(on_gpsimd, out_02, result_chunk(0, 2), 0, COLS)
+        adds(12, 16)
+        y_group(20, 24)
+        adds(16, 24)
+        silus(12, 16, 1)
+        silus(16, 24, 2)
+        out_10 = new_rounded("out_10", tag="r3")
+        interleave(on_gpsimd, out_10, result_chunk(1, 0), 0, COLS)
+        hand_on(0, COLS, [out_012[:, :PACK * COLS], out_02])
+        hand_on(1, 0, [out_10])
+        out_11 = new_rounded("out_11", tag="r1")
         out_12 = [new_rounded("out_12_%d" % q, PIECE) for q in range(2)]
+        interleave(on_vector, out_11, result_chunk(1, 1), 0, S11)
+        interleave(on_scalar, out_11, result_chunk(1, 1), S11, COLS)
         interleave(on_vector, out_12[0], result_chunk(1, 2), 0, OUT_12_SPLIT)
         interleave(on_scalar, out_12[0], result_chunk(1, 2), OUT_12_SPLIT, PIECE)
         interleave(on_scalar, out_12[1], result_chunk(1, 2)[:, :, PIECE:], 0, PIECE)
-        hand_on(1, COLS, [rounded[1, 1], out_12[0]])
+        hand_on(1, COLS, [out_11, out_12[0]])
         hand_on(1, 2 * COLS + PIECE, [out_12[1]])
-        store_scales(0, M)
+        scale_rows = out_2.rearrange("a (q r) n -> q a r n", r=4)
+        for q in (0, 2, 1, 3):
+            nc.scalar.dma_start(out=scale_rows[q].bitcast(I32), in_=out_scales[32 * q:32 * q + 8, :].bitcast(I32))

@@ -30,8 +30,8 @@ ORDER = ([(chunk, i) for chunk in range(CHUNKS) for i in range(PACK)],
          [(0, i) for i in range(PACK)] + [(chunk, i) for i in range(PACK) for chunk in (1, 2)])
 Y_BANKS = 4
 BIASED_BUFS = 8
-S01 = 128
-S11 = 384
+S01 = 64
+S11 = 576
 X0A_SPLIT = 256
 Y_BANK = [4, 5, 6, 7] * 4 + [0, 1, 2, 3, 4, 5, 6, 7]
 BESIDE_C1 = 9
@@ -103,7 +103,12 @@ def tile_mix_bilin_tm_pl_silu_kernel(tc, x, wx, c, wc, w_words, w_scales, b, out
         c0_raw = load_rows("c0_raw", c[:, :HALF])
         wx_raw = load_rows("wx_raw", wx)
         x0_raw = load_pieces("x0_raw", x[:, :HALF])
+        w_scale_tile = new_tile("w_scale_tile", [P, M], U8)
+        nc.vector.memset(w_scale_tile[:].bitcast(I32), 0)
+        w_scale_rows = w_scales[0].rearrange("(q r) n -> r q n", r=4)
         c1_raw = [load_rows("c1_raw0", c[:, HALF:HALF + PIECE])]
+        for r in range(4):
+            nc.sync.dma_start(out=w_scale_tile[r:P:32, :].bitcast(I32), in_=w_scale_rows[r].bitcast(I32))
 
         def load_w(lo, hi):
             words = new_tile("w_codes%d" % lo, [P, 2 * COLS * (hi - lo)], U8)
@@ -120,11 +125,6 @@ def tile_mix_bilin_tm_pl_silu_kernel(tc, x, wx, c, wc, w_words, w_scales, b, out
         make_identity(nc, ident[:])
         warm = new_tile("warm", [P, 1], F32)
         nc.scalar.activation(out=warm[:], in_=ident[:, 0:1], func=ACT.Silu)
-        w_scale_tile = new_tile("w_scale_tile", [P, M], U8)
-        nc.vector.memset(w_scale_tile[:].bitcast(I32), 0)
-        w_scale_rows = w_scales[0].rearrange("(q r) n -> r q n", r=4)
-        for r in range(4):
-            nc.gpsimd.dma_start(out=w_scale_tile[r:P:32, :].bitcast(I32), in_=w_scale_rows[r].bitcast(I32))
 
         bias = new_tile("bias", [P, M], F32)
         bias_ns = bias[:].rearrange("p (n s) -> p n s", s=b_per_row)
@@ -265,21 +265,18 @@ def tile_mix_bilin_tm_pl_silu_kernel(tc, x, wx, c, wc, w_words, w_scales, b, out
         c1_rounded = new_rounded("c1", tag="r0")
         for q in range(2):
             interleave(on_scalar, piece_of(c1_rounded, q), c1_raw[q], 0, PIECE)
-        product(h0_rounded, 0, 0, 1)
-        product(h0_rounded, 0, 0, 2)
-        product(h0_rounded, 0, 0, 3)
-        product(h0_rounded, 0, 1, 0)
-        product(h0_rounded, 0, 1, 1)
-        product(h0_rounded, 0, 1, 2)
+        x1_rounded = new_rounded("x1", tag="r1")
+        deal(on_scalar, x1_rounded[:], x1_raw[0], 0, PIECE)
+        for i in range(1, PACK):
+            product(h0_rounded, 0, 0, i)
+        for i in range(PACK - 1):
+            product(h0_rounded, 0, 1, i)
         quantize(h_mx[0], h0_rounded, E4M3, 0, PIECE)
         y_group(0, 2)
         product(h0_rounded, 0, 1, 3)
         quantize(c_mx[1], c1_rounded, E5M2)
         quantize(h_mx[0], h0_rounded, E4M3, PIECE, HALF)
         y_group(2, 4)
-        x1_rounded = new_rounded("x1", tag="r4")
-        for q in range(2):
-            interleave(on_gpsimd, piece_of(x1_rounded, q), x1_raw[q], 0, PIECE)
         pc_dealt[1] = new_tile("pc1", [P, PACK, HALF], F32, "pc")
         pc_matmul(1, 1)
         pc_matmul(1, 0)
@@ -287,36 +284,37 @@ def tile_mix_bilin_tm_pl_silu_kernel(tc, x, wx, c, wc, w_words, w_scales, b, out
         y_group(4, 6)
         pc_matmul(1, 3)
         pc_matmul(1, 2)
-        silus(0, 2, 1)
+        deal(on_scalar, x1_rounded[:], x1_raw[1], 0, PIECE, m0=PIECE // PACK)
+        silu(0, 2)
         pc_copy(1, 0)
         pc_copy(1, 1)
         adds(2, 4)
         y_group(6, 8)
+        quantize(x_mx[1], x1_rounded, E4M3)
         silu(2, 4)
         pc_copy(1, 2)
         pc_copy(1, 3)
+        out_001 = new_rounded("out_001", 2 * COLS, tag="r1")
+        interleave(on_gpsimd, out_001, result_chunk(0, 0), 0, COLS)
         adds(4, 6)
         y_group(8, 10)
         adds(6, 8)
         y_group(10, 12)
-        quantize(x_mx[1], x1_rounded, E4M3)
-        for j in reversed(range(PACK)):
+        for j in range(PACK):
             px_matmul(1, j)
-        out_00 = new_rounded("out_00", tag="r4")
-        interleave(on_gpsimd, out_00, result_chunk(0, 0), 0, COLS)
+        silu(4, 6)
         adds(8, 12)
-        silus(4, 12, 2)
-        out_012 = new_rounded("out_012")
-        interleave(on_gpsimd, out_012, result_chunk(0, 1), 0, S01)
-        interleave(on_scalar, out_012, result_chunk(0, 1), S01, COLS)
+        silus(6, 12, 2)
+        if S01 > 0:
+            interleave(on_gpsimd, out_001[:, PACK * COLS:], result_chunk(0, 1), 0, S01)
+        interleave(on_scalar, out_001[:, PACK * COLS:], result_chunk(0, 1), S01, COLS)
         h1_rounded = new_rounded("h1", tag="r2")
-        for i in range(PACK):
-            if i == PACK - 1:
-                quantize(h_mx[1], h1_rounded, E4M3, 0, PIECE)
-                y_group(12, 14)
-            for part in range(PACK):
-                product_plain(h1_rounded, part, i)
-        hand_on(0, 0, [out_00])
+        for i in range(PACK - 1):
+            product(h1_rounded, 1, 0, i)
+        quantize(h_mx[1], h1_rounded, E4M3, 0, PIECE)
+        y_group(12, 14)
+        product(h1_rounded, 1, 0, PACK - 1)
+        hand_on(0, 0, [out_001[:, :PACK * COLS]])
         quantize(h_mx[1], h1_rounded, E4M3, PIECE, HALF)
         y_group(14, 16)
         y_group(16, 20)
@@ -329,17 +327,13 @@ def tile_mix_bilin_tm_pl_silu_kernel(tc, x, wx, c, wc, w_words, w_scales, b, out
         silus(16, 24, 2)
         out_10 = new_rounded("out_10", tag="r3")
         interleave(on_gpsimd, out_10, result_chunk(1, 0), 0, COLS)
-        hand_on(0, COLS, [out_012[:, :PACK * COLS], out_02])
+        hand_on(0, COLS, [out_001[:, PACK * COLS:], out_02])
         hand_on(1, 0, [out_10])
-        out_11 = new_rounded("out_11", tag="r1")
-        out_12 = [new_rounded("out_12_%d" % q, PIECE) for q in range(2)]
-        interleave(on_vector, out_11, result_chunk(1, 1), 0, S11)
-        interleave(on_scalar, out_11, result_chunk(1, 1), S11, COLS)
-        interleave(on_vector, out_12[0], result_chunk(1, 2), 0, OUT_12_SPLIT)
-        interleave(on_scalar, out_12[0], result_chunk(1, 2), OUT_12_SPLIT, PIECE)
-        interleave(on_scalar, out_12[1], result_chunk(1, 2)[:, :, PIECE:], 0, PIECE)
-        hand_on(1, COLS, [out_11, out_12[0]])
-        hand_on(1, 2 * COLS + PIECE, [out_12[1]])
+        out_112 = new_rounded("out_112", 2 * COLS, tag="r0")
+        interleave(on_vector, out_112, result[1][1], 0, S11)
+        interleave(on_scalar, out_112, result[1][1], S11, 2 * COLS)
+        hand_on(1, COLS, [out_112[:, :PACK * COLS], out_112[:, PACK * COLS:PACK * (COLS + PIECE)]])
+        hand_on(1, 2 * COLS + PIECE, [out_112[:, PACK * (COLS + PIECE):]])
         scale_rows = out_2.rearrange("a (q r) n -> q a r n", r=4)
         for q in (0, 2, 1, 3):
             nc.scalar.dma_start(out=scale_rows[q].bitcast(I32), in_=out_scales[32 * q:32 * q + 8, :].bitcast(I32))

@@ -40,7 +40,7 @@ PC_AFTER = [2, 3, 5, 6]
 WC_SPLIT = 384
 C0_SPLIT = 352
 WX_SPLIT = 352
-X0_SPLIT = 160
+X0_SPLIT = 192
 OUT_01_SPLIT = 224
 OUT_11_SPLIT = 320
 OUT_12_SPLIT = 128
@@ -118,9 +118,8 @@ def tile_mix_bilin_tm_pl_silu_kernel(tc, x, wx, c, wc, w_words, w_scales, b, out
         c1_raw.append(load_rows("c1_raw1", c[:, HALF + PIECE:]))
         w_codes = load_w(0, 1)
         x1_raw = [load_rows("x1_raw0", x[:, HALF:HALF + PIECE])]
-        w_codes.extend(load_w(1, 2))
         x1_raw.append(load_rows("x1_raw1", x[:, HALF + PIECE:]))
-        w_codes.extend(load_w(2, 3))
+        w_codes.extend(load_w(1, 3))
         ident = new_tile("ident", [P, P], F32)
         make_identity(nc, ident[:])
         warm = new_tile("warm", [P, 1], F32)
@@ -258,7 +257,6 @@ def tile_mix_bilin_tm_pl_silu_kernel(tc, x, wx, c, wc, w_words, w_scales, b, out
         px_matmul(0, 0)
         px_matmul(0, 1)
         shared(deal, piece_of(x0_rounded, 1), x0_raw[1], X0_SPLIT, PIECE)
-        product(h0_rounded, 0, 0, 0)
         quantize(x_mx[0], x0_rounded, E4M3, PIECE, HALF)
         px_matmul(0, 2)
         px_matmul(0, 3)
@@ -267,16 +265,18 @@ def tile_mix_bilin_tm_pl_silu_kernel(tc, x, wx, c, wc, w_words, w_scales, b, out
             interleave(on_scalar, piece_of(c1_rounded, q), c1_raw[q], 0, PIECE)
         x1_rounded = new_rounded("x1", tag="r1")
         deal(on_scalar, x1_rounded[:], x1_raw[0], 0, PIECE)
-        for i in range(1, PACK):
+        for i in range(PACK):
             product(h0_rounded, 0, 0, i)
         for i in range(PACK - 1):
             product(h0_rounded, 0, 1, i)
         quantize(h_mx[0], h0_rounded, E4M3, 0, PIECE)
-        y_group(0, 2)
+        y_matmul(0)
+        y_matmul(1)
         product(h0_rounded, 0, 1, 3)
         quantize(c_mx[1], c1_rounded, E5M2)
         quantize(h_mx[0], h0_rounded, E4M3, PIECE, HALF)
-        y_group(2, 4)
+        y_matmul(2)
+        y_matmul(3)
         pc_dealt[1] = new_tile("pc1", [P, PACK, HALF], F32, "pc")
         pc_matmul(1, 1)
         pc_matmul(1, 0)
@@ -312,12 +312,15 @@ def tile_mix_bilin_tm_pl_silu_kernel(tc, x, wx, c, wc, w_words, w_scales, b, out
         for i in range(PACK - 1):
             product(h1_rounded, 1, 0, i)
         quantize(h_mx[1], h1_rounded, E4M3, 0, PIECE)
-        y_group(12, 14)
+        y_matmul(12)
+        y_matmul(13)
         product(h1_rounded, 1, 0, PACK - 1)
         hand_on(0, 0, [out_001[:, :PACK * COLS]])
         quantize(h_mx[1], h1_rounded, E4M3, PIECE, HALF)
-        y_group(14, 16)
-        y_group(16, 20)
+        y_matmul(14)
+        y_matmul(15)
+        y_group(16, 18)
+        y_group(18, 20)
         out_02 = new_rounded("out_02", tag="r2")
         interleave(on_gpsimd, out_02, result_chunk(0, 2), 0, COLS)
         adds(12, 16)
@@ -332,8 +335,8 @@ def tile_mix_bilin_tm_pl_silu_kernel(tc, x, wx, c, wc, w_words, w_scales, b, out
         out_112 = new_rounded("out_112", 2 * COLS, tag="r0")
         interleave(on_vector, out_112, result[1][1], 0, S11)
         interleave(on_scalar, out_112, result[1][1], S11, 2 * COLS)
-        hand_on(1, COLS, [out_112[:, :PACK * COLS], out_112[:, PACK * COLS:PACK * (COLS + PIECE)]])
-        hand_on(1, 2 * COLS + PIECE, [out_112[:, PACK * (COLS + PIECE):]])
+        hand_on(1, COLS, [out_112[:, :PACK * COLS]])
+        hand_on(1, 2 * COLS, [out_112[:, PACK * COLS:]])
         scale_rows = out_2.rearrange("a (q r) n -> q a r n", r=4)
         for q in (0, 2, 1, 3):
             nc.scalar.dma_start(out=scale_rows[q].bitcast(I32), in_=out_scales[32 * q:32 * q + 8, :].bitcast(I32))

from contextlib import ExitStack

import concourse.mybir as mybir
from concourse.masks import make_identity

K, L, R, M, T = 512, 512, 512, 1536, 1024
FLOPS = 2 * K * R * T + 2 * L * R * T + 2 * R * M * T

F32 = mybir.dt.float32
BF16 = mybir.dt.bfloat16
I32 = mybir.dt.int32
U32 = mybir.dt.uint32
U8 = mybir.dt.uint8
E4M3 = mybir.dt.float8_e4m3fn_x4
E5M2 = mybir.dt.float8_e5m2_x4
E2M1 = mybir.dt.float4_e2m1fn_x4
ALU = mybir.AluOpType
ACT = mybir.ActivationFunctionType

P = 128
PACK = 4
HALF = P * PACK
COLS = 512
CHUNKS = M // COLS
PIECE = HALF // 2
PIECES = (2, 1)

STEPS = CHUNKS * PACK
ORDER = ([(chunk, i) for chunk in range(CHUNKS) for i in range(PACK)],
         [(0, i) for i in range(PACK)] + [(chunk, i) for i in range(PACK) for chunk in (1, 2)])
Y_BANKS = 4
BIASED_BUFS = 8
S01 = 64
S11 = 576
X0A_SPLIT = 256
Y_BANK = [4, 5, 6, 7] * 4 + [0, 1, 2, 3, 4, 5, 6, 7]
BESIDE_C1 = 9
PC_AFTER = [2, 3, 5, 6]

WC_SPLIT = 384
C0_SPLIT = 352
WX_SPLIT = 352
X0_SPLIT = 192
OUT_01_SPLIT = 224
OUT_11_SPLIT = 320
OUT_12_SPLIT = 128


def tile_mix_bilin_tm_pl_silu_kernel(tc, x, wx, c, wc, w_words, w_scales, b, out_0, out_1, out_2):
    nc = tc.nc
    with ExitStack() as ctx:
        sbuf = ctx.enter_context(tc.tile_pool(name="sbuf", bufs=1))
        psum = ctx.enter_context(tc.psum_pool(name="psum", bufs=1))
        ctx.enter_context(tc.manual_schedule())

        def new_tile(name, shape, dtype, tag=None):
            return sbuf.tile(shape, dtype, name=name, tag=tag or name, align_bytes=64)

        def new_bank(name, bank):
            return psum.tile([P, COLS], F32, name=name, tag="bank%d" % bank)

        def new_mx(name, width):
            return new_tile(name + "_codes", [P, width], U32), new_tile(name + "_scales", [P, width], U8)

        def new_rounded(name, width=HALF, tag=None):
            return new_tile(name + "_bf16", [P, PACK * width], BF16, tag)

        def load_rows(name, rows):
            raw = new_tile(name, [P, PACK, rows.shape[1]], F32)
            nc.sync.dma_start(out=raw[:], in_=rows.rearrange("(p e) n -> p e n", e=PACK))
            return raw

        def load_pieces(name, rows):
            return [load_rows("%s%d" % (name, q), rows[:, PIECE * q:PIECE * (q + 1)]) for q in range(2)]

        def on_gpsimd(out, in_):
            nc.gpsimd.tensor_scalar(out=out, in0=in_, scalar1=1.0, scalar2=-0.0, op0=ALU.mult, op1=ALU.add)

        on_vector, on_scalar = nc.vector.tensor_copy, nc.scalar.copy

        def interleave(copy, rounded, raw, lo, hi):
            out = rounded[:, PACK * lo:PACK * hi].rearrange("p (g u e) -> p g e u", u=4, e=PACK)
            copy(out=out, in_=raw[:, :, lo:hi].rearrange("p e (g u) -> p g e u", u=4))

        def deal(copy, rounded, raw, lo, hi, m0=0):
            out = rounded.rearrange("p (j m e) -> p m e j", j=PACK, e=PACK)[:, m0 + lo // PACK:m0 + hi // PACK]
            copy(out=out, in_=raw[:, :, lo:hi].rearrange("p e (m j) -> p m e j", j=PACK))

        def piece_of(rounded, q):
            return rounded[:, PACK * PIECE * q:PACK * PIECE * (q + 1)]

        def quantize(mx, rounded, fmt, lo=0, hi=HALF):
            codes, scales = mx
            nc.vector.quantize_mx(out=codes[:, lo:hi].bitcast(fmt), scales=scales[:, lo:hi], in_=rounded[:, PACK * lo:PACK * hi])

        def dealt_cols(j):
            return slice(P * j, P * (j + 1))

        b_per_row = M // P
        b_rows = new_tile("b_rows", [P, b_per_row], F32)
        nc.sync.dma_start(out=b_rows[:], in_=b.rearrange("(p s) -> p s", p=P))
        wc_raw = load_rows("wc_raw", wc)
        c0_raw = load_rows("c0_raw", c[:, :HALF])
        wx_raw = load_rows("wx_raw", wx)
        x0_raw = load_pieces("x0_raw", x[:, :HALF])
        w_scale_tile = new_tile("w_scale_tile", [P, M], U8)
        nc.vector.memset(w_scale_tile[:].bitcast(I32), 0)
        w_scale_rows = w_scales[0].rearrange("(q r) n -> r q n", r=4)
        c1_raw = [load_rows("c1_raw0", c[:, HALF:HALF + PIECE])]
        for r in range(4):
            nc.sync.dma_start(out=w_scale_tile[r:P:32, :].bitcast(I32), in_=w_scale_rows[r].bitcast(I32))

        def load_w(lo, hi):
            words = new_tile("w_codes%d" % lo, [P, 2 * COLS * (hi - lo)], U8)
            nc.sync.dma_start(out=words[:].bitcast(I32), in_=w_words[0, :, 2 * COLS * lo:2 * COLS * hi].bitcast(I32))
            return [words[:, 2 * COLS * u:2 * COLS * (u + 1)] for u in range(hi - lo)]

        c1_raw.append(load_rows("c1_raw1", c[:, HALF + PIECE:]))
        w_codes = load_w(0, 1)
        x1_raw = [load_rows("x1_raw0", x[:, HALF:HALF + PIECE])]
        x1_raw.append(load_rows("x1_raw1", x[:, HALF + PIECE:]))
        w_codes.extend(load_w(1, 3))
        ident = new_tile("ident", [P, P], F32)
        make_identity(nc, ident[:])
        warm = new_tile("warm", [P, 1], F32)
        nc.scalar.activation(out=warm[:], in_=ident[:, 0:1], func=ACT.Silu)

        bias = new_tile("bias", [P, M], F32)
        bias_ns = bias[:].rearrange("p (n s) -> p n s", s=b_per_row)
        for group in range(b_per_row // 4):
            bank = new_bank("bias%d" % group, group)
            for u in range(4):
                s = 4 * group + u
                nc.tensor.transpose(bank[:, P * u:P * (u + 1)], b_rows[:, s:s + 1].to_broadcast([P, P]), ident[:])
            nc.scalar.copy(out=bias_ns[:, :, 4 * group:4 * group + 4], in_=bank[:].rearrange("p (u n) -> p n u", u=4))

        wc_mx, wx_mx = new_mx("wc", R), new_mx("wx", R)
        c_mx = [new_mx("c%d" % a, HALF) for a in range(2)]
        x_mx = [new_mx("x%d" % a, HALF) for a in range(2)]
        h_mx = [new_mx("h%d" % a, HALF) for a in range(2)]
        pc_dealt = {0: new_tile("pc0", [P, PACK, HALF], F32, "pc")}
        result = [[new_tile("result0_%d" % chunk, [P, PACK, COLS], F32) for chunk in range(CHUNKS)],
                  [new_tile("result1_0", [P, PACK, COLS], F32), new_tile("result1_12", [P, PACK, 2 * COLS], F32)]]
        out_scales = new_tile("out_scales", [P, M], U8)
        out_rows = out_0.rearrange("(a p i) n -> a p i n", a=2, i=PACK)
        pc_banks, px_banks, y_banks, biased = {}, {}, {}, {}

        def pc_matmul(a, j):
            pc_banks[a, j] = new_bank("pc%d_%d" % (a, j), 4 * (1 - a) + j)
            cols = dealt_cols(j)
            nc.tensor.matmul_mx(out=pc_banks[a, j][:], lhsT=wc_mx[0][:, cols].bitcast(E4M3), lhsT_scale=wc_mx[1][:, cols],
                                rhs=c_mx[a][0][:].bitcast(E5M2), rhs_scale=c_mx[a][1][:], start=True, stop=True)

        def pc_copy(a, j):
            nc.scalar.copy(out=pc_dealt[a][:, j].rearrange("p (q i m) -> p q i m", q=PIECES[a], i=PACK),
                           in_=pc_banks[a, j][:].rearrange("p (q m i) -> p q i m", q=PIECES[a], i=PACK))

        def px_matmul(a, part):
            px_banks[a, part] = new_bank("px%d_%d" % (a, part), part)
            tokens = dealt_cols(part)
            for j in range(PACK):
                cols = dealt_cols(j)
                nc.tensor.matmul_mx(out=px_banks[a, part][:, cols], lhsT=wx_mx[0][:, cols].bitcast(E4M3), lhsT_scale=wx_mx[1][:, cols],
                                    rhs=x_mx[a][0][:, tokens].bitcast(E4M3), rhs_scale=x_mx[a][1][:, tokens], start=True, stop=True)

        def product(h_rounded, a, q, i):
            count = P // PIECES[a]
            place = PACK * count * q + count * i
            part, lo = divmod(place, P)
            first = PACK * (P * i + count * q)
            out = h_rounded[:, first:first + PACK * count].rearrange("p (g u j) -> p g j u", u=2, j=PACK)
            px = px_banks[a, part][:].rearrange("p (j t) -> p j t", j=PACK)[:, :, lo:lo + count]
            nc.vector.tensor_tensor(out=out, in0=px.rearrange("p j (g u) -> p g j u", u=2),
                                    in1=pc_dealt[a][:, :, place:place + count].rearrange("p j (g u) -> p g j u", u=2), op=ALU.mult)

        def product_plain(h_rounded, part, i):
            count = P // PACK
            place = P * i + count * part
            out = h_rounded[:, PACK * place:PACK * (place + count)].rearrange("p (g u j) -> p g j u", u=2, j=PACK)
            px = px_banks[1, part][:].rearrange("p (j g u i) -> p i g j u", j=PACK, u=2, i=PACK)[:, i]
            nc.vector.tensor_tensor(out=out, in0=px, in1=pc_dealt[1][:, :, place:place + count].rearrange("p j (g u) -> p g j u", u=2), op=ALU.mult)

        def tile_of(step):
            return (step // STEPS,) + ORDER[step // STEPS][step % STEPS]

        def result_cols(a, lo, hi):
            index = min(lo // COLS, len(result[a]) - 1)
            return result[a][index][:, :, lo - COLS * index:hi - COLS * index]

        def result_chunk(a, chunk):
            return result_cols(a, COLS * chunk, COLS * (chunk + 1))

        def y_matmul(step):
            a, chunk, i = tile_of(step)
            y_banks[step] = new_bank("y%d" % step, Y_BANK[step])
            tokens, n0 = dealt_cols(i), COLS * chunk
            nc.tensor.matmul_mx(out=y_banks[step][:], lhsT=h_mx[a][0][:, tokens].bitcast(E4M3), lhsT_scale=h_mx[a][1][:, tokens],
                                rhs=w_codes[chunk].bitcast(E2M1), rhs_scale=w_scale_tile[:, n0:n0 + COLS],
                                start=True, stop=True)

        def y_group(lo, hi):
            for step in reversed(range(lo, hi)):
                y_matmul(step)

        def adds(lo, hi):
            for step in range(lo, hi):
                a, chunk, i = tile_of(step)
                n0 = COLS * chunk
                nc.vector.tensor_tensor(out=result_chunk(a, chunk)[:, i, :], in0=y_banks[step][:], in1=bias[:, n0:n0 + COLS], op=ALU.add)

        def silu(lo, hi):
            a, chunk, i = tile_of(lo)
            last, i_last = tile_of(hi - 1)[1:]
            n0, n1 = COLS * chunk, COLS * (last + 1)
            rows = result_cols(a, n0, n1)[:, i:i_last + 1, :]
            nc.scalar.activation(out=rows, in_=rows, func=ACT.Silu)
            nc.sync.dma_start(out=out_rows[a, :, i:i_last + 1, n0:n1], in_=rows)

        def silus(lo, hi, width):
            for step in range(lo, hi, width):
                silu(step, step + width)

        def hand_on(a, n0, tiles):
            total = sum(t.shape[1] for t in tiles) // PACK
            codes = new_tile("out_codes%d_%d" % (a, n0), [P, total], U32)
            at = 0
            for t in tiles:
                cols = t.shape[1] // PACK
                nc.vector.quantize_mx(out=codes[:, at:at + cols].bitcast(E4M3), scales=out_scales[4 * a:, n0 + at:n0 + at + cols], in_=t[:])
                at += cols
            nc.sync.dma_start(out=out_1[a, :, n0:n0 + total, :].rearrange("p n i -> p (n i)").bitcast(I32), in_=codes[:].bitcast(I32))

        def shared(walk, rounded, raw, split, width):
            if split > 0:
                walk(on_vector, rounded, raw, 0, split)
            if split < width:
                walk(on_scalar, rounded, raw, split, width)

        wc_rounded = new_rounded("wc", tag="r0")
        shared(deal, wc_rounded[:], wc_raw, WC_SPLIT, R)
        quantize(wc_mx, wc_rounded, E4M3)
        c0_rounded = new_rounded("c0", tag="r1")
        shared(interleave, c0_rounded, c0_raw, C0_SPLIT, HALF)
        quantize(c_mx[0], c0_rounded, E5M2)
        for j in range(PACK):
            pc_matmul(0, j)
        wx_rounded = new_rounded("wx", tag="r2")
        x0_rounded = new_rounded("x0", tag="r3")
        h0_rounded = new_rounded("h0", tag="r4")
        shared(deal, wx_rounded[:], wx_raw, WX_SPLIT, R)
        for j in range(PACK - 1):
            pc_copy(0, j)
        quantize(wx_mx, wx_rounded, E4M3)
        shared(deal, piece_of(x0_rounded, 0), x0_raw[0], X0A_SPLIT, PIECE)
        pc_copy(0, PACK - 1)
        quantize(x_mx[0], x0_rounded, E4M3, 0, PIECE)
        px_matmul(0, 0)
        px_matmul(0, 1)
        shared(deal, piece_of(x0_rounded, 1), x0_raw[1], X0_SPLIT, PIECE)
        quantize(x_mx[0], x0_rounded, E4M3, PIECE, HALF)
        px_matmul(0, 2)
        px_matmul(0, 3)
        c1_rounded = new_rounded("c1", tag="r0")
        for q in range(2):
            interleave(on_scalar, piece_of(c1_rounded, q), c1_raw[q], 0, PIECE)
        x1_rounded = new_rounded("x1", tag="r1")
        deal(on_scalar, x1_rounded[:], x1_raw[0], 0, PIECE)
        for i in range(PACK):
            product(h0_rounded, 0, 0, i)
        for i in range(PACK - 1):
            product(h0_rounded, 0, 1, i)
        quantize(h_mx[0], h0_rounded, E4M3, 0, PIECE)
        y_matmul(0)
        y_matmul(1)
        product(h0_rounded, 0, 1, 3)
        quantize(c_mx[1], c1_rounded, E5M2)
        quantize(h_mx[0], h0_rounded, E4M3, PIECE, HALF)
        y_matmul(2)
        y_matmul(3)
        pc_dealt[1] = new_tile("pc1", [P, PACK, HALF], F32, "pc")
        pc_matmul(1, 1)
        pc_matmul(1, 0)
        adds(0, 2)
        y_group(4, 6)
        pc_matmul(1, 3)
        pc_matmul(1, 2)
        deal(on_scalar, x1_rounded[:], x1_raw[1], 0, PIECE, m0=PIECE // PACK)
        silu(0, 2)
        pc_copy(1, 0)
        pc_copy(1, 1)
        adds(2, 4)
        y_group(6, 8)
        quantize(x_mx[1], x1_rounded, E4M3)
        silu(2, 4)
        pc_copy(1, 2)
        pc_copy(1, 3)
        out_001 = new_rounded("out_001", 2 * COLS, tag="r1")
        interleave(on_gpsimd, out_001, result_chunk(0, 0), 0, COLS)
        adds(4, 6)
        y_group(8, 10)
        adds(6, 8)
        y_group(10, 12)
        for j in range(PACK):
            px_matmul(1, j)
        silu(4, 6)
        adds(8, 12)
        silus(6, 12, 2)
        if S01 > 0:
            interleave(on_gpsimd, out_001[:, PACK * COLS:], result_chunk(0, 1), 0, S01)
        interleave(on_scalar, out_001[:, PACK * COLS:], result_chunk(0, 1), S01, COLS)
        h1_rounded = new_rounded("h1", tag="r2")
        for i in range(PACK - 1):
            product(h1_rounded, 1, 0, i)
        quantize(h_mx[1], h1_rounded, E4M3, 0, PIECE)
        y_matmul(12)
        y_matmul(13)
        product(h1_rounded, 1, 0, PACK - 1)
        hand_on(0, 0, [out_001[:, :PACK * COLS]])
        quantize(h_mx[1], h1_rounded, E4M3, PIECE, HALF)
        y_matmul(14)
        y_matmul(15)
        y_group(16, 18)
        y_group(18, 20)
        out_02 = new_rounded("out_02", tag="r2")
        interleave(on_gpsimd, out_02, result_chunk(0, 2), 0, COLS)
        adds(12, 16)
        y_group(20, 24)
        adds(16, 24)
        silus(12, 16, 1)
        silus(16, 24, 2)
        out_10 = new_rounded("out_10", tag="r3")
        interleave(on_gpsimd, out_10, result_chunk(1, 0), 0, COLS)
        hand_on(0, COLS, [out_001[:, PACK * COLS:], out_02])
        hand_on(1, 0, [out_10])
        out_112 = new_rounded("out_112", 2 * COLS, tag="r0")
        interleave(on_vector, out_112, result[1][1], 0, S11)
        interleave(on_scalar, out_112, result[1][1], S11, 2 * COLS)
        hand_on(1, COLS, [out_112[:, :PACK * COLS]])
        hand_on(1, 2 * COLS, [out_112[:, PACK * COLS:]])
        scale_rows = out_2.rearrange("a (q r) n -> q a r n", r=4)
        for q in (0, 2, 1, 3):
            nc.scalar.dma_start(out=scale_rows[q].bitcast(I32), in_=out_scales[32 * q:32 * q + 8, :].bitcast(I32))
